import numpy as np
import ml_dtypes


def mxq(x, axis, fmt="e4m3"):
    dtype, down = {"e4m3": (ml_dtypes.float8_e4m3fn, 7), "e5m2": (ml_dtypes.float8_e5m2, 14)}[fmt]
    v = np.moveaxis(np.asarray(x, np.float32).astype(ml_dtypes.bfloat16).astype(np.float64), axis, -1)
    blocks = v.reshape(v.shape[:-1] + (-1, 32))
    amax = np.abs(blocks).max(-1, keepdims=True)
    byte = np.maximum(np.where(amax > 0, np.frexp(amax)[1] - 1 + 127, 0) - down, 1)
    scale = np.exp2(byte - 127.0)
    codes = (blocks / scale).astype(np.float32).astype(dtype).astype(np.float64)
    return np.moveaxis((codes * scale).reshape(v.shape), -1, axis)


WIDE = False


def mx_kscale(k):
    if not WIDE:
        return np.ones(k)
    levels = np.array([10, -10, 5, -5, 0])
    if k % 512:
        return np.exp2(np.random.permutation(np.resize(levels, k // 32))).repeat(32)
    a = np.empty((k // 512, 16))
    for p in range(k // 512):
        a[p, :8] = np.random.permutation(np.resize(levels, 8))
        for g in range(8):
            far = levels[np.abs(levels - a[p, g]) >= 10]
            a[p, g + 8] = far[np.random.randint(len(far))]
    return np.exp2(a.ravel()).repeat(32)


def f64(x):
    return np.asarray(x).astype(np.float64)


def striped(idx):
    return np.tile(idx.reshape(-1, 16).T, (8, 1)).astype(np.uint16)


def unstriped(offs):
    return offs[:16].T.reshape(-1).astype(np.int64)


E2M1 = np.array([0.0, 0.5, 1.0, 1.5, 2.0, 3.0, 4.0, 6.0, -0.0, -0.5, -1.0, -1.5, -2.0, -3.0, -4.0, -6.0])


def pack_weight(w, fmt):
    k, n = w.shape
    w = f64(np.asarray(w, np.float32).astype(ml_dtypes.bfloat16)).reshape(k // 32, 32, n)
    amax = np.abs(w).max(1)
    if fmt == "e4m3":
        byte = np.frexp(amax)[1] - 1 + 127 - 7
    else:
        mant, ex = np.frexp(amax / 6.0)
        byte = np.where(mant > 0.5, ex, ex - 1) + 127
    byte = np.clip(np.where(amax > 0, byte, 1), 1, 254)
    scaled = (w * np.exp2(127.0 - byte)[:, None, :]).reshape(k, n).astype(np.float32)
    by_word = np.ascontiguousarray(scaled.reshape(k // 512, 128, 4, n).transpose(0, 1, 3, 2))
    if fmt == "e4m3":
        words = by_word.astype(ml_dtypes.float8_e4m3fn).view(np.uint8)
    else:
        c = by_word.astype(ml_dtypes.float4_e2m1fn).view(np.uint8) & 0xF
        words = (c[..., 0::2] | (c[..., 1::2] << 4)).reshape(k // 512, 128, 2 * n)
    return np.ascontiguousarray(words), np.ascontiguousarray(byte.astype(np.uint8).reshape(k // 512, 16, n))


def unpack_weight(words, scales, fmt):
    g, _, n = scales.shape
    words = np.ascontiguousarray(words).reshape(g, 128, n, -1)
    if fmt == "e4m3":
        vals = words.view(ml_dtypes.float8_e4m3fn).astype(np.float64)
    else:
        nib = np.empty((g, 128, n, 4), np.uint8)
        nib[..., 0::2] = words & 0xF
        nib[..., 1::2] = words >> 4
        vals = E2M1[nib]
    vals = vals * np.repeat(np.exp2(scales.astype(np.float64) - 127.0), 8, axis=1)[..., None]
    return vals.transpose(0, 1, 3, 2).reshape(g * 512, n)


def d_silu(v):
    s = 1.0 / (1.0 + np.exp(-np.maximum(v, -700.0)))
    return s * (1.0 + v * (1.0 - s))


K, T, E, C, H, N = 256, 640, 20, 128, 512, 512
TOP = 4


def by_expert(wq, xq):
    return np.concatenate([wq[e].T @ xq[:, e * C:(e + 1) * C] for e in range(E)], axis=1)


def setup_inputs():
    n = np.random.standard_normal
    s = mx_kscale(N)[:, None]
    u = mx_kscale(H)
    deal = np.repeat(np.arange(E), C).reshape(TOP, T)[:, np.random.permutation(T)]
    deal = np.take_along_axis(deal, np.argsort(np.random.rand(TOP, T), axis=0), axis=0)
    for _ in range(8):
        s_, t_ = np.random.permutation(T).reshape(2, -1); r = np.random.randint(TOP, size=T // 2); x, y = deal[r, s_].copy(), deal[r, t_].copy()
        ok = ~((deal[:, s_] == y).any(0) | (deal[:, t_] == x).any(0)); deal[r[ok], s_[ok]] = y[ok]; deal[r[ok], t_[ok]] = x[ok]
    order = np.lexsort((np.random.rand(TOP * T), deal.reshape(-1)))
    slot_token = order % T; pos = np.empty(TOP * T, np.int64); pos[order] = np.arange(TOP * T); pos = pos.reshape(TOP, T)
    g = np.random.uniform(0.5, 1.5, (TOP, T)); g = g / g.sum(0)
    w_slot = np.empty(E * C)
    for r in range(TOP): w_slot[pos[r]] = g[r]
    w2 = [pack_weight(m, "e2m1") for m in n((E, N, H)) / np.sqrt(N) / s[None] * u[None, None, :]]
    w1 = [pack_weight(m, "e2m1") for m in n((E, H, K)) / np.sqrt(H) / u[None, :, None]]
    return {
        "dyT": (n((N, T)) * s).astype(np.float32),
        "a": n((H, E * C)).astype(np.float32),
        "w2_words": np.stack([m[0] for m in w2]),
        "w2_scales": np.stack([m[1] for m in w2]),
        "w1_words": np.stack([m[0] for m in w1]),
        "w1_scales": np.stack([m[1] for m in w1]),
        "gate": np.tile(w_slot, (N, 1)).astype(np.float32),
        "offs": striped(slot_token),
        "pos1": striped(pos[0]),
        "pos2": striped(pos[1]),
        "pos3": striped(pos[2]),
        "pos4": striped(pos[3]),
    }


def reference(dyT, a, w2_words, w2_scales, w1_words, w1_scales, gate, offs, pos1, pos2, pos3, pos4):
    idx = unstriped(offs)
    w2 = np.stack([unpack_weight(w2_words[e], w2_scales[e], "e2m1") for e in range(E)])
    w1 = np.stack([unpack_weight(w1_words[e], w1_scales[e], "e2m1") for e in range(E)])
    gq = mxq(f64(gate) * f64(dyT)[:, idx], 0, "e4m3")
    dh = by_expert(w2, gq)
    da = dh * d_silu(f64(a))
    dx = by_expert(w1, mxq(da, 0, "e4m3"))
    return dx[:, unstriped(pos1)] + dx[:, unstriped(pos2)] + dx[:, unstriped(pos3)] + dx[:, unstriped(pos4)]

@@ -1,0 +1,260 @@
+from contextlib import ExitStack
+
+import concourse.mybir as mybir
+from concourse.masks import make_identity
+
+K, T, E, C, H, N = 256, 640, 20, 128, 512, 512
+TOP = 4
+S = E * C
+P = 128
+PACK = 4
+CHUNK = 512
+EPC = CHUNK // C
+NCH = S // CHUNK
+PAIR = 2 * C
+LEAD = 6
+
+FLOPS = 2 * S * (N * H + H * K)
+BYTES = 4 * N * T + 4 * H * S + E * (P * 2 * H + 16 * H + P * 2 * K + 16 * K) + 4 * S + 2 * P * (S + TOP * T) // 16 + 4 * K * T
+
+F32 = mybir.dt.float32
+BF16 = mybir.dt.bfloat16
+I32 = mybir.dt.int32
+U32 = mybir.dt.uint32
+U16 = mybir.dt.uint16
+U8 = mybir.dt.uint8
+FP8X4 = mybir.dt.float8_e4m3fn_x4
+FP4X4 = mybir.dt.float4_e2m1fn_x4
+ALU = mybir.AluOpType
+ACT = mybir.ActivationFunctionType
+
+
+def tile_moe_bdx_mlp_silu_kernel(
+    tc, dyT, a, w2_words, w2_scales, w1_words, w1_scales, gate, offs, pos1, pos2, pos3, pos4, out
+):
+    nc = tc.nc
+    with ExitStack() as ctx:
+        keep = ctx.enter_context(tc.tile_pool(name="keep", bufs=1))
+        ring2 = ctx.enter_context(tc.tile_pool(name="ring2", bufs=2))
+        ring3 = ctx.enter_context(tc.tile_pool(name="ring3", bufs=3))
+        ring6 = ctx.enter_context(tc.tile_pool(name="ring6", bufs=6))
+        psum = ctx.enter_context(tc.psum_pool(name="psum", bufs=2))
+
+        offs_sb = keep.tile([P, S // 16], U16, name="offs_sb")
+        pos_sb = [keep.tile([P, T // 16], U16, name=f"pos_sb{r}") for r in range(TOP)]
+        dy_sb = [keep.tile([P, T], F32, name=f"dy_sb{j}") for j in range(PACK)]
+        gate_sb = [keep.tile([P, CHUNK], F32, name=f"gate_sb{c}") for c in range(NCH)]
+        a_sb = [keep.tile([P, PACK, PAIR], F32, name=f"a_sb{u}") for u in range(E // 2)]
+        w2_sb = [keep.tile([P, EPC, 2 * H], U8, name=f"w2_sb{c}", align_bytes=64) for c in range(NCH)]
+        w1_sb = [keep.tile([P, EPC, 2 * K], U8, name=f"w1_sb{c}", align_bytes=64) for c in range(NCH)]
+        w2_plane = keep.tile([P, E, H], U8, name="w2_plane", align_bytes=64)
+        w1_plane = keep.tile([P, E, K], U8, name="w1_plane", align_bytes=64)
+        dx_sb = keep.tile([P, K // P, S], F32, name="dx_sb")
+        ident = keep.tile([P, P], F32, name="ident")
+
+        make_identity(nc, ident[:])
+        nc.gpsimd.memset(w2_plane[:].bitcast(I32), 0)
+        nc.gpsimd.memset(w1_plane[:].bitcast(I32), 0)
+
+        dy_rows = dyT.rearrange("(p j) t -> p j t", j=PACK)
+        a_rows = a.rearrange("(p j) s -> p j s", j=PACK)
+
+        def load_dy(j):
+            nc.sync.dma_start(dy_sb[j][:], dy_rows[:, j, :])
+
+        def load_gate(c):
+            nc.sync.dma_start(gate_sb[c][:], gate[0:P, c * CHUNK : (c + 1) * CHUNK])
+
+        def load_a(u):
+            nc.sync.dma_start(a_sb[u][:], a_rows[:, :, u * PAIR : (u + 1) * PAIR])
+
+        def load_words(tiles, words, c):
+            src = words[c * EPC : (c + 1) * EPC, 0].rearrange("e p b -> p e b")
+            nc.sync.dma_start(tiles[c][:].bitcast(I32), src.bitcast(I32))
+
+        def load_plane(plane, scales):
+            for q in range(4):
+                src = scales[:, 0, 4 * q : 4 * q + 4, :].rearrange("e f i -> f e i")
+                nc.sync.dma_start(plane[32 * q : 32 * q + 4, :, :].bitcast(I32), src.bitcast(I32))
+
+        nc.sync.dma_start(offs_sb[:], offs)
+        load_dy(0)
+        load_gate(0)
+        load_dy(1)
+        load_a(0)
+        load_dy(2)
+        load_dy(3)
+        load_gate(1)
+        load_a(1)
+        load_plane(w2_plane, w2_scales)
+        load_words(w2_sb, w2_words, 0)
+        load_a(2)
+        load_plane(w1_plane, w1_scales)
+        load_words(w1_sb, w1_words, 0)
+        for c in range(1, NCH):
+            if c + 1 < NCH:
+                load_gate(c + 1)
+            load_a(2 * c + 1)
+            load_words(w2_sb, w2_words, c)
+            if c + 1 < NCH:
+                load_a(2 * c + 2)
+            load_words(w1_sb, w1_words, c)
+        for r, pos in enumerate((pos1, pos2, pos3, pos4)):
+            nc.sync.dma_start(pos_sb[r][:], pos)
+
+        g_planes, g_codes, g_scales = {}, {}, {}
+        th, nsilu, dh_ps, a_ps2, da_bf, da_codes, da_scales, dx_ps, g_bfs = {}, {}, {}, {}, {}, {}, {}, {}, {}
+
+        def gather(i):
+            c, j = divmod(i, PACK)
+            if j == 0:
+                g_planes[c] = ring3.tile([P, PACK, CHUNK], F32, name="planes")
+            cols = CHUNK // 16
+            nc.vector.tensor_tensor(
+                g_planes[c][:, j, :], dy_sb[j][:].indirect(offs_sb[:, c * cols : (c + 1) * cols]), gate_sb[c][:], ALU.mult
+            )
+            if j == PACK - 1:
+                g_bf = ring2.tile([P, CHUNK, PACK], BF16, name="g_bf", align_bytes=64)
+                for u in range(2):
+                    half = slice(u * PAIR, (u + 1) * PAIR)
+                    nc.scalar.copy(
+                        g_bf[:, half, :].rearrange("p (c i) t -> p c t i", i=2),
+                        g_planes[c][:, :, half].rearrange("p t (c i) -> p c t i", i=2),
+                    )
+                g_bfs[c] = g_bf
+
+        def quantize_g(c):
+            g_codes[c] = ring3.tile([P, CHUNK], U32, name="g_codes", align_bytes=64)
+            g_scales[c] = ring3.tile([P, CHUNK], U8, name="g_scales", align_bytes=64)
+            nc.vector.quantize_mx(
+                out=g_codes[c][:].bitcast(FP8X4), scales=g_scales[c][:], in_=g_bfs[c][:].rearrange("p s t -> p (s t)")
+            )
+
+        def activations(e):
+            u, v = divmod(e, 2)
+            a_e = a_sb[u][:, :, v * C : (v + 1) * C]
+            nsilu[e] = ring6.tile([P, C, PACK], F32, name="nsilu")
+            nc.scalar.activation(
+                nsilu[e][:].rearrange("p (c i) t -> p c t i", i=2),
+                a_e.rearrange("p t (c i) -> p c t i", i=2),
+                ACT.Silu,
+                scale=-1.0,
+            )
+            at_ps = psum.tile([P, PACK, P], F32, name="at_ps")
+            for j in range(PACK):
+                nc.tensor.transpose(at_ps[:, j, :], a_e[:, j, :], ident[:])
+            th[e] = ring6.tile([P, PACK, P], F32, name="th")
+            nc.scalar.activation(th[e][:], at_ps[:], ACT.Tanh, scale=-0.5)
+
+        def first_product(e):
+            c, v = divmod(e, EPC)
+            cols = slice(v * C, (v + 1) * C)
+            dh_ps[e] = psum.tile([P, H], F32, name="dh_ps")
+            nc.tensor.matmul_mx(
+                out=dh_ps[e][:],
+                lhsT=g_codes[c][:, cols].bitcast(FP8X4),
+                lhsT_scale=g_scales[c][:, cols],
+                rhs=w2_sb[c][:, v, :].bitcast(FP4X4),
+                rhs_scale=w2_plane[:, e, :],
+                start=True,
+                stop=True,
+            )
+
+        def first_factor(e):
+            part = ring3.tile([P, PACK, P], F32, name="part")
+            nc.vector.scalar_tensor_tensor(
+                part[:], th[e][:], 1.0, dh_ps[e][:].rearrange("s (p j) -> s j p", j=PACK), ALU.subtract, ALU.mult
+            )
+            a_ps2[e] = psum.tile([P, PACK, C], F32, name="part_ps")
+            for j in range(PACK):
+                nc.tensor.transpose(a_ps2[e][:, j, :], part[:, j, :], ident[:])
+
+        def second_factor(e):
+            u, v = divmod(e, 2)
+            if v == 0:
+                da_bf[u] = ring3.tile([P, PAIR, PACK], BF16, name="da_bf", align_bytes=64)
+            nc.vector.scalar_tensor_tensor(
+                da_bf[u][:, v * C : (v + 1) * C, :],
+                nsilu[e][:],
+                1.0,
+                a_ps2[e][:].rearrange("p j s -> p s j"),
+                ALU.subtract,
+                ALU.mult,
+            )
+
+        def second_product(u):
+            codes = ring3.tile([P, PAIR], U32, name="da_codes", align_bytes=64)
+            scales = ring3.tile([P, PAIR], U8, name="da_scales", align_bytes=64)
+            nc.vector.quantize_mx(out=codes[:].bitcast(FP8X4), scales=scales[:], in_=da_bf[u][:].rearrange("p s t -> p (s t)"))
+            bank = psum.tile([P, K // P, PAIR], F32, name="dx_ps")
+            for v in range(2):
+                e = 2 * u + v
+                c, w = divmod(e, EPC)
+                cols = slice(v * C, (v + 1) * C)
+                for h in range(K // P):
+                    nc.tensor.matmul_mx(
+                        out=bank[:, h, cols],
+                        lhsT=w1_sb[c][:, w, 2 * P * h : 2 * P * (h + 1)].bitcast(FP4X4),
+                        lhsT_scale=w1_plane[:, e, P * h : P * (h + 1)],
+                        rhs=codes[:, cols].bitcast(FP8X4),
+                        rhs_scale=scales[:, cols],
+                        start=True,
+                        stop=True,
+                    )
+            nc.scalar.activation(dx_sb[:, :, u * PAIR : (u + 1) * PAIR], bank[:], ACT.Copy, scale=0.5)
+
+        activations(0)
+        for i in range(LEAD):
+            gather(i)
+        activations(1)
+        quantize_g(0)
+        first_product(0)
+        for e in range(E + 2):
+            if e + 2 < E:
+                activations(e + 2)
+            if e + LEAD < NCH * PACK:
+                gather(e + LEAD)
+            if e + 1 < E and (e + 1) % EPC == 0:
+                quantize_g((e + 1) // EPC)
+            if e + 1 < E:
+                first_product(e + 1)
+            if e < E:
+                first_factor(e)
+            if e >= 3 and e % 2 == 1:
+                second_product((e - 3) // 2)
+            if 1 <= e <= E:
+                second_factor(e - 1)
+
+        pieces = ((0, 3), (3, 5))
+        first3, back, last = {}, {}, {}
+        for h in range(K // P):
+            first3[h] = ring3.tile([P, TOP - 1, T], F32, name="planes")
+            for r in range(TOP - 1):
+                nc.vector.tensor_copy(first3[h][:, r, :], dx_sb[:, h, :].indirect(pos_sb[r][:]))
+            sum_t = ring2.tile([P, T // P, P], F32, name="sum_t")
+            for x, (b0, b1) in enumerate(pieces):
+                bank = psum.tile([P, PACK, P], F32, name="at_ps")
+                for b in range(b0, b1):
+                    for r in range(TOP - 1):
+                        nc.tensor.matmul(
+                            bank[:, b - b0, :],
+                            lhsT=first3[h][:, r, b * P : (b + 1) * P],
+                            rhs=ident[:],
+                            start=(r == 0),
+                            stop=(r == TOP - 2),
+                            is_transpose=True,
+                        )
+                nc.scalar.copy(sum_t[:, b0:b1, :], bank[:, 0 : b1 - b0, :])
+                back[h, x] = psum.tile([P, PACK, C], F32, name=("part_ps", "dh_ps")[x])
+                for b in range(b0, b1):
+                    nc.tensor.transpose(back[h, x][:, b - b0, :], sum_t[:, b, :], ident[:])
+        for h in range(K // P):
+            last[h] = ring2.tile([P, T], F32, name="last")
+            nc.vector.tensor_copy(last[h][:], dx_sb[:, h, :].indirect(pos_sb[TOP - 1][:]))
+            res = ring2.tile([P, T], F32, name="res")
+            for x, (b0, b1) in enumerate(pieces):
+                cols = slice(b0 * P, b1 * P)
+                nc.vector.tensor_tensor(
+                    res[:, cols], last[h][:, cols], back[h, x][:, 0 : b1 - b0, :].rearrange("p b c -> p (b c)"), ALU.add
+                )
+                nc.sync.dma_start(out[h * P : (h + 1) * P, cols], res[:, cols])

@@ -12,7 +12,23 @@ CHUNK = 512
 EPC = CHUNK // C
 NCH = S // CHUNK
 PAIR = 2 * C
+NPAIR = E // 2
 LEAD = 6
+ACT_LEAD = 2
+QLEAD = 1
+GROUPS = [[0, 4], [4, 8], [8, 12], [12, 16], [16, 18], [18, 19], [19, 20]]
+BACK = [['part_ps', 'part_ps'], ['at_ps', 'at_ps']]
+ORDER = 'd0 o0 g0 d1 a0 d2 d3 g1 a1 S0 W0 g2 a2 s0 w0 a3 S1 W1 g3 a4 s1 w1 a5 W2 a6 g4 w2 a7 W3 a8 w3 a9 W4 w4'
+SUMT = ['at_ps', 'at_ps', 'dh_ps', 'dh_ps', 'dx_ps']
+MLEAD = 1
+OLEAD = 0
+LAG = 1
+DEEP = 99
+DEEP2 = 99
+LAST1 = 0
+SPLITH = 1
+ACT_LAST = 0
+EARLY = EPC
 
 FLOPS = 2 * S * (N * H + H * K)
 BYTES = 4 * N * T + 4 * H * S + E * (P * 2 * H + 16 * H + P * 2 * K + 16 * K) + 4 * S + 2 * P * (S + TOP * T) // 16 + 4 * K * T
@@ -37,24 +53,26 @@ def tile_moe_bdx_mlp_silu_kernel(
         keep = ctx.enter_context(tc.tile_pool(name="keep", bufs=1))
         ring2 = ctx.enter_context(tc.tile_pool(name="ring2", bufs=2))
         ring3 = ctx.enter_context(tc.tile_pool(name="ring3", bufs=3))
-        ring6 = ctx.enter_context(tc.tile_pool(name="ring6", bufs=6))
-        psum = ctx.enter_context(tc.psum_pool(name="psum", bufs=2))
+        ring8 = ctx.enter_context(tc.tile_pool(name="ring8", bufs=8))
+        psum2 = ctx.enter_context(tc.psum_pool(name="psum2", bufs=2))
 
+        groups = ((0, EARLY), (EARLY, E))
         offs_sb = keep.tile([P, S // 16], U16, name="offs_sb")
         pos_sb = [keep.tile([P, T // 16], U16, name=f"pos_sb{r}") for r in range(TOP)]
         dy_sb = [keep.tile([P, T], F32, name=f"dy_sb{j}") for j in range(PACK)]
         gate_sb = [keep.tile([P, CHUNK], F32, name=f"gate_sb{c}") for c in range(NCH)]
-        a_sb = [keep.tile([P, PACK, PAIR], F32, name=f"a_sb{u}") for u in range(E // 2)]
+        a_sb = [keep.tile([P, PACK, PAIR], F32, name=f"a_sb{u}") for u in range(NPAIR)]
         w2_sb = [keep.tile([P, EPC, 2 * H], U8, name=f"w2_sb{c}", align_bytes=64) for c in range(NCH)]
         w1_sb = [keep.tile([P, EPC, 2 * K], U8, name=f"w1_sb{c}", align_bytes=64) for c in range(NCH)]
-        w2_plane = keep.tile([P, E, H], U8, name="w2_plane", align_bytes=64)
-        w1_plane = keep.tile([P, E, K], U8, name="w1_plane", align_bytes=64)
+        w2_plane = [keep.tile([P, e1 - e0, H], U8, name=f"w2_plane{e0}", align_bytes=64) for e0, e1 in groups]
+        w1_plane = [keep.tile([P, e1 - e0, K], U8, name=f"w1_plane{e0}", align_bytes=64) for e0, e1 in groups]
         dx_sb = keep.tile([P, K // P, S], F32, name="dx_sb")
         ident = keep.tile([P, P], F32, name="ident")
 
         make_identity(nc, ident[:])
-        nc.gpsimd.memset(w2_plane[:].bitcast(I32), 0)
-        nc.gpsimd.memset(w1_plane[:].bitcast(I32), 0)
+        for x in range(2):
+            nc.gpsimd.memset(w2_plane[x][:].bitcast(I32), 0)
+            nc.gpsimd.memset(w1_plane[x][:].bitcast(I32), 0)
 
         dy_rows = dyT.rearrange("(p j) t -> p j t", j=PACK)
         a_rows = a.rearrange("(p j) s -> p j s", j=PACK)
@@ -72,38 +90,32 @@ def tile_moe_bdx_mlp_silu_kernel(
             src = words[c * EPC : (c + 1) * EPC, 0].rearrange("e p b -> p e b")
             nc.sync.dma_start(tiles[c][:].bitcast(I32), src.bitcast(I32))
 
-        def load_plane(plane, scales):
+        def load_plane(planes, scales, x):
+            e0, e1 = groups[x]
             for q in range(4):
-                src = scales[:, 0, 4 * q : 4 * q + 4, :].rearrange("e f i -> f e i")
-                nc.sync.dma_start(plane[32 * q : 32 * q + 4, :, :].bitcast(I32), src.bitcast(I32))
+                src = scales[e0:e1, 0, 4 * q : 4 * q + 4, :].rearrange("e f i -> f e i")
+                nc.sync.dma_start(planes[x][32 * q : 32 * q + 4, :, :].bitcast(I32), src.bitcast(I32))
 
-        nc.sync.dma_start(offs_sb[:], offs)
-        load_dy(0)
-        load_gate(0)
-        load_dy(1)
-        load_a(0)
-        load_dy(2)
-        load_dy(3)
-        load_gate(1)
-        load_a(1)
-        load_plane(w2_plane, w2_scales)
-        load_words(w2_sb, w2_words, 0)
-        load_a(2)
-        load_plane(w1_plane, w1_scales)
-        load_words(w1_sb, w1_words, 0)
-        for c in range(1, NCH):
-            if c + 1 < NCH:
-                load_gate(c + 1)
-            load_a(2 * c + 1)
-            load_words(w2_sb, w2_words, c)
-            if c + 1 < NCH:
-                load_a(2 * c + 2)
-            load_words(w1_sb, w1_words, c)
+        def plane_of(planes, e):
+            return planes[0][:, e, :] if e < EARLY else planes[1][:, e - EARLY, :]
+
+        loaders = {
+            "o": lambda x: nc.sync.dma_start(offs_sb[:], offs),
+            "d": load_dy,
+            "g": load_gate,
+            "a": load_a,
+            "W": lambda c: load_words(w2_sb, w2_words, c),
+            "w": lambda c: load_words(w1_sb, w1_words, c),
+            "S": lambda x: load_plane(w2_plane, w2_scales, x),
+            "s": lambda x: load_plane(w1_plane, w1_scales, x),
+        }
+        for item in ORDER.split():
+            loaders[item[0]](int(item[1:]))
         for r, pos in enumerate((pos1, pos2, pos3, pos4)):
             nc.sync.dma_start(pos_sb[r][:], pos)
 
-        g_planes, g_codes, g_scales = {}, {}, {}
-        th, nsilu, dh_ps, a_ps2, da_bf, da_codes, da_scales, dx_ps, g_bfs = {}, {}, {}, {}, {}, {}, {}, {}, {}
+        g_planes, g_bf, g_codes, g_scales = {}, {}, {}, {}
+        th, nsilu, dh_ps, part_ps, da_bf = {}, {}, {}, {}, {}
 
         def gather(i):
             c, j = divmod(i, PACK)
@@ -114,48 +126,50 @@ def tile_moe_bdx_mlp_silu_kernel(
                 g_planes[c][:, j, :], dy_sb[j][:].indirect(offs_sb[:, c * cols : (c + 1) * cols]), gate_sb[c][:], ALU.mult
             )
             if j == PACK - 1:
-                g_bf = ring2.tile([P, CHUNK, PACK], BF16, name="g_bf", align_bytes=64)
+                g_bf[c] = ring2.tile([P, CHUNK, PACK], BF16, name="g_bf", align_bytes=64)
                 for u in range(2):
                     half = slice(u * PAIR, (u + 1) * PAIR)
                     nc.scalar.copy(
-                        g_bf[:, half, :].rearrange("p (c i) t -> p c t i", i=2),
+                        g_bf[c][:, half, :].rearrange("p (c i) t -> p c t i", i=2),
                         g_planes[c][:, :, half].rearrange("p t (c i) -> p c t i", i=2),
                     )
-                g_bfs[c] = g_bf
 
-        def quantize_g(c):
-            g_codes[c] = ring3.tile([P, CHUNK], U32, name="g_codes", align_bytes=64)
-            g_scales[c] = ring3.tile([P, CHUNK], U8, name="g_scales", align_bytes=64)
+        def quantize_g(c, s0, s1):
+            if s0 == 0:
+                g_codes[c] = ring3.tile([P, CHUNK], U32, name="g_codes", align_bytes=64)
+                g_scales[c] = ring3.tile([P, CHUNK], U8, name="g_scales", align_bytes=64)
             nc.vector.quantize_mx(
-                out=g_codes[c][:].bitcast(FP8X4), scales=g_scales[c][:], in_=g_bfs[c][:].rearrange("p s t -> p (s t)")
+                out=g_codes[c][:, s0:s1].bitcast(FP8X4),
+                scales=g_scales[c][:, s0:s1],
+                in_=g_bf[c][:, s0:s1, :].rearrange("p s t -> p (s t)"),
             )
 
         def activations(e):
             u, v = divmod(e, 2)
             a_e = a_sb[u][:, :, v * C : (v + 1) * C]
-            nsilu[e] = ring6.tile([P, C, PACK], F32, name="nsilu")
+            at_ps = psum2.tile([P, PACK, P], F32, name="at_ps")
+            for j in range(PACK):
+                nc.tensor.transpose(at_ps[:, j, :], a_e[:, j, :], ident[:])
+            nsilu[e] = ring8.tile([P, C, PACK], F32, name="nsilu")
             nc.scalar.activation(
                 nsilu[e][:].rearrange("p (c i) t -> p c t i", i=2),
                 a_e.rearrange("p t (c i) -> p c t i", i=2),
                 ACT.Silu,
                 scale=-1.0,
             )
-            at_ps = psum.tile([P, PACK, P], F32, name="at_ps")
-            for j in range(PACK):
-                nc.tensor.transpose(at_ps[:, j, :], a_e[:, j, :], ident[:])
-            th[e] = ring6.tile([P, PACK, P], F32, name="th")
+            th[e] = ring8.tile([P, PACK, P], F32, name="th")
             nc.scalar.activation(th[e][:], at_ps[:], ACT.Tanh, scale=-0.5)
 
         def first_product(e):
-            c, v = divmod(e, EPC)
-            cols = slice(v * C, (v + 1) * C)
-            dh_ps[e] = psum.tile([P, H], F32, name="dh_ps")
+            c, w = divmod(e, EPC)
+            cols = slice(w * C, (w + 1) * C)
+            dh_ps[e] = psum2.tile([P, H], F32, name="dh_ps")
             nc.tensor.matmul_mx(
                 out=dh_ps[e][:],
                 lhsT=g_codes[c][:, cols].bitcast(FP8X4),
                 lhsT_scale=g_scales[c][:, cols],
-                rhs=w2_sb[c][:, v, :].bitcast(FP4X4),
-                rhs_scale=w2_plane[:, e, :],
+                rhs=w2_sb[c][:, w, :].bitcast(FP4X4),
+                rhs_scale=plane_of(w2_plane, e),
                 start=True,
                 stop=True,
             )
@@ -165,96 +179,143 @@ def tile_moe_bdx_mlp_silu_kernel(
             nc.vector.scalar_tensor_tensor(
                 part[:], th[e][:], 1.0, dh_ps[e][:].rearrange("s (p j) -> s j p", j=PACK), ALU.subtract, ALU.mult
             )
-            a_ps2[e] = psum.tile([P, PACK, C], F32, name="part_ps")
+            part_ps[e] = psum2.tile([P, PACK, C], F32, name=("at_ps" if e >= DEEP2 and e % 2 == 1 else "part_ps"))
             for j in range(PACK):
-                nc.tensor.transpose(a_ps2[e][:, j, :], part[:, j, :], ident[:])
+                nc.tensor.transpose(part_ps[e][:, j, :], part[:, j, :], ident[:])
+
+        group_of = {}
+        for e0, e1 in GROUPS:
+            for e in range(e0, e1):
+                group_of[e] = (e0, e1)
 
         def second_factor(e):
-            u, v = divmod(e, 2)
-            if v == 0:
-                da_bf[u] = ring3.tile([P, PAIR, PACK], BF16, name="da_bf", align_bytes=64)
+            e0, e1 = group_of[e]
+            if e == e0:
+                da_bf[e0] = ring3.tile([P, (e1 - e0) * C, PACK], BF16, name="da_bf", align_bytes=64)
             nc.vector.scalar_tensor_tensor(
-                da_bf[u][:, v * C : (v + 1) * C, :],
+                da_bf[e0][:, (e - e0) * C : (e - e0 + 1) * C, :],
                 nsilu[e][:],
                 1.0,
-                a_ps2[e][:].rearrange("p j s -> p s j"),
+                part_ps[e][:].rearrange("p j s -> p s j"),
                 ALU.subtract,
                 ALU.mult,
             )
 
-        def second_product(u):
-            codes = ring3.tile([P, PAIR], U32, name="da_codes", align_bytes=64)
-            scales = ring3.tile([P, PAIR], U8, name="da_scales", align_bytes=64)
-            nc.vector.quantize_mx(out=codes[:].bitcast(FP8X4), scales=scales[:], in_=da_bf[u][:].rearrange("p s t -> p (s t)"))
-            bank = psum.tile([P, K // P, PAIR], F32, name="dx_ps")
-            for v in range(2):
-                e = 2 * u + v
-                c, w = divmod(e, EPC)
-                cols = slice(v * C, (v + 1) * C)
+        def second_product(e0, e1):
+            width = (e1 - e0) * C
+            codes = ring3.tile([P, width], U32, name="da_codes", align_bytes=64)
+            scales = ring3.tile([P, width], U8, name="da_scales", align_bytes=64)
+            nc.vector.quantize_mx(out=codes[:].bitcast(FP8X4), scales=scales[:], in_=da_bf[e0][:].rearrange("p s t -> p (s t)"))
+            if e0 == E - 1 and SPLITH:
+                c, w = divmod(e0, EPC)
                 for h in range(K // P):
+                    bank = psum2.tile([P, C], F32, name=("dx_ps", "dh_ps")[h])
                     nc.tensor.matmul_mx(
-                        out=bank[:, h, cols],
+                        out=bank[:],
                         lhsT=w1_sb[c][:, w, 2 * P * h : 2 * P * (h + 1)].bitcast(FP4X4),
-                        lhsT_scale=w1_plane[:, e, P * h : P * (h + 1)],
-                        rhs=codes[:, cols].bitcast(FP8X4),
-                        rhs_scale=scales[:, cols],
+                        lhsT_scale=plane_of(w1_plane, e0)[:, P * h : P * (h + 1)],
+                        rhs=codes[:].bitcast(FP8X4),
+                        rhs_scale=scales[:],
                         start=True,
                         stop=True,
                     )
-            nc.scalar.activation(dx_sb[:, :, u * PAIR : (u + 1) * PAIR], bank[:], ACT.Copy, scale=0.5)
+                    nc.scalar.activation(dx_sb[:, h, e0 * C : e1 * C], bank[:], ACT.Copy, scale=0.5)
+                return
+            for f0 in range(e0, e1, 2):
+                f1 = min(f0 + 2, e1)
+                bank = psum2.tile([P, K // P, (f1 - f0) * C], F32, name="dx_ps")
+                for e in range(f0, f1):
+                    c, w = divmod(e, EPC)
+                    cols = slice((e - e0) * C, (e - e0 + 1) * C)
+                    for h in range(K // P):
+                        nc.tensor.matmul_mx(
+                            out=bank[:, h, (e - f0) * C : (e - f0 + 1) * C],
+                            lhsT=w1_sb[c][:, w, 2 * P * h : 2 * P * (h + 1)].bitcast(FP4X4),
+                            lhsT_scale=plane_of(w1_plane, e)[:, P * h : P * (h + 1)],
+                            rhs=codes[:, cols].bitcast(FP8X4),
+                            rhs_scale=scales[:, cols],
+                            start=True,
+                            stop=True,
+                        )
+                nc.scalar.activation(dx_sb[:, :, f0 * C : f1 * C], bank[:], ACT.Copy, scale=0.5)
 
-        activations(0)
+        for e in range(ACT_LEAD):
+            activations(e)
         for i in range(LEAD):
             gather(i)
-        activations(1)
-        quantize_g(0)
+        quantize_g(0, 0, PAIR)
         first_product(0)
-        for e in range(E + 2):
-            if e + 2 < E:
-                activations(e + 2)
+        quantize_g(0, PAIR, CHUNK)
+        for e in range(1, MLEAD):
+            first_product(e)
+        done2 = set()
+        doneq = set()
+        for e in range(E + 6):
+            if e + ACT_LEAD < E and not ACT_LAST:
+                activations(e + ACT_LEAD)
             if e + LEAD < NCH * PACK:
                 gather(e + LEAD)
-            if e + 1 < E and (e + 1) % EPC == 0:
-                quantize_g((e + 1) // EPC)
-            if e + 1 < E:
-                first_product(e + 1)
+            if e + QLEAD < E and (e + QLEAD) % EPC == 0 and e + QLEAD > 0:
+                quantize_g((e + QLEAD) // EPC, 0, CHUNK)
+            if e + MLEAD < E:
+                first_product(e + MLEAD)
             if e < E:
                 first_factor(e)
-            if e >= 3 and e % 2 == 1:
-                second_product((e - 3) // 2)
-            if 1 <= e <= E:
-                second_factor(e - 1)
+            for e0, e1 in GROUPS:
+                if e0 not in doneq and all(x in done2 for x in range(e0, e1)):
+                    second_product(e0, e1)
+                    doneq.add(e0)
+            for x in range(E):
+                if x not in done2 and x + (LAG if x >= DEEP else 1) <= e and all(y in done2 for y in range(group_of[x][0], x)):
+                    second_factor(x)
+                    done2.add(x)
+            if e + ACT_LEAD < E and ACT_LAST:
+                activations(e + ACT_LEAD)
 
         pieces = ((0, 3), (3, 5))
-        first3, back, last = {}, {}, {}
-        for h in range(K // P):
-            first3[h] = ring3.tile([P, TOP - 1, T], F32, name="planes")
+        back = {}
+
+        def sum_first_three(h):
+            first3 = ring3.tile([P, TOP - 1, T], F32, name="planes")
+            tags = SUMT
+            banks = [psum2.tile([P, P], F32, name=tag) for tag in tags]
             for r in range(TOP - 1):
-                nc.vector.tensor_copy(first3[h][:, r, :], dx_sb[:, h, :].indirect(pos_sb[r][:]))
+                nc.vector.tensor_copy(first3[:, r, :], dx_sb[:, h, :].indirect(pos_sb[r][:]))
+                for b in range(T // P):
+                    nc.tensor.matmul(
+                        banks[b][:],
+                        lhsT=first3[:, r, b * P : (b + 1) * P],
+                        rhs=ident[:],
+                        start=(r == 0),
+                        stop=(r == TOP - 2),
+                        is_transpose=True,
+                    )
             sum_t = ring2.tile([P, T // P, P], F32, name="sum_t")
-            for x, (b0, b1) in enumerate(pieces):
-                bank = psum.tile([P, PACK, P], F32, name="at_ps")
+            for b in range(T // P):
+                nc.scalar.copy(sum_t[:, b, :], banks[b][:])
+            return sum_t
+
+        def turn_back(h, sum_t, blocks):
+            for x, (b0, b1) in enumerate(blocks):
+                back[h, x] = psum2.tile([P, H], F32, name=BACK[h][x])
                 for b in range(b0, b1):
-                    for r in range(TOP - 1):
-                        nc.tensor.matmul(
-                            bank[:, b - b0, :],
-                            lhsT=first3[h][:, r, b * P : (b + 1) * P],
-                            rhs=ident[:],
-                            start=(r == 0),
-                            stop=(r == TOP - 2),
-                            is_transpose=True,
-                        )
-                nc.scalar.copy(sum_t[:, b0:b1, :], bank[:, 0 : b1 - b0, :])
-                back[h, x] = psum.tile([P, PACK, C], F32, name=("part_ps", "dh_ps")[x])
-                for b in range(b0, b1):
-                    nc.tensor.transpose(back[h, x][:, b - b0, :], sum_t[:, b, :], ident[:])
-        for h in range(K // P):
-            last[h] = ring2.tile([P, T], F32, name="last")
-            nc.vector.tensor_copy(last[h][:], dx_sb[:, h, :].indirect(pos_sb[TOP - 1][:]))
-            res = ring2.tile([P, T], F32, name="res")
-            for x, (b0, b1) in enumerate(pieces):
-                cols = slice(b0 * P, b1 * P)
-                nc.vector.tensor_tensor(
-                    res[:, cols], last[h][:, cols], back[h, x][:, 0 : b1 - b0, :].rearrange("p b c -> p (b c)"), ALU.add
-                )
-                nc.sync.dma_start(out[h * P : (h + 1) * P, cols], res[:, cols])
+                    nc.tensor.transpose(back[h, x][:, (b - b0) * P : (b - b0 + 1) * P], sum_t[:, b, :], ident[:])
+
+        def finish(h, x, first, t0, t1, fourth):
+            nc.vector.tensor_tensor(res[h][:, t0:t1], fourth, back[h, x][:, t0 - first : t1 - first], ALU.add)
+            nc.sync.dma_start(out[h * P : (h + 1) * P, t0:t1], res[h][:, t0:t1])
+
+        sums = [sum_first_three(h) for h in range(K // P)]
+        turn_back(0, sums[0], ((0, 3), (3, 5)))
+        turn_back(1, sums[1], ((0, 3), (2, 5)))
+        res = [ring2.tile([P, T], F32, name="res") for h in range(K // P)]
+        half = T // 2
+        last = keep.tile([P, T], F32, name="last")
+        early = keep.tile([P, half], F32, name="early")
+        nc.vector.tensor_copy(last[:], dx_sb[:, 0, :].indirect(pos_sb[TOP - 1][:]))
+        nc.vector.tensor_copy(early[:], dx_sb[:, 1, :].indirect(pos_sb[TOP - 1][:, 0 : half // 16]))
+        finish(0, 0, 0, 0, 3 * P, last[:, 0 : 3 * P])
+        finish(0, 1, 3 * P, 3 * P, T, last[:, 3 * P : T])
+        nc.vector.tensor_copy(last[:, 0:half], dx_sb[:, 1, :].indirect(pos_sb[TOP - 1][:, half // 16 : T // 16]))
+        finish(1, 0, 0, 0, half, early[:])
+        finish(1, 1, 2 * P, half, T, last[:, 0:half])

@@ -8,30 +8,26 @@ TOP = 4
 S = E * C
 P = 128
 PACK = 4
-CHUNK = 512
-EPC = CHUNK // C
-NCH = S // CHUNK
+LIST_COL = 16
+BANK = 512
+K_TILES = K // P
+T_BLOCKS = T // P
+
+CHUNK_EXPERTS = 4
+CHUNK = CHUNK_EXPERTS * C
+CHUNKS = S // CHUNK
+GATHERS = CHUNKS * PACK
 PAIR = 2 * C
-NPAIR = E // 2
-LEAD = 6
-ACT_LEAD = 2
-QLEAD = 1
-GROUPS = [[0, 4], [4, 8], [8, 12], [12, 16], [16, 18], [18, 19], [19, 20]]
-BACK = [['part_ps', 'part_ps'], ['at_ps', 'at_ps']]
-ORDER = 'd0 o0 g0 d1 a0 d2 d3 g1 a1 S0 W0 g2 a2 s0 w0 a3 S1 W1 g3 a4 s1 w1 a5 W2 a6 g4 w2 a7 W3 a8 w3 a9 W4 w4'
-SUMT = ['at_ps', 'at_ps', 'dh_ps', 'dh_ps', 'dx_ps']
-MLEAD = 1
-OLEAD = 0
-LAG = 1
-DEEP = 99
-DEEP2 = 99
-LAST1 = 0
-SPLITH = 1
-ACT_LAST = 0
-EARLY = EPC
+
+SCALE_GROUPS = ((0, CHUNK_EXPERTS), (CHUNK_EXPERTS, E))
+DA_GROUPS = tuple((e, e + 2) for e in range(0, E - 2, 2)) + ((E - 2, E - 1), (E - 1, E))
+FIRST_CUT = C
+
+GATHER_LEAD = 6
+ACTIVATION_LEAD = 2
 
 FLOPS = 2 * S * (N * H + H * K)
-BYTES = 4 * N * T + 4 * H * S + E * (P * 2 * H + 16 * H + P * 2 * K + 16 * K) + 4 * S + 2 * P * (S + TOP * T) // 16 + 4 * K * T
+BYTES = 4 * (N * T + H * S + S + K * T) + E * (2 * P + 16) * (H + K) + 2 * P * (S + TOP * T) // LIST_COL
 
 F32 = mybir.dt.float32
 BF16 = mybir.dt.bfloat16
@@ -53,117 +49,134 @@ def tile_moe_bdx_mlp_silu_kernel(
         keep = ctx.enter_context(tc.tile_pool(name="keep", bufs=1))
         ring2 = ctx.enter_context(tc.tile_pool(name="ring2", bufs=2))
         ring3 = ctx.enter_context(tc.tile_pool(name="ring3", bufs=3))
-        ring8 = ctx.enter_context(tc.tile_pool(name="ring8", bufs=8))
-        psum2 = ctx.enter_context(tc.psum_pool(name="psum2", bufs=2))
+        ring6 = ctx.enter_context(tc.tile_pool(name="ring6", bufs=6))
+        psum = ctx.enter_context(tc.psum_pool(name="psum", bufs=2))
 
-        groups = ((0, EARLY), (EARLY, E))
-        offs_sb = keep.tile([P, S // 16], U16, name="offs_sb")
-        pos_sb = [keep.tile([P, T // 16], U16, name=f"pos_sb{r}") for r in range(TOP)]
+        offs_sb = keep.tile([P, S // LIST_COL], U16, name="offs_sb")
+        pos_sb = [keep.tile([P, T // LIST_COL], U16, name=f"pos_sb{r}") for r in range(TOP)]
         dy_sb = [keep.tile([P, T], F32, name=f"dy_sb{j}") for j in range(PACK)]
-        gate_sb = [keep.tile([P, CHUNK], F32, name=f"gate_sb{c}") for c in range(NCH)]
-        a_sb = [keep.tile([P, PACK, PAIR], F32, name=f"a_sb{u}") for u in range(NPAIR)]
-        w2_sb = [keep.tile([P, EPC, 2 * H], U8, name=f"w2_sb{c}", align_bytes=64) for c in range(NCH)]
-        w1_sb = [keep.tile([P, EPC, 2 * K], U8, name=f"w1_sb{c}", align_bytes=64) for c in range(NCH)]
-        w2_plane = [keep.tile([P, e1 - e0, H], U8, name=f"w2_plane{e0}", align_bytes=64) for e0, e1 in groups]
-        w1_plane = [keep.tile([P, e1 - e0, K], U8, name=f"w1_plane{e0}", align_bytes=64) for e0, e1 in groups]
-        dx_sb = keep.tile([P, K // P, S], F32, name="dx_sb")
+        gate_sb = [keep.tile([P, CHUNK], F32, name=f"gate_sb{c}") for c in range(CHUNKS)]
+        a_sb = [keep.tile([P, PACK, PAIR], F32, name=f"a_sb{u}") for u in range(E // 2)]
+        w2_sb = [keep.tile([P, CHUNK_EXPERTS, 2 * H], U8, name=f"w2_sb{c}", align_bytes=64) for c in range(CHUNKS)]
+        w1_sb = [keep.tile([P, CHUNK_EXPERTS, 2 * K], U8, name=f"w1_sb{c}", align_bytes=64) for c in range(CHUNKS)]
+        w2_plane = [keep.tile([P, e1 - e0, H], U8, name=f"w2_plane{e0}", align_bytes=64) for e0, e1 in SCALE_GROUPS]
+        w1_plane = [keep.tile([P, e1 - e0, K], U8, name=f"w1_plane{e0}", align_bytes=64) for e0, e1 in SCALE_GROUPS]
+        dx_sb = keep.tile([P, K_TILES, S], F32, name="dx_sb")
         ident = keep.tile([P, P], F32, name="ident")
 
         make_identity(nc, ident[:])
-        for x in range(2):
+        for x in range(len(SCALE_GROUPS)):
             nc.gpsimd.memset(w2_plane[x][:].bitcast(I32), 0)
             nc.gpsimd.memset(w1_plane[x][:].bitcast(I32), 0)
 
         dy_rows = dyT.rearrange("(p j) t -> p j t", j=PACK)
         a_rows = a.rearrange("(p j) s -> p j s", j=PACK)
 
+        def pieces(is_first):
+            return ((0, FIRST_CUT), (FIRST_CUT, CHUNK)) if is_first else ((0, CHUNK),)
+
         def load_dy(j):
             nc.sync.dma_start(dy_sb[j][:], dy_rows[:, j, :])
 
         def load_gate(c):
-            nc.sync.dma_start(gate_sb[c][:], gate[0:P, c * CHUNK : (c + 1) * CHUNK])
+            for s0, s1 in pieces(c == 0):
+                nc.sync.dma_start(gate_sb[c][:, s0:s1], gate[0:P, c * CHUNK + s0 : c * CHUNK + s1])
 
         def load_a(u):
             nc.sync.dma_start(a_sb[u][:], a_rows[:, :, u * PAIR : (u + 1) * PAIR])
 
         def load_words(tiles, words, c):
-            src = words[c * EPC : (c + 1) * EPC, 0].rearrange("e p b -> p e b")
+            src = words[c * CHUNK_EXPERTS : (c + 1) * CHUNK_EXPERTS, 0].rearrange("e p b -> p e b")
             nc.sync.dma_start(tiles[c][:].bitcast(I32), src.bitcast(I32))
 
         def load_plane(planes, scales, x):
-            e0, e1 = groups[x]
+            e0, e1 = SCALE_GROUPS[x]
             for q in range(4):
                 src = scales[e0:e1, 0, 4 * q : 4 * q + 4, :].rearrange("e f i -> f e i")
                 nc.sync.dma_start(planes[x][32 * q : 32 * q + 4, :, :].bitcast(I32), src.bitcast(I32))
 
-        def plane_of(planes, e):
-            return planes[0][:, e, :] if e < EARLY else planes[1][:, e - EARLY, :]
+        def load_w2(c):
+            load_words(w2_sb, w2_words, c)
 
-        loaders = {
-            "o": lambda x: nc.sync.dma_start(offs_sb[:], offs),
-            "d": load_dy,
-            "g": load_gate,
-            "a": load_a,
-            "W": lambda c: load_words(w2_sb, w2_words, c),
-            "w": lambda c: load_words(w1_sb, w1_words, c),
-            "S": lambda x: load_plane(w2_plane, w2_scales, x),
-            "s": lambda x: load_plane(w1_plane, w1_scales, x),
-        }
-        for item in ORDER.split():
-            loaders[item[0]](int(item[1:]))
+        def load_w1(c):
+            load_words(w1_sb, w1_words, c)
+
+        def load_s2(x):
+            load_plane(w2_plane, w2_scales, x)
+
+        def load_s1(x):
+            load_plane(w1_plane, w1_scales, x)
+
+        def plane_of(planes, e):
+            return [planes[x][:, e - e0, :] for x, (e0, e1) in enumerate(SCALE_GROUPS) if e0 <= e < e1][0]
+
+        load_dy(0)
+        nc.sync.dma_start(offs_sb[:], offs)
+        for load, index in (
+            (load_gate, 0), (load_dy, 1), (load_a, 0), (load_dy, 2), (load_dy, 3), (load_gate, 1), (load_a, 1),
+            (load_s2, 0), (load_w2, 0), (load_gate, 2), (load_a, 2), (load_s1, 0), (load_w1, 0), (load_a, 3),
+            (load_s2, 1), (load_w2, 1), (load_gate, 3), (load_a, 4), (load_s1, 1), (load_w1, 1), (load_a, 5),
+            (load_w2, 2), (load_a, 6), (load_gate, 4), (load_w1, 2), (load_a, 7),
+            (load_w2, 3), (load_a, 8), (load_w1, 3), (load_a, 9),
+            (load_w2, 4), (load_w1, 4),
+        ):
+            load(index)
         for r, pos in enumerate((pos1, pos2, pos3, pos4)):
             nc.sync.dma_start(pos_sb[r][:], pos)
 
-        g_planes, g_bf, g_codes, g_scales = {}, {}, {}, {}
-        th, nsilu, dh_ps, part_ps, da_bf = {}, {}, {}, {}, {}
+        g_f32, g_bf, g_codes, g_scales = {}, {}, {}, {}
+        tanh_t, silu_neg, dh_ps, half_da_ps, da_bf = {}, {}, {}, {}, {}
+        da_group = {e: (e0, e1) for e0, e1 in DA_GROUPS for e in range(e0, e1)}
 
-        def gather(i):
-            c, j = divmod(i, PACK)
+        def gather(number):
+            c, j = divmod(number, PACK)
             if j == 0:
-                g_planes[c] = ring3.tile([P, PACK, CHUNK], F32, name="planes")
-            cols = CHUNK // 16
-            nc.vector.tensor_tensor(
-                g_planes[c][:, j, :], dy_sb[j][:].indirect(offs_sb[:, c * cols : (c + 1) * cols]), gate_sb[c][:], ALU.mult
-            )
+                g_f32[c] = ring3.tile([P, PACK, CHUNK], F32, name="gathered")
+            for s0, s1 in pieces(number == 0):
+                entries = offs_sb[:, (c * CHUNK + s0) // LIST_COL : (c * CHUNK + s1) // LIST_COL]
+                nc.vector.tensor_tensor(g_f32[c][:, j, s0:s1], dy_sb[j][:].indirect(entries), gate_sb[c][:, s0:s1], ALU.mult)
             if j == PACK - 1:
                 g_bf[c] = ring2.tile([P, CHUNK, PACK], BF16, name="g_bf", align_bytes=64)
-                for u in range(2):
-                    half = slice(u * PAIR, (u + 1) * PAIR)
+                for s0 in range(0, CHUNK, PAIR):
                     nc.scalar.copy(
-                        g_bf[c][:, half, :].rearrange("p (c i) t -> p c t i", i=2),
-                        g_planes[c][:, :, half].rearrange("p t (c i) -> p c t i", i=2),
+                        g_bf[c][:, s0 : s0 + PAIR, :].rearrange("p (s i) j -> p s j i", i=2),
+                        g_f32[c][:, :, s0 : s0 + PAIR].rearrange("p j (s i) -> p s j i", i=2),
                     )
 
-        def quantize_g(c, s0, s1):
+        def quantise_g(c, s0, s1):
             if s0 == 0:
                 g_codes[c] = ring3.tile([P, CHUNK], U32, name="g_codes", align_bytes=64)
                 g_scales[c] = ring3.tile([P, CHUNK], U8, name="g_scales", align_bytes=64)
             nc.vector.quantize_mx(
                 out=g_codes[c][:, s0:s1].bitcast(FP8X4),
                 scales=g_scales[c][:, s0:s1],
-                in_=g_bf[c][:, s0:s1, :].rearrange("p s t -> p (s t)"),
+                in_=g_bf[c][:, s0:s1, :].rearrange("p s j -> p (s j)"),
             )
 
-        def activations(e):
+        def a_of(e):
             u, v = divmod(e, 2)
-            a_e = a_sb[u][:, :, v * C : (v + 1) * C]
-            at_ps = psum2.tile([P, PACK, P], F32, name="at_ps")
-            for j in range(PACK):
-                nc.tensor.transpose(at_ps[:, j, :], a_e[:, j, :], ident[:])
-            nsilu[e] = ring8.tile([P, C, PACK], F32, name="nsilu")
+            return a_sb[u][:, :, v * C : (v + 1) * C]
+
+        def silu_factor(e):
+            silu_neg[e] = ring6.tile([P, C, PACK], F32, name="silu_neg")
             nc.scalar.activation(
-                nsilu[e][:].rearrange("p (c i) t -> p c t i", i=2),
-                a_e.rearrange("p t (c i) -> p c t i", i=2),
+                silu_neg[e][:].rearrange("p (s i) j -> p s j i", i=2),
+                a_of(e).rearrange("p j (s i) -> p s j i", i=2),
                 ACT.Silu,
                 scale=-1.0,
             )
-            th[e] = ring8.tile([P, PACK, P], F32, name="th")
-            nc.scalar.activation(th[e][:], at_ps[:], ACT.Tanh, scale=-0.5)
+
+        def tanh_factor(e):
+            a_turned = psum.tile([P, PACK, P], F32, name="a_turned")
+            for j in range(PACK):
+                nc.tensor.transpose(a_turned[:, j, :], a_of(e)[:, j, :], ident[:])
+            tanh_t[e] = ring6.tile([P, PACK, P], F32, name="tanh_t")
+            nc.scalar.activation(tanh_t[e][:], a_turned[:], ACT.Tanh, scale=-0.5)
 
         def first_product(e):
-            c, w = divmod(e, EPC)
+            c, w = divmod(e, CHUNK_EXPERTS)
             cols = slice(w * C, (w + 1) * C)
-            dh_ps[e] = psum2.tile([P, H], F32, name="dh_ps")
+            dh_ps[e] = psum.tile([P, H], F32, name="dh")
             nc.tensor.matmul_mx(
                 out=dh_ps[e][:],
                 lhsT=g_codes[c][:, cols].bitcast(FP8X4),
@@ -174,148 +187,127 @@ def tile_moe_bdx_mlp_silu_kernel(
                 stop=True,
             )
 
-        def first_factor(e):
-            part = ring3.tile([P, PACK, P], F32, name="part")
+        def apply_tanh_factor(e):
+            half_da_t = ring3.tile([P, PACK, P], F32, name="half_da_t")
             nc.vector.scalar_tensor_tensor(
-                part[:], th[e][:], 1.0, dh_ps[e][:].rearrange("s (p j) -> s j p", j=PACK), ALU.subtract, ALU.mult
+                half_da_t[:], tanh_t[e][:], 1.0, dh_ps[e][:].rearrange("s (p j) -> s j p", j=PACK), ALU.subtract, ALU.mult
             )
-            part_ps[e] = psum2.tile([P, PACK, C], F32, name=("at_ps" if e >= DEEP2 and e % 2 == 1 else "part_ps"))
+            half_da_ps[e] = psum.tile([P, PACK, C], F32, name="half_da")
             for j in range(PACK):
-                nc.tensor.transpose(part_ps[e][:, j, :], part[:, j, :], ident[:])
+                nc.tensor.transpose(half_da_ps[e][:, j, :], half_da_t[:, j, :], ident[:])
 
-        group_of = {}
-        for e0, e1 in GROUPS:
-            for e in range(e0, e1):
-                group_of[e] = (e0, e1)
-
-        def second_factor(e):
-            e0, e1 = group_of[e]
+        def apply_silu_factor(e):
+            e0, e1 = da_group[e]
             if e == e0:
                 da_bf[e0] = ring3.tile([P, (e1 - e0) * C, PACK], BF16, name="da_bf", align_bytes=64)
             nc.vector.scalar_tensor_tensor(
                 da_bf[e0][:, (e - e0) * C : (e - e0 + 1) * C, :],
-                nsilu[e][:],
+                silu_neg[e][:],
                 1.0,
-                part_ps[e][:].rearrange("p j s -> p s j"),
+                half_da_ps[e][:].rearrange("p j s -> p s j"),
                 ALU.subtract,
                 ALU.mult,
             )
 
         def second_product(e0, e1):
-            width = (e1 - e0) * C
-            codes = ring3.tile([P, width], U32, name="da_codes", align_bytes=64)
-            scales = ring3.tile([P, width], U8, name="da_scales", align_bytes=64)
-            nc.vector.quantize_mx(out=codes[:].bitcast(FP8X4), scales=scales[:], in_=da_bf[e0][:].rearrange("p s t -> p (s t)"))
-            if e0 == E - 1 and SPLITH:
-                c, w = divmod(e0, EPC)
-                for h in range(K // P):
-                    bank = psum2.tile([P, C], F32, name=("dx_ps", "dh_ps")[h])
-                    nc.tensor.matmul_mx(
-                        out=bank[:],
-                        lhsT=w1_sb[c][:, w, 2 * P * h : 2 * P * (h + 1)].bitcast(FP4X4),
-                        lhsT_scale=plane_of(w1_plane, e0)[:, P * h : P * (h + 1)],
-                        rhs=codes[:].bitcast(FP8X4),
-                        rhs_scale=scales[:],
-                        start=True,
-                        stop=True,
-                    )
+            codes = ring3.tile([P, (e1 - e0) * C], U32, name="da_codes", align_bytes=64)
+            scales = ring3.tile([P, (e1 - e0) * C], U8, name="da_scales", align_bytes=64)
+            nc.vector.quantize_mx(out=codes[:].bitcast(FP8X4), scales=scales[:], in_=da_bf[e0][:].rearrange("p s j -> p (s j)"))
+
+            def multiply(dst, e, h):
+                c, w = divmod(e, CHUNK_EXPERTS)
+                cols = slice((e - e0) * C, (e - e0 + 1) * C)
+                nc.tensor.matmul_mx(
+                    out=dst,
+                    lhsT=w1_sb[c][:, w, 2 * P * h : 2 * P * (h + 1)].bitcast(FP4X4),
+                    lhsT_scale=plane_of(w1_plane, e)[:, P * h : P * (h + 1)],
+                    rhs=codes[:, cols].bitcast(FP8X4),
+                    rhs_scale=scales[:, cols],
+                    start=True,
+                    stop=True,
+                )
+
+            if e1 == E:
+                for h, name in enumerate(("dx", "dh")):
+                    bank = psum.tile([P, C], F32, name=name)
+                    multiply(bank[:], e0, h)
                     nc.scalar.activation(dx_sb[:, h, e0 * C : e1 * C], bank[:], ACT.Copy, scale=0.5)
-                return
-            for f0 in range(e0, e1, 2):
-                f1 = min(f0 + 2, e1)
-                bank = psum2.tile([P, K // P, (f1 - f0) * C], F32, name="dx_ps")
-                for e in range(f0, f1):
-                    c, w = divmod(e, EPC)
-                    cols = slice((e - e0) * C, (e - e0 + 1) * C)
-                    for h in range(K // P):
-                        nc.tensor.matmul_mx(
-                            out=bank[:, h, (e - f0) * C : (e - f0 + 1) * C],
-                            lhsT=w1_sb[c][:, w, 2 * P * h : 2 * P * (h + 1)].bitcast(FP4X4),
-                            lhsT_scale=plane_of(w1_plane, e)[:, P * h : P * (h + 1)],
-                            rhs=codes[:, cols].bitcast(FP8X4),
-                            rhs_scale=scales[:, cols],
-                            start=True,
-                            stop=True,
-                        )
-                nc.scalar.activation(dx_sb[:, :, f0 * C : f1 * C], bank[:], ACT.Copy, scale=0.5)
+            else:
+                bank = psum.tile([P, K_TILES, (e1 - e0) * C], F32, name="dx")
+                for e in range(e0, e1):
+                    for h in range(K_TILES):
+                        multiply(bank[:, h, (e - e0) * C : (e - e0 + 1) * C], e, h)
+                nc.scalar.activation(dx_sb[:, :, e0 * C : e1 * C], bank[:], ACT.Copy, scale=0.5)
 
-        for e in range(ACT_LEAD):
-            activations(e)
-        for i in range(LEAD):
-            gather(i)
-        quantize_g(0, 0, PAIR)
+        for e in range(ACTIVATION_LEAD):
+            silu_factor(e)
+            tanh_factor(e)
+        for number in range(GATHER_LEAD):
+            gather(number)
+        quantise_g(0, 0, PAIR)
         first_product(0)
-        quantize_g(0, PAIR, CHUNK)
-        for e in range(1, MLEAD):
-            first_product(e)
-        done2 = set()
-        doneq = set()
-        for e in range(E + 6):
-            if e + ACT_LEAD < E and not ACT_LAST:
-                activations(e + ACT_LEAD)
-            if e + LEAD < NCH * PACK:
-                gather(e + LEAD)
-            if e + QLEAD < E and (e + QLEAD) % EPC == 0 and e + QLEAD > 0:
-                quantize_g((e + QLEAD) // EPC, 0, CHUNK)
-            if e + MLEAD < E:
-                first_product(e + MLEAD)
-            if e < E:
-                first_factor(e)
-            for e0, e1 in GROUPS:
-                if e0 not in doneq and all(x in done2 for x in range(e0, e1)):
-                    second_product(e0, e1)
-                    doneq.add(e0)
-            for x in range(E):
-                if x not in done2 and x + (LAG if x >= DEEP else 1) <= e and all(y in done2 for y in range(group_of[x][0], x)):
-                    second_factor(x)
-                    done2.add(x)
-            if e + ACT_LEAD < E and ACT_LAST:
-                activations(e + ACT_LEAD)
+        quantise_g(0, PAIR, CHUNK)
 
-        pieces = ((0, 3), (3, 5))
-        back = {}
+        for e in range(E + 2):
+            if e + ACTIVATION_LEAD < E:
+                silu_factor(e + ACTIVATION_LEAD)
+                tanh_factor(e + ACTIVATION_LEAD)
+            if e + GATHER_LEAD < GATHERS:
+                gather(e + GATHER_LEAD)
+            if e + 1 < E:
+                if (e + 1) % CHUNK_EXPERTS == 0:
+                    quantise_g((e + 1) // CHUNK_EXPERTS, 0, CHUNK)
+                first_product(e + 1)
+            if e < E:
+                apply_tanh_factor(e)
+            for e0, e1 in DA_GROUPS:
+                if e == e1 + 1:
+                    second_product(e0, e1)
+            if 1 <= e <= E:
+                apply_silu_factor(e - 1)
 
         def sum_first_three(h):
-            first3 = ring3.tile([P, TOP - 1, T], F32, name="planes")
-            tags = SUMT
-            banks = [psum2.tile([P, P], F32, name=tag) for tag in tags]
+            first_three = ring3.tile([P, TOP - 1, T], F32, name="gathered")
+            banks = [psum.tile([P, P], F32, name=name) for name in ("a_turned", "a_turned", "dh", "dh", "dx")]
             for r in range(TOP - 1):
-                nc.vector.tensor_copy(first3[:, r, :], dx_sb[:, h, :].indirect(pos_sb[r][:]))
-                for b in range(T // P):
+                nc.vector.tensor_copy(first_three[:, r, :], dx_sb[:, h, :].indirect(pos_sb[r][:]))
+                for b in range(T_BLOCKS):
                     nc.tensor.matmul(
                         banks[b][:],
-                        lhsT=first3[:, r, b * P : (b + 1) * P],
+                        lhsT=first_three[:, r, b * P : (b + 1) * P],
                         rhs=ident[:],
                         start=(r == 0),
                         stop=(r == TOP - 2),
                         is_transpose=True,
                     )
-            sum_t = ring2.tile([P, T // P, P], F32, name="sum_t")
-            for b in range(T // P):
+            sum_t = ring2.tile([P, T_BLOCKS, P], F32, name="sum_t")
+            for b in range(T_BLOCKS):
                 nc.scalar.copy(sum_t[:, b, :], banks[b][:])
             return sum_t
 
-        def turn_back(h, sum_t, blocks):
-            for x, (b0, b1) in enumerate(blocks):
-                back[h, x] = psum2.tile([P, H], F32, name=BACK[h][x])
-                for b in range(b0, b1):
-                    nc.tensor.transpose(back[h, x][:, (b - b0) * P : (b - b0 + 1) * P], sum_t[:, b, :], ident[:])
+        def turn_back(sum_t, b0, b1, name):
+            bank = psum.tile([P, BANK], F32, name=name)
+            for b in range(b0, b1):
+                nc.tensor.transpose(bank[:, (b - b0) * P : (b - b0 + 1) * P], sum_t[:, b, :], ident[:])
+            return bank, b0 * P
 
-        def finish(h, x, first, t0, t1, fourth):
-            nc.vector.tensor_tensor(res[h][:, t0:t1], fourth, back[h, x][:, t0 - first : t1 - first], ALU.add)
+        def finish(h, turned, t0, t1, fourth):
+            bank, first = turned
+            nc.vector.tensor_tensor(res[h][:, t0:t1], fourth, bank[:, t0 - first : t1 - first], ALU.add)
             nc.sync.dma_start(out[h * P : (h + 1) * P, t0:t1], res[h][:, t0:t1])
 
-        sums = [sum_first_three(h) for h in range(K // P)]
-        turn_back(0, sums[0], ((0, 3), (3, 5)))
-        turn_back(1, sums[1], ((0, 3), (2, 5)))
-        res = [ring2.tile([P, T], F32, name="res") for h in range(K // P)]
-        half = T // 2
-        last = keep.tile([P, T], F32, name="last")
-        early = keep.tile([P, half], F32, name="early")
-        nc.vector.tensor_copy(last[:], dx_sb[:, 0, :].indirect(pos_sb[TOP - 1][:]))
-        nc.vector.tensor_copy(early[:], dx_sb[:, 1, :].indirect(pos_sb[TOP - 1][:, 0 : half // 16]))
-        finish(0, 0, 0, 0, 3 * P, last[:, 0 : 3 * P])
-        finish(0, 1, 3 * P, 3 * P, T, last[:, 3 * P : T])
-        nc.vector.tensor_copy(last[:, 0:half], dx_sb[:, 1, :].indirect(pos_sb[TOP - 1][:, half // 16 : T // 16]))
-        finish(1, 0, 0, 0, half, early[:])
-        finish(1, 1, 2 * P, half, T, last[:, 0:half])
+        sums = [sum_first_three(h) for h in range(K_TILES)]
+        cut, half = 3 * P, T // 2
+        low0, high0 = turn_back(sums[0], 0, 3, "half_da"), turn_back(sums[0], 3, T_BLOCKS, "half_da")
+        low1, high1 = turn_back(sums[1], 0, 3, "a_turned"), turn_back(sums[1], 2, T_BLOCKS, "a_turned")
+        res = [ring2.tile([P, T], F32, name="res") for h in range(K_TILES)]
+        fourth_whole = keep.tile([P, T], F32, name="fourth_whole")
+        fourth_half = keep.tile([P, half], F32, name="fourth_half")
+        last_list = pos_sb[TOP - 1]
+        nc.vector.tensor_copy(fourth_whole[:], dx_sb[:, 0, :].indirect(last_list[:]))
+        nc.vector.tensor_copy(fourth_half[:], dx_sb[:, 1, :].indirect(last_list[:, 0 : half // LIST_COL]))
+        finish(0, low0, 0, cut, fourth_whole[:, 0:cut])
+        finish(0, high0, cut, T, fourth_whole[:, cut:T])
+        nc.vector.tensor_copy(fourth_whole[:, 0:half], dx_sb[:, 1, :].indirect(last_list[:, half // LIST_COL : T // LIST_COL]))
+        finish(1, low1, 0, half, fourth_half[:])
+        finish(1, high1, half, T, fourth_whole[:, 0:half])

@@ -61,7 +61,7 @@ def tile_moe_bdx_mlp_silu_kernel(
         w1_sb = [keep.tile([P, CHUNK_EXPERTS, 2 * K], U8, name=f"w1_sb{c}", align_bytes=64) for c in range(CHUNKS)]
         w2_plane = [keep.tile([P, e1 - e0, H], U8, name=f"w2_plane{e0}", align_bytes=64) for e0, e1 in SCALE_GROUPS]
         w1_plane = [keep.tile([P, e1 - e0, K], U8, name=f"w1_plane{e0}", align_bytes=64) for e0, e1 in SCALE_GROUPS]
-        dx_sb = keep.tile([P, K_TILES, S], F32, name="dx_sb")
+        dx_sb = [keep.tile([P, S], F32, name=f"dx_sb{h}") for h in range(K_TILES)]
         ident = keep.tile([P, P], F32, name="ident")
 
         make_identity(nc, ident[:])
@@ -231,13 +231,14 @@ def tile_moe_bdx_mlp_silu_kernel(
                 for h, name in enumerate(("dx", "dh")):
                     bank = psum.tile([P, C], F32, name=name)
                     multiply(bank[:], e0, h)
-                    nc.scalar.activation(dx_sb[:, h, e0 * C : e1 * C], bank[:], ACT.Copy, scale=0.5)
+                    nc.scalar.activation(dx_sb[h][:, e0 * C : e1 * C], bank[:], ACT.Copy, scale=0.5)
             else:
                 bank = psum.tile([P, K_TILES, (e1 - e0) * C], F32, name="dx")
                 for e in range(e0, e1):
                     for h in range(K_TILES):
                         multiply(bank[:, h, (e - e0) * C : (e - e0 + 1) * C], e, h)
-                nc.scalar.activation(dx_sb[:, :, e0 * C : e1 * C], bank[:], ACT.Copy, scale=0.5)
+                for h in range(K_TILES):
+                    nc.scalar.activation(dx_sb[h][:, e0 * C : e1 * C], bank[:, h, :], ACT.Copy, scale=0.5)
 
         for e in range(ACTIVATION_LEAD):
             silu_factor(e)
@@ -266,48 +267,16 @@ def tile_moe_bdx_mlp_silu_kernel(
             if 1 <= e <= E:
                 apply_silu_factor(e - 1)
 
-        def sum_first_three(h):
-            first_three = ring3.tile([P, TOP - 1, T], F32, name="gathered")
-            banks = [psum.tile([P, P], F32, name=name) for name in ("a_turned", "a_turned", "dh", "dh", "dx")]
-            for r in range(TOP - 1):
-                nc.vector.tensor_copy(first_three[:, r, :], dx_sb[:, h, :].indirect(pos_sb[r][:]))
-                for b in range(T_BLOCKS):
-                    nc.tensor.matmul(
-                        banks[b][:],
-                        lhsT=first_three[:, r, b * P : (b + 1) * P],
-                        rhs=ident[:],
-                        start=(r == 0),
-                        stop=(r == TOP - 2),
-                        is_transpose=True,
-                    )
-            sum_t = ring2.tile([P, T_BLOCKS, P], F32, name="sum_t")
-            for b in range(T_BLOCKS):
-                nc.scalar.copy(sum_t[:, b, :], banks[b][:])
-            return sum_t
-
-        def turn_back(sum_t, b0, b1, name):
-            bank = psum.tile([P, BANK], F32, name=name)
-            for b in range(b0, b1):
-                nc.tensor.transpose(bank[:, (b - b0) * P : (b - b0 + 1) * P], sum_t[:, b, :], ident[:])
-            return bank, b0 * P
-
-        def finish(h, turned, t0, t1, fourth):
-            bank, first = turned
-            nc.vector.tensor_tensor(res[h][:, t0:t1], fourth, bank[:, t0 - first : t1 - first], ALU.add)
-            nc.sync.dma_start(out[h * P : (h + 1) * P, t0:t1], res[h][:, t0:t1])
-
-        sums = [sum_first_three(h) for h in range(K_TILES)]
-        cut, half = 3 * P, T // 2
-        low0, high0 = turn_back(sums[0], 0, 3, "half_da"), turn_back(sums[0], 3, T_BLOCKS, "half_da")
-        low1, high1 = turn_back(sums[1], 0, 3, "a_turned"), turn_back(sums[1], 2, T_BLOCKS, "a_turned")
-        res = [ring2.tile([P, T], F32, name="res") for h in range(K_TILES)]
-        fourth_whole = keep.tile([P, T], F32, name="fourth_whole")
-        fourth_half = keep.tile([P, half], F32, name="fourth_half")
-        last_list = pos_sb[TOP - 1]
-        nc.vector.tensor_copy(fourth_whole[:], dx_sb[:, 0, :].indirect(last_list[:]))
-        nc.vector.tensor_copy(fourth_half[:], dx_sb[:, 1, :].indirect(last_list[:, 0 : half // LIST_COL]))
-        finish(0, low0, 0, cut, fourth_whole[:, 0:cut])
-        finish(0, high0, cut, T, fourth_whole[:, cut:T])
-        nc.vector.tensor_copy(fourth_whole[:, 0:half], dx_sb[:, 1, :].indirect(last_list[:, half // LIST_COL : T // LIST_COL]))
-        finish(1, low1, 0, half, fourth_half[:])
-        finish(1, high1, half, T, fourth_whole[:, 0:half])
+        sums = [[keep.tile([P, T], F32, name=f"sum{h}_{r}") for r in range(2)] for h in range(K_TILES)]
+        for r in range(TOP):
+            for h in range(K_TILES):
+                dst, src = sums[h][r % 2], sums[h][(r + 1) % 2]
+                if r == 0:
+                    nc.vector.tensor_copy(dst[:], dx_sb[h][:].indirect(pos_sb[r][:]))
+                    continue
+                cuts = (0, T // 2, T) if (r, h) == (TOP - 1, K_TILES - 1) else (0, T)
+                for t0, t1 in zip(cuts, cuts[1:]):
+                    entries = pos_sb[r][:, t0 // LIST_COL : t1 // LIST_COL]
+                    nc.vector.tensor_tensor(dst[:, t0:t1], dx_sb[h][:].indirect(entries), src[:, t0:t1], ALU.add)
+                    if r == TOP - 1:
+                        nc.sync.dma_start(out[h * P : (h + 1) * P, t0:t1], dst[:, t0:t1])

@@ -9,22 +9,15 @@ S = E * C
 P = 128
 PACK = 4
 LIST_COL = 16
-BANK = 512
 K_TILES = K // P
-T_BLOCKS = T // P
-
-CHUNK_EXPERTS = 4
-CHUNK = CHUNK_EXPERTS * C
-CHUNKS = S // CHUNK
-GATHERS = CHUNKS * PACK
 PAIR = 2 * C
+PAIRS = E // 2
+WIDE = PACK * C
+GATE_COLS = 2 * PAIR
+LEAD = 2
+WORK_TILES = 2
 
-SCALE_GROUPS = ((0, CHUNK_EXPERTS), (CHUNK_EXPERTS, E))
-DA_GROUPS = tuple((e, e + 2) for e in range(0, E - 2, 2)) + ((E - 2, E - 1), (E - 1, E))
-FIRST_CUT = C
-
-GATHER_LEAD = 6
-ACTIVATION_LEAD = 2
+SCALE_GROUPS = ((0, 4), (4, E))
 
 FLOPS = 2 * S * (N * H + H * K)
 BYTES = 4 * (N * T + H * S + S + K * T) + E * (2 * P + 16) * (H + K) + 2 * P * (S + TOP * T) // LIST_COL
@@ -49,45 +42,46 @@ def tile_moe_bdx_mlp_silu_kernel(
         keep = ctx.enter_context(tc.tile_pool(name="keep", bufs=1))
         ring2 = ctx.enter_context(tc.tile_pool(name="ring2", bufs=2))
         ring3 = ctx.enter_context(tc.tile_pool(name="ring3", bufs=3))
-        ring6 = ctx.enter_context(tc.tile_pool(name="ring6", bufs=6))
-        psum = ctx.enter_context(tc.psum_pool(name="psum", bufs=2))
+        banks = ctx.enter_context(tc.psum_pool(name="banks", bufs=1))
+        banks2 = ctx.enter_context(tc.psum_pool(name="banks2", bufs=2))
 
         offs_sb = keep.tile([P, S // LIST_COL], U16, name="offs_sb")
         pos_sb = [keep.tile([P, T // LIST_COL], U16, name=f"pos_sb{r}") for r in range(TOP)]
         dy_sb = [keep.tile([P, T], F32, name=f"dy_sb{j}") for j in range(PACK)]
-        gate_sb = [keep.tile([P, CHUNK], F32, name=f"gate_sb{c}") for c in range(CHUNKS)]
-        a_sb = [keep.tile([P, PACK, PAIR], F32, name=f"a_sb{u}") for u in range(E // 2)]
-        w2_sb = [keep.tile([P, CHUNK_EXPERTS, 2 * H], U8, name=f"w2_sb{c}", align_bytes=64) for c in range(CHUNKS)]
-        w1_sb = [keep.tile([P, CHUNK_EXPERTS, 2 * K], U8, name=f"w1_sb{c}", align_bytes=64) for c in range(CHUNKS)]
+        gate_sb, a_sb, w2_sb, w1_sb = {}, {}, {}, {}
         w2_plane = [keep.tile([P, e1 - e0, H], U8, name=f"w2_plane{e0}", align_bytes=64) for e0, e1 in SCALE_GROUPS]
         w1_plane = [keep.tile([P, e1 - e0, K], U8, name=f"w1_plane{e0}", align_bytes=64) for e0, e1 in SCALE_GROUPS]
         dx_sb = [keep.tile([P, S], F32, name=f"dx_sb{h}") for h in range(K_TILES)]
         ident = keep.tile([P, P], F32, name="ident")
+        work = [keep.tile([P, 5 * WIDE], F32, name=f"work{x}", align_bytes=64) for x in range(WORK_TILES)]
+        first_g = keep.tile([P, 2 * WIDE], F32, name="first_g")
+        first_tanh = keep.tile([P, WIDE], F32, name="first_tanh")
 
         make_identity(nc, ident[:])
         for x in range(len(SCALE_GROUPS)):
-            nc.gpsimd.memset(w2_plane[x][:].bitcast(I32), 0)
+            nc.vector.memset(w2_plane[x][:].bitcast(I32), 0)
             nc.gpsimd.memset(w1_plane[x][:].bitcast(I32), 0)
 
         dy_rows = dyT.rearrange("(p j) t -> p j t", j=PACK)
         a_rows = a.rearrange("(p j) s -> p j s", j=PACK)
 
-        def pieces(is_first):
-            return ((0, FIRST_CUT), (FIRST_CUT, CHUNK)) if is_first else ((0, CHUNK),)
-
         def load_dy(j):
             nc.sync.dma_start(dy_sb[j][:], dy_rows[:, j, :])
 
-        def load_gate(c):
-            for s0, s1 in pieces(c == 0):
-                nc.sync.dma_start(gate_sb[c][:, s0:s1], gate[0:P, c * CHUNK + s0 : c * CHUNK + s1])
+        def load_gate(s0, s1):
+            c, o = divmod(s0, GATE_COLS)
+            if o == 0:
+                gate_sb[c] = ring2.tile([P, GATE_COLS], F32, name="gate_sb")
+            nc.sync.dma_start(gate_sb[c][:, o : o + s1 - s0], gate[0:P, s0:s1])
 
-        def load_a(u):
-            nc.sync.dma_start(a_sb[u][:], a_rows[:, :, u * PAIR : (u + 1) * PAIR])
+        def load_a(n):
+            a_sb[n] = ring3.tile([P, PACK, PAIR], F32, name="a_sb")
+            nc.sync.dma_start(a_sb[n][:], a_rows[:, :, n * PAIR : (n + 1) * PAIR])
 
-        def load_words(tiles, words, c):
-            src = words[c * CHUNK_EXPERTS : (c + 1) * CHUNK_EXPERTS, 0].rearrange("e p b -> p e b")
-            nc.sync.dma_start(tiles[c][:].bitcast(I32), src.bitcast(I32))
+        def load_words(tiles, words, n, name):
+            tiles[n] = ring3.tile([P, 2, words.shape[-1]], U8, name=name, align_bytes=64)
+            src = words[2 * n : 2 * n + 2, 0].rearrange("e p b -> p e b")
+            nc.sync.dma_start(tiles[n][:].bitcast(I32), src.bitcast(I32))
 
         def load_plane(planes, scales, x):
             e0, e1 = SCALE_GROUPS[x]
@@ -95,177 +89,214 @@ def tile_moe_bdx_mlp_silu_kernel(
                 src = scales[e0:e1, 0, 4 * q : 4 * q + 4, :].rearrange("e f i -> f e i")
                 nc.sync.dma_start(planes[x][32 * q : 32 * q + 4, :, :].bitcast(I32), src.bitcast(I32))
 
-        def load_w2(c):
-            load_words(w2_sb, w2_words, c)
-
-        def load_w1(c):
-            load_words(w1_sb, w1_words, c)
-
-        def load_s2(x):
-            load_plane(w2_plane, w2_scales, x)
-
-        def load_s1(x):
-            load_plane(w1_plane, w1_scales, x)
-
         def plane_of(planes, e):
             return [planes[x][:, e - e0, :] for x, (e0, e1) in enumerate(SCALE_GROUPS) if e0 <= e < e1][0]
 
-        load_dy(0)
         nc.sync.dma_start(offs_sb[:], offs)
-        for load, index in (
-            (load_gate, 0), (load_dy, 1), (load_a, 0), (load_dy, 2), (load_dy, 3), (load_gate, 1), (load_a, 1),
-            (load_s2, 0), (load_w2, 0), (load_gate, 2), (load_a, 2), (load_s1, 0), (load_w1, 0), (load_a, 3),
-            (load_s2, 1), (load_w2, 1), (load_gate, 3), (load_a, 4), (load_s1, 1), (load_w1, 1), (load_a, 5),
-            (load_w2, 2), (load_a, 6), (load_gate, 4), (load_w1, 2), (load_a, 7),
-            (load_w2, 3), (load_a, 8), (load_w1, 3), (load_a, 9),
-            (load_w2, 4), (load_w1, 4),
-        ):
-            load(index)
+        load_dy(0)
+        load_gate(0, PAIR)
+        load_gate(PAIR, GATE_COLS)
+        load_dy(1)
+        load_a(0)
+        load_dy(2)
+        load_dy(3)
+        load_plane(w2_plane, w2_scales, 0)
+        load_words(w2_sb, w2_words, 0, "w2_sb")
+        load_gate(GATE_COLS, 2 * GATE_COLS)
+        load_a(1)
+        load_plane(w1_plane, w1_scales, 0)
+        load_words(w2_sb, w2_words, 1, "w2_sb")
+        load_words(w1_sb, w1_words, 0, "w1_sb")
+        load_a(2)
+        load_plane(w2_plane, w2_scales, 1)
+        load_words(w2_sb, w2_words, 2, "w2_sb")
+        load_words(w1_sb, w1_words, 1, "w1_sb")
+        load_plane(w1_plane, w1_scales, 1)
+        load_words(w1_sb, w1_words, 2, "w1_sb")
         for r, pos in enumerate((pos1, pos2, pos3, pos4)):
             nc.sync.dma_start(pos_sb[r][:], pos)
 
-        g_f32, g_bf, g_codes, g_scales = {}, {}, {}, {}
-        tanh_t, silu_neg, dh_ps, half_da_ps, da_bf = {}, {}, {}, {}, {}
-        da_group = {e: (e0, e1) for e0, e1 in DA_GROUPS for e in range(e0, e1)}
+        def refill(n):
+            if n + 4 < PAIRS:
+                load_a(n + 4)
+                load_words(w2_sb, w2_words, n + 4, "w2_sb")
+            if 0 <= n and n + 3 < PAIRS:
+                load_words(w1_sb, w1_words, n + 3, "w1_sb")
+            if n % 2 == 1 and n + 5 < PAIRS:
+                load_gate((n + 5) * PAIR, (n + 7) * PAIR)
 
-        def gather(number):
-            c, j = divmod(number, PACK)
-            if j == 0:
-                g_f32[c] = ring3.tile([P, PACK, CHUNK], F32, name="gathered")
-            for s0, s1 in pieces(number == 0):
-                entries = offs_sb[:, (c * CHUNK + s0) // LIST_COL : (c * CHUNK + s1) // LIST_COL]
-                nc.vector.tensor_tensor(g_f32[c][:, j, s0:s1], dy_sb[j][:].indirect(entries), gate_sb[c][:, s0:s1], ALU.mult)
-            if j == PACK - 1:
-                g_bf[c] = ring2.tile([P, CHUNK, PACK], BF16, name="g_bf", align_bytes=64)
-                for s0 in range(0, CHUNK, PAIR):
-                    nc.scalar.copy(
-                        g_bf[c][:, s0 : s0 + PAIR, :].rearrange("p (s i) j -> p s j i", i=2),
-                        g_f32[c][:, :, s0 : s0 + PAIR].rearrange("p j (s i) -> p s j i", i=2),
-                    )
+        g_bf, g_codes, g_scales, dh_ps, turned, da_bf = {}, {}, {}, {}, {}, {}
 
-        def quantise_g(c, s0, s1):
-            if s0 == 0:
-                g_codes[c] = ring3.tile([P, CHUNK], U32, name="g_codes", align_bytes=64)
-                g_scales[c] = ring3.tile([P, CHUNK], U8, name="g_scales", align_bytes=64)
-            nc.vector.quantize_mx(
-                out=g_codes[c][:, s0:s1].bitcast(FP8X4),
-                scales=g_scales[c][:, s0:s1],
-                in_=g_bf[c][:, s0:s1, :].rearrange("p s j -> p (s j)"),
+        def g_f32(n):
+            return first_g[:] if n == 0 else work[n % WORK_TILES][:, PAIR : PAIR + 2 * WIDE]
+
+        def tanh_of(n, v):
+            if (n, v) == (0, 0):
+                return first_tanh[:]
+            return work[n % WORK_TILES][:, (3 * v + 1) * WIDE : (3 * v + 2) * WIDE]
+
+        def silu_of(n):
+            return work[n % WORK_TILES][:, 2 * WIDE : 4 * WIDE]
+
+        def gather(n, j):
+            c, o = divmod(n * PAIR, GATE_COLS)
+            entries = offs_sb[:, n * PAIR // LIST_COL : (n + 1) * PAIR // LIST_COL]
+            nc.vector.tensor_tensor(
+                g_f32(n)[:, j * PAIR : (j + 1) * PAIR], dy_sb[j][:].indirect(entries), gate_sb[c][:, o : o + PAIR], ALU.mult
             )
 
-        def a_of(e):
-            u, v = divmod(e, 2)
-            return a_sb[u][:, :, v * C : (v + 1) * C]
+        def round_g(n, s0, s1):
+            words = work[0][:, WIDE : 2 * WIDE] if n == 0 else work[(n - 1) % WORK_TILES][:, 0:WIDE]
+            g_bf[n] = words.bitcast(BF16).rearrange("p (s j) -> p s j", j=PACK)
+            planes = g_f32(n).rearrange("p (j s) -> p j s", j=PACK)
+            nc.scalar.copy(
+                g_bf[n][:, s0:s1, :].rearrange("p (s i) j -> p s j i", i=2),
+                planes[:, :, s0:s1].rearrange("p j (s i) -> p s j i", i=2),
+            )
 
-        def silu_factor(e):
-            silu_neg[e] = ring6.tile([P, C, PACK], F32, name="silu_neg")
+        def quantise_g(n, s0, s1):
+            if s0 == 0:
+                g_codes[n] = ring2.tile([P, PAIR], U32, name="g_codes", align_bytes=64)
+                g_scales[n] = ring2.tile([P, PAIR], U8, name="g_scales", align_bytes=64)
+            nc.vector.quantize_mx(
+                out=g_codes[n][:, s0:s1].bitcast(FP8X4),
+                scales=g_scales[n][:, s0:s1],
+                in_=g_bf[n][:, s0:s1, :].rearrange("p s j -> p (s j)"),
+            )
+
+        def silu_factor(n, s0=0, s1=PAIR):
             nc.scalar.activation(
-                silu_neg[e][:].rearrange("p (s i) j -> p s j i", i=2),
-                a_of(e).rearrange("p j (s i) -> p s j i", i=2),
+                silu_of(n)[:, PACK * s0 : PACK * s1].rearrange("p (s i j) -> p s j i", i=2, j=PACK),
+                a_sb[n][:, :, s0:s1].rearrange("p j (s i) -> p s j i", i=2),
                 ACT.Silu,
                 scale=-1.0,
             )
 
-        def tanh_factor(e):
-            a_turned = psum.tile([P, PACK, P], F32, name="a_turned")
-            for j in range(PACK):
-                nc.tensor.transpose(a_turned[:, j, :], a_of(e)[:, j, :], ident[:])
-            tanh_t[e] = ring6.tile([P, PACK, P], F32, name="tanh_t")
-            nc.scalar.activation(tanh_t[e][:], a_turned[:], ACT.Tanh, scale=-0.5)
+        def bank_of(n, v):
+            return banks.tile([P, WIDE], F32, name=f"bank{n % 2}{v}")
 
-        def first_product(e):
-            c, w = divmod(e, CHUNK_EXPERTS)
-            cols = slice(w * C, (w + 1) * C)
-            dh_ps[e] = psum.tile([P, H], F32, name="dh")
+        def tanh_factor(n, v):
+            a_turned = bank_of(n, v)
+            for j in range(PACK):
+                nc.tensor.transpose(a_turned[:, j * P : (j + 1) * P], a_sb[n][:, j, v * C : (v + 1) * C], ident[:])
+            nc.scalar.activation(tanh_of(n, v), a_turned[:], ACT.Tanh, scale=-0.5)
+
+        def first_product(n, v):
+            cols = slice(v * C, (v + 1) * C)
+            dh_ps[n, v] = bank_of(n + 1, v)
             nc.tensor.matmul_mx(
-                out=dh_ps[e][:],
-                lhsT=g_codes[c][:, cols].bitcast(FP8X4),
-                lhsT_scale=g_scales[c][:, cols],
-                rhs=w2_sb[c][:, w, :].bitcast(FP4X4),
-                rhs_scale=plane_of(w2_plane, e),
+                out=dh_ps[n, v][:],
+                lhsT=g_codes[n][:, cols].bitcast(FP8X4),
+                lhsT_scale=g_scales[n][:, cols],
+                rhs=w2_sb[n][:, v, :].bitcast(FP4X4),
+                rhs_scale=plane_of(w2_plane, 2 * n + v),
                 start=True,
                 stop=True,
             )
 
-        def apply_tanh_factor(e):
-            half_da_t = ring3.tile([P, PACK, P], F32, name="half_da_t")
+        def apply_tanh_factor(n, v):
+            half_da_t = ring2.tile([P, PACK, P], F32, name="half_da_t")
             nc.vector.scalar_tensor_tensor(
-                half_da_t[:], tanh_t[e][:], 1.0, dh_ps[e][:].rearrange("s (p j) -> s j p", j=PACK), ALU.subtract, ALU.mult
-            )
-            half_da_ps[e] = psum.tile([P, PACK, C], F32, name="half_da")
-            for j in range(PACK):
-                nc.tensor.transpose(half_da_ps[e][:, j, :], half_da_t[:, j, :], ident[:])
-
-        def apply_silu_factor(e):
-            e0, e1 = da_group[e]
-            if e == e0:
-                da_bf[e0] = ring3.tile([P, (e1 - e0) * C, PACK], BF16, name="da_bf", align_bytes=64)
-            nc.vector.scalar_tensor_tensor(
-                da_bf[e0][:, (e - e0) * C : (e - e0 + 1) * C, :],
-                silu_neg[e][:],
+                half_da_t[:],
+                tanh_of(n, v).rearrange("s (j p) -> s j p", j=PACK),
                 1.0,
-                half_da_ps[e][:].rearrange("p j s -> p s j"),
+                dh_ps[n, v][:].rearrange("s (p j) -> s j p", j=PACK),
+                ALU.subtract,
+                ALU.mult,
+            )
+            turned[n, v] = banks.tile([P, PACK, C], F32, name=f"turned{v}")
+            for j in range(PACK):
+                nc.tensor.transpose(turned[n, v][:, j, :], half_da_t[:, j, :], ident[:])
+
+        def apply_silu_factor(n, v):
+            if v == 0:
+                da_bf[n] = ring2.tile([P, PAIR, PACK], BF16, name="da_bf", align_bytes=64)
+            nc.vector.scalar_tensor_tensor(
+                da_bf[n][:, v * C : (v + 1) * C, :],
+                silu_of(n)[:, v * WIDE : (v + 1) * WIDE].rearrange("p (s j) -> p s j", j=PACK),
+                1.0,
+                turned[n, v][:].rearrange("p j s -> p s j"),
                 ALU.subtract,
                 ALU.mult,
             )
 
-        def second_product(e0, e1):
-            codes = ring3.tile([P, (e1 - e0) * C], U32, name="da_codes", align_bytes=64)
-            scales = ring3.tile([P, (e1 - e0) * C], U8, name="da_scales", align_bytes=64)
-            nc.vector.quantize_mx(out=codes[:].bitcast(FP8X4), scales=scales[:], in_=da_bf[e0][:].rearrange("p s j -> p (s j)"))
-
-            def multiply(dst, e, h):
-                c, w = divmod(e, CHUNK_EXPERTS)
-                cols = slice((e - e0) * C, (e - e0 + 1) * C)
-                nc.tensor.matmul_mx(
-                    out=dst,
-                    lhsT=w1_sb[c][:, w, 2 * P * h : 2 * P * (h + 1)].bitcast(FP4X4),
-                    lhsT_scale=plane_of(w1_plane, e)[:, P * h : P * (h + 1)],
-                    rhs=codes[:, cols].bitcast(FP8X4),
-                    rhs_scale=scales[:, cols],
-                    start=True,
-                    stop=True,
-                )
-
-            if e1 == E:
-                for h, name in enumerate(("dx", "dh")):
-                    bank = psum.tile([P, C], F32, name=name)
-                    multiply(bank[:], e0, h)
-                    nc.scalar.activation(dx_sb[h][:, e0 * C : e1 * C], bank[:], ACT.Copy, scale=0.5)
-            else:
-                bank = psum.tile([P, K_TILES, (e1 - e0) * C], F32, name="dx")
-                for e in range(e0, e1):
-                    for h in range(K_TILES):
-                        multiply(bank[:, h, (e - e0) * C : (e - e0 + 1) * C], e, h)
+        def second_product(n, v0, v1):
+            width = (v1 - v0) * C
+            codes = ring2.tile([P, width], U32, name="da_codes", align_bytes=64)
+            scales = ring2.tile([P, width], U8, name="da_scales", align_bytes=64)
+            nc.vector.quantize_mx(
+                out=codes[:].bitcast(FP8X4), scales=scales[:], in_=da_bf[n][:, v0 * C : v1 * C, :].rearrange("p s j -> p (s j)")
+            )
+            slots = slice(n * PAIR + v0 * C, n * PAIR + v1 * C)
+            last = (n, v1) == (PAIRS - 1, 2)
+            shared = None if last else banks2.tile([P, K_TILES, width], F32, name="dx")
+            for h in range(K_TILES):
+                dst = bank_of(n, h)[:, 0:width] if last else shared[:, h, :]
+                for v in range(v0, v1):
+                    cols = slice((v - v0) * C, (v - v0 + 1) * C)
+                    nc.tensor.matmul_mx(
+                        out=dst[:, cols],
+                        lhsT=w1_sb[n][:, v, 2 * P * h : 2 * P * (h + 1)].bitcast(FP4X4),
+                        lhsT_scale=plane_of(w1_plane, 2 * n + v)[:, P * h : P * (h + 1)],
+                        rhs=codes[:, cols].bitcast(FP8X4),
+                        rhs_scale=scales[:, cols],
+                        start=True,
+                        stop=True,
+                    )
+                if last:
+                    nc.scalar.activation(dx_sb[h][:, slots], dst, ACT.Copy, scale=0.5)
+            if not last:
                 for h in range(K_TILES):
-                    nc.scalar.activation(dx_sb[h][:, e0 * C : e1 * C], bank[:, h, :], ACT.Copy, scale=0.5)
+                    nc.scalar.activation(dx_sb[h][:, slots], shared[:, h, :], ACT.Copy, scale=0.5)
 
-        for e in range(ACTIVATION_LEAD):
-            silu_factor(e)
-            tanh_factor(e)
-        for number in range(GATHER_LEAD):
-            gather(number)
-        quantise_g(0, 0, PAIR)
-        first_product(0)
-        quantise_g(0, PAIR, CHUNK)
+        def halves(n):
+            return ((0, C), (C, PAIR)) if n in (0, PAIRS - 1) else ((0, PAIR),)
 
-        for e in range(E + 2):
-            if e + ACTIVATION_LEAD < E:
-                silu_factor(e + ACTIVATION_LEAD)
-                tanh_factor(e + ACTIVATION_LEAD)
-            if e + GATHER_LEAD < GATHERS:
-                gather(e + GATHER_LEAD)
-            if e + 1 < E:
-                if (e + 1) % CHUNK_EXPERTS == 0:
-                    quantise_g((e + 1) // CHUNK_EXPERTS, 0, CHUNK)
-                first_product(e + 1)
-            if e < E:
-                apply_tanh_factor(e)
-            for e0, e1 in DA_GROUPS:
-                if e == e1 + 1:
-                    second_product(e0, e1)
-            if 1 <= e <= E:
-                apply_silu_factor(e - 1)
+        silu_factor(0, 0, C)
+        for v in range(2):
+            tanh_factor(0, v)
+        for n, j in ((0, 0), (1, 0), (0, 1), (1, 1), (0, 2), (0, 3)):
+            gather(n, j)
+        for s0, s1 in halves(0):
+            round_g(0, s0, s1)
+        silu_factor(0, C, PAIR)
+        gather(1, 2)
+        gather(1, 3)
+        quantise_g(0, 0, C)
+        first_product(0, 0)
+        quantise_g(0, C, PAIR)
+        first_product(0, 1)
+        round_g(1, 0, PAIR)
+        refill(-1)
+
+        for n in range(PAIRS):
+            ahead = n + LEAD
+            for v in range(2):
+                apply_tanh_factor(n, v)
+            if n + 1 < PAIRS:
+                silu_factor(n + 1)
+                for v in range(2):
+                    tanh_factor(n + 1, v)
+            if ahead < PAIRS:
+                for j in (1, 2):
+                    gather(ahead, j)
+            for v in range(2):
+                apply_silu_factor(n, v)
+            if n + 1 < PAIRS:
+                for s0, s1 in halves(n + 1):
+                    quantise_g(n + 1, s0, s1)
+                for v in range(2):
+                    first_product(n + 1, v)
+                second_product(n, 0, 2)
+            else:
+                for v in range(2):
+                    second_product(n, v, v + 1)
+            if ahead < PAIRS:
+                for j in (3, 0):
+                    gather(ahead, j)
+                for s0, s1 in halves(ahead):
+                    round_g(ahead, s0, s1)
+            refill(n)
 
         sums = [[keep.tile([P, T], F32, name=f"sum{h}_{r}") for r in range(2)] for h in range(K_TILES)]
         for r in range(TOP):

@@ -55,6 +55,8 @@ def tile_moe_bdx_mlp_silu_kernel(
         ident = keep.tile([P, P], F32, name="ident")
         work = [keep.tile([P, 5 * WIDE], F32, name=f"work{x}", align_bytes=64) for x in range(WORK_TILES)]
         first_g = keep.tile([P, 2 * WIDE], F32, name="first_g")
+        codes = [keep.tile([P, 3 * C], U32, name=f"codes{x}", align_bytes=64) for x in range(2)]
+        code_scales = [keep.tile([P, PAIR], U8, name=f"code_scales{x}", align_bytes=64) for x in range(2)]
         first_tanh = keep.tile([P, WIDE], F32, name="first_tanh")
 
         make_identity(nc, ident[:])
@@ -156,8 +158,8 @@ def tile_moe_bdx_mlp_silu_kernel(
 
         def quantise_g(n, s0, s1):
             if s0 == 0:
-                g_codes[n] = ring2.tile([P, PAIR], U32, name="g_codes", align_bytes=64)
-                g_scales[n] = ring2.tile([P, PAIR], U8, name="g_scales", align_bytes=64)
+                g_codes[n] = codes[n % 2][:, C : 3 * C]
+                g_scales[n] = code_scales[n % 2]
             nc.vector.quantize_mx(
                 out=g_codes[n][:, s0:s1].bitcast(FP8X4),
                 scales=g_scales[n][:, s0:s1],
@@ -222,10 +224,10 @@ def tile_moe_bdx_mlp_silu_kernel(
 
         def second_product(n, v0, v1):
             width = (v1 - v0) * C
-            codes = ring2.tile([P, width], U32, name="da_codes", align_bytes=64)
-            scales = ring2.tile([P, width], U8, name="da_scales", align_bytes=64)
+            da_codes = codes[(n + 1) % 2][:, v0 * C : v1 * C]
+            scales = code_scales[n % 2][:, v0 * C : v1 * C]
             nc.vector.quantize_mx(
-                out=codes[:].bitcast(FP8X4), scales=scales[:], in_=da_bf[n][:, v0 * C : v1 * C, :].rearrange("p s j -> p (s j)")
+                out=da_codes.bitcast(FP8X4), scales=scales, in_=da_bf[n][:, v0 * C : v1 * C, :].rearrange("p s j -> p (s j)")
             )
             slots = slice(n * PAIR + v0 * C, n * PAIR + v1 * C)
             last = (n, v1) == (PAIRS - 1, 2)
@@ -238,7 +240,7 @@ def tile_moe_bdx_mlp_silu_kernel(
                         out=dst[:, cols],
                         lhsT=w1_sb[n][:, v, 2 * P * h : 2 * P * (h + 1)].bitcast(FP4X4),
                         lhsT_scale=plane_of(w1_plane, 2 * n + v)[:, P * h : P * (h + 1)],
-                        rhs=codes[:, cols].bitcast(FP8X4),
+                        rhs=da_codes[:, cols].bitcast(FP8X4),
                         rhs_scale=scales[:, cols],
                         start=True,
                         stop=True,

@@ -196,6 +196,18 @@ def tile_moe_bdx_mlp_silu_kernel(
                 stop=True,
             )
 
+        def warm_up(n):
+            unread = banks2.tile([P, H], F32, name="dx")
+            nc.tensor.matmul_mx(
+                out=unread[:],
+                lhsT=g_codes[n][:, C:PAIR].bitcast(FP8X4),
+                lhsT_scale=g_scales[n][:, C:PAIR],
+                rhs=w2_sb[n][:, 1, :].bitcast(FP4X4),
+                rhs_scale=plane_of(w2_plane, 2 * n + 1),
+                start=True,
+                stop=True,
+            )
+
         def apply_tanh_factor(n, v):
             half_da_t = ring2.tile([P, PACK, P], F32, name="half_da_t")
             nc.vector.scalar_tensor_tensor(
@@ -289,6 +301,8 @@ def tile_moe_bdx_mlp_silu_kernel(
                     quantise_g(n + 1, s0, s1)
                 for v in range(2):
                     first_product(n + 1, v)
+                if 1 <= n <= 7:
+                    warm_up(n + 1)
                 second_product(n, 0, 2)
             else:
                 for v in range(2):

@@ -12,12 +12,14 @@ LIST_COL = 16
 K_TILES = K // P
 PAIR = 2 * C
 PAIRS = E // 2
+LAST = PAIRS - 1
 WIDE = PACK * C
 GATE_COLS = 2 * PAIR
-LEAD = 2
-WORK_TILES = 2
+GATHER_LEAD = 2
+STREAM_BUFS = 3
 
 SCALE_GROUPS = ((0, 4), (4, E))
+WARM_PAIRS = range(1, 8)
 
 FLOPS = 2 * S * (N * H + H * K)
 BYTES = 4 * (N * T + H * S + S + K * T) + E * (2 * P + 16) * (H + K) + 2 * P * (S + TOP * T) // LIST_COL
@@ -41,7 +43,7 @@ def tile_moe_bdx_mlp_silu_kernel(
     with ExitStack() as ctx:
         keep = ctx.enter_context(tc.tile_pool(name="keep", bufs=1))
         ring2 = ctx.enter_context(tc.tile_pool(name="ring2", bufs=2))
-        ring3 = ctx.enter_context(tc.tile_pool(name="ring3", bufs=3))
+        ring3 = ctx.enter_context(tc.tile_pool(name="ring3", bufs=STREAM_BUFS))
         banks = ctx.enter_context(tc.psum_pool(name="banks", bufs=1))
         banks2 = ctx.enter_context(tc.psum_pool(name="banks2", bufs=2))
 
@@ -53,10 +55,11 @@ def tile_moe_bdx_mlp_silu_kernel(
         w1_plane = [keep.tile([P, e1 - e0, K], U8, name=f"w1_plane{e0}", align_bytes=64) for e0, e1 in SCALE_GROUPS]
         dx_sb = [keep.tile([P, S], F32, name=f"dx_sb{h}") for h in range(K_TILES)]
         ident = keep.tile([P, P], F32, name="ident")
-        work = [keep.tile([P, 5 * WIDE], F32, name=f"work{x}", align_bytes=64) for x in range(WORK_TILES)]
+        work = [keep.tile([P, 5 * WIDE], F32, name=f"work{x}", align_bytes=64) for x in range(2)]
         first_g = keep.tile([P, 2 * WIDE], F32, name="first_g")
         codes = [keep.tile([P, 3 * C], U32, name=f"codes{x}", align_bytes=64) for x in range(2)]
         code_scales = [keep.tile([P, PAIR], U8, name=f"code_scales{x}", align_bytes=64) for x in range(2)]
+        last_tanh = keep.tile([P, 2 * WIDE], F32, name="last_tanh")
         first_tanh = keep.tile([P, WIDE], F32, name="first_tanh")
 
         make_identity(nc, ident[:])
@@ -71,10 +74,10 @@ def tile_moe_bdx_mlp_silu_kernel(
             nc.sync.dma_start(dy_sb[j][:], dy_rows[:, j, :])
 
         def load_gate(s0, s1):
-            c, o = divmod(s0, GATE_COLS)
-            if o == 0:
+            c, first = divmod(s0, GATE_COLS)
+            if first == 0:
                 gate_sb[c] = ring2.tile([P, GATE_COLS], F32, name="gate_sb")
-            nc.sync.dma_start(gate_sb[c][:, o : o + s1 - s0], gate[0:P, s0:s1])
+            nc.sync.dma_start(gate_sb[c][:, first : first + s1 - s0], gate[0:P, s0:s1])
 
         def load_a(n):
             a_sb[n] = ring3.tile([P, PACK, PAIR], F32, name="a_sb")
@@ -85,10 +88,16 @@ def tile_moe_bdx_mlp_silu_kernel(
             src = words[2 * n : 2 * n + 2, 0].rearrange("e p b -> p e b")
             nc.sync.dma_start(tiles[n][:].bitcast(I32), src.bitcast(I32))
 
-        def load_plane(planes, scales, x):
+        def load_w2(n):
+            load_words(w2_sb, w2_words, n, "w2_sb")
+
+        def load_w1(n):
+            load_words(w1_sb, w1_words, n, "w1_sb")
+
+        def load_plane(planes, scale_rows, x):
             e0, e1 = SCALE_GROUPS[x]
             for q in range(4):
-                src = scales[e0:e1, 0, 4 * q : 4 * q + 4, :].rearrange("e f i -> f e i")
+                src = scale_rows[e0:e1, 0, 4 * q : 4 * q + 4, :].rearrange("e f i -> f e i")
                 nc.sync.dma_start(planes[x][32 * q : 32 * q + 4, :, :].bitcast(I32), src.bitcast(I32))
 
         def plane_of(planes, e):
@@ -103,110 +112,111 @@ def tile_moe_bdx_mlp_silu_kernel(
         load_dy(2)
         load_dy(3)
         load_plane(w2_plane, w2_scales, 0)
-        load_words(w2_sb, w2_words, 0, "w2_sb")
+        load_w2(0)
         load_gate(GATE_COLS, 2 * GATE_COLS)
         load_a(1)
         load_plane(w1_plane, w1_scales, 0)
-        load_words(w2_sb, w2_words, 1, "w2_sb")
-        load_words(w1_sb, w1_words, 0, "w1_sb")
+        load_w2(1)
+        load_w1(0)
         load_a(2)
         load_plane(w2_plane, w2_scales, 1)
-        load_words(w2_sb, w2_words, 2, "w2_sb")
-        load_words(w1_sb, w1_words, 1, "w1_sb")
+        load_w2(2)
+        load_w1(1)
         load_plane(w1_plane, w1_scales, 1)
-        load_words(w1_sb, w1_words, 2, "w1_sb")
+        load_w1(2)
         for r, pos in enumerate((pos1, pos2, pos3, pos4)):
             nc.sync.dma_start(pos_sb[r][:], pos)
 
         def refill(n):
-            if n + 4 < PAIRS:
-                load_a(n + 4)
-                load_words(w2_sb, w2_words, n + 4, "w2_sb")
-            if 0 <= n and n + 3 < PAIRS:
-                load_words(w1_sb, w1_words, n + 3, "w1_sb")
-            if n % 2 == 1 and n + 5 < PAIRS:
-                load_gate((n + 5) * PAIR, (n + 7) * PAIR)
+            if n + 1 + STREAM_BUFS < PAIRS:
+                load_a(n + 1 + STREAM_BUFS)
+                load_w2(n + 1 + STREAM_BUFS)
+            if 0 <= n < PAIRS - STREAM_BUFS:
+                load_w1(n + STREAM_BUFS)
+            first_pair = n + GATHER_LEAD + 3
+            if n % 2 == 1 and first_pair < PAIRS:
+                load_gate(first_pair * PAIR, first_pair * PAIR + GATE_COLS)
 
-        g_bf, g_codes, g_scales, dh_ps, turned, da_bf = {}, {}, {}, {}, {}, {}
+        g_bf, dh_ps, turned, da_bf = {}, {}, {}, {}
+
+        def part(n, x0, x1):
+            return work[n % 2][:, x0 * WIDE : x1 * WIDE]
 
         def g_f32(n):
-            return first_g[:] if n == 0 else work[n % WORK_TILES][:, PAIR : PAIR + 2 * WIDE]
+            return first_g[:] if n == 0 else work[n % 2][:, PAIR : PAIR + 2 * WIDE]
 
         def tanh_of(n, v):
             if (n, v) == (0, 0):
                 return first_tanh[:]
-            return work[n % WORK_TILES][:, (3 * v + 1) * WIDE : (3 * v + 2) * WIDE]
+            if n == LAST:
+                return last_tanh[:, v * WIDE : (v + 1) * WIDE]
+            return part(n, 1, 2) if v == 0 else part(n, 4, 5)
 
-        def silu_of(n):
-            return work[n % WORK_TILES][:, 2 * WIDE : 4 * WIDE]
+        def g_codes(n):
+            return codes[n % 2][:, C : 3 * C]
 
         def gather(n, j):
-            c, o = divmod(n * PAIR, GATE_COLS)
+            c, first = divmod(n * PAIR, GATE_COLS)
             entries = offs_sb[:, n * PAIR // LIST_COL : (n + 1) * PAIR // LIST_COL]
             nc.vector.tensor_tensor(
-                g_f32(n)[:, j * PAIR : (j + 1) * PAIR], dy_sb[j][:].indirect(entries), gate_sb[c][:, o : o + PAIR], ALU.mult
+                g_f32(n)[:, j * PAIR : (j + 1) * PAIR],
+                dy_sb[j][:].indirect(entries),
+                gate_sb[c][:, first : first + PAIR],
+                ALU.mult,
             )
 
         def round_g(n, s0, s1):
-            words = work[0][:, WIDE : 2 * WIDE] if n == 0 else work[(n - 1) % WORK_TILES][:, 0:WIDE]
+            words = part(0, 1, 2) if n == 0 else part(n - 1, 0, 1)
             g_bf[n] = words.bitcast(BF16).rearrange("p (s j) -> p s j", j=PACK)
-            planes = g_f32(n).rearrange("p (j s) -> p j s", j=PACK)
+            by_j = g_f32(n).rearrange("p (j s) -> p j s", j=PACK)
             nc.scalar.copy(
                 g_bf[n][:, s0:s1, :].rearrange("p (s i) j -> p s j i", i=2),
-                planes[:, :, s0:s1].rearrange("p j (s i) -> p s j i", i=2),
+                by_j[:, :, s0:s1].rearrange("p j (s i) -> p s j i", i=2),
             )
 
         def quantise_g(n, s0, s1):
-            if s0 == 0:
-                g_codes[n] = codes[n % 2][:, C : 3 * C]
-                g_scales[n] = code_scales[n % 2]
             nc.vector.quantize_mx(
-                out=g_codes[n][:, s0:s1].bitcast(FP8X4),
-                scales=g_scales[n][:, s0:s1],
+                out=g_codes(n)[:, s0:s1].bitcast(FP8X4),
+                scales=code_scales[n % 2][:, s0:s1],
                 in_=g_bf[n][:, s0:s1, :].rearrange("p s j -> p (s j)"),
             )
 
-        def silu_factor(n, s0=0, s1=PAIR):
+        def silu_factor(n, s0, s1):
             nc.scalar.activation(
-                silu_of(n)[:, PACK * s0 : PACK * s1].rearrange("p (s i j) -> p s j i", i=2, j=PACK),
+                part(n, 2, 4)[:, PACK * s0 : PACK * s1].rearrange("p (s i j) -> p s j i", i=2, j=PACK),
                 a_sb[n][:, :, s0:s1].rearrange("p j (s i) -> p s j i", i=2),
                 ACT.Silu,
                 scale=-1.0,
             )
 
-        def bank_of(n, v):
-            return banks.tile([P, WIDE], F32, name=f"bank{n % 2}{v}")
+        def bank(side, v):
+            return banks.tile([P, WIDE], F32, name=f"bank{side}{v}")
 
         def tanh_factor(n, v):
-            a_turned = bank_of(n, v)
+            a_turned = bank(min(n, LAST - 1) % 2, v)
             for j in range(PACK):
                 nc.tensor.transpose(a_turned[:, j * P : (j + 1) * P], a_sb[n][:, j, v * C : (v + 1) * C], ident[:])
             nc.scalar.activation(tanh_of(n, v), a_turned[:], ACT.Tanh, scale=-0.5)
 
-        def first_product(n, v):
+        def multiply_w2(dst, n, v):
             cols = slice(v * C, (v + 1) * C)
-            dh_ps[n, v] = bank_of(n + 1, v)
             nc.tensor.matmul_mx(
-                out=dh_ps[n, v][:],
-                lhsT=g_codes[n][:, cols].bitcast(FP8X4),
-                lhsT_scale=g_scales[n][:, cols],
+                out=dst[:],
+                lhsT=g_codes(n)[:, cols].bitcast(FP8X4),
+                lhsT_scale=code_scales[n % 2][:, cols],
                 rhs=w2_sb[n][:, v, :].bitcast(FP4X4),
                 rhs_scale=plane_of(w2_plane, 2 * n + v),
                 start=True,
                 stop=True,
             )
 
+        def first_product(n, v):
+            dh_ps[n, v] = bank((n + 1) % 2, v)
+            multiply_w2(dh_ps[n, v], n, v)
+
         def warm_up(n):
             unread = banks2.tile([P, H], F32, name="dx")
-            nc.tensor.matmul_mx(
-                out=unread[:],
-                lhsT=g_codes[n][:, C:PAIR].bitcast(FP8X4),
-                lhsT_scale=g_scales[n][:, C:PAIR],
-                rhs=w2_sb[n][:, 1, :].bitcast(FP4X4),
-                rhs_scale=plane_of(w2_plane, 2 * n + 1),
-                start=True,
-                stop=True,
-            )
+            multiply_w2(unread, n, 1)
 
         def apply_tanh_factor(n, v):
             half_da_t = ring2.tile([P, PACK, P], F32, name="half_da_t")
@@ -227,68 +237,76 @@ def tile_moe_bdx_mlp_silu_kernel(
                 da_bf[n] = ring2.tile([P, PAIR, PACK], BF16, name="da_bf", align_bytes=64)
             nc.vector.scalar_tensor_tensor(
                 da_bf[n][:, v * C : (v + 1) * C, :],
-                silu_of(n)[:, v * WIDE : (v + 1) * WIDE].rearrange("p (s j) -> p s j", j=PACK),
+                part(n, 2 + v, 3 + v).rearrange("p (s j) -> p s j", j=PACK),
                 1.0,
                 turned[n, v][:].rearrange("p j s -> p s j"),
                 ALU.subtract,
                 ALU.mult,
             )
 
-        def second_product(n, v0, v1):
-            width = (v1 - v0) * C
-            da_codes = codes[(n + 1) % 2][:, v0 * C : v1 * C]
-            scales = code_scales[n % 2][:, v0 * C : v1 * C]
+        def quantise_da(n, v0, v1):
             nc.vector.quantize_mx(
-                out=da_codes.bitcast(FP8X4), scales=scales, in_=da_bf[n][:, v0 * C : v1 * C, :].rearrange("p s j -> p (s j)")
+                out=codes[(n + 1) % 2][:, v0 * C : v1 * C].bitcast(FP8X4),
+                scales=code_scales[n % 2][:, v0 * C : v1 * C],
+                in_=da_bf[n][:, v0 * C : v1 * C, :].rearrange("p s j -> p (s j)"),
             )
-            slots = slice(n * PAIR + v0 * C, n * PAIR + v1 * C)
-            last = (n, v1) == (PAIRS - 1, 2)
-            shared = None if last else banks2.tile([P, K_TILES, width], F32, name="dx")
-            for h in range(K_TILES):
-                dst = bank_of(n, h)[:, 0:width] if last else shared[:, h, :]
-                for v in range(v0, v1):
-                    cols = slice((v - v0) * C, (v - v0 + 1) * C)
-                    nc.tensor.matmul_mx(
-                        out=dst[:, cols],
-                        lhsT=w1_sb[n][:, v, 2 * P * h : 2 * P * (h + 1)].bitcast(FP4X4),
-                        lhsT_scale=plane_of(w1_plane, 2 * n + v)[:, P * h : P * (h + 1)],
-                        rhs=da_codes[:, cols].bitcast(FP8X4),
-                        rhs_scale=scales[:, cols],
-                        start=True,
-                        stop=True,
-                    )
-                if last:
-                    nc.scalar.activation(dx_sb[h][:, slots], dst, ACT.Copy, scale=0.5)
-            if not last:
-                for h in range(K_TILES):
-                    nc.scalar.activation(dx_sb[h][:, slots], shared[:, h, :], ACT.Copy, scale=0.5)
 
-        def halves(n):
-            return ((0, C), (C, PAIR)) if n in (0, PAIRS - 1) else ((0, PAIR),)
+        def multiply_w1(dst, n, v, h):
+            cols = slice(v * C, (v + 1) * C)
+            nc.tensor.matmul_mx(
+                out=dst,
+                lhsT=w1_sb[n][:, v, 2 * P * h : 2 * P * (h + 1)].bitcast(FP4X4),
+                lhsT_scale=plane_of(w1_plane, 2 * n + v)[:, P * h : P * (h + 1)],
+                rhs=codes[(n + 1) % 2][:, cols].bitcast(FP8X4),
+                rhs_scale=code_scales[n % 2][:, cols],
+                start=True,
+                stop=True,
+            )
+
+        def second_product(n, v0, v1):
+            dx_ps = banks2.tile([P, K_TILES, (v1 - v0) * C], F32, name="dx")
+            for h in range(K_TILES):
+                for v in range(v0, v1):
+                    multiply_w1(dx_ps[:, h, (v - v0) * C : (v - v0 + 1) * C], n, v, h)
+            for h in range(K_TILES):
+                nc.scalar.activation(dx_sb[h][:, n * PAIR + v0 * C : n * PAIR + v1 * C], dx_ps[:, h, :], ACT.Copy, scale=0.5)
+
+        def last_second_product():
+            for h in range(K_TILES):
+                dx_ps = bank(LAST % 2, h)[:, 0:C]
+                multiply_w1(dx_ps, LAST, 1, h)
+                nc.scalar.activation(dx_sb[h][:, S - C : S], dx_ps, ACT.Copy, scale=0.5)
+
+        def pieces(n):
+            return ((0, C), (C, PAIR)) if n in (0, LAST) else ((0, PAIR),)
 
         silu_factor(0, 0, C)
         for v in range(2):
             tanh_factor(0, v)
-        for n, j in ((0, 0), (1, 0), (0, 1), (1, 1), (0, 2), (0, 3)):
-            gather(n, j)
-        for s0, s1 in halves(0):
+        for j in range(PACK):
+            gather(0, j)
+            if j < 2:
+                gather(1, j)
+        for s0, s1 in pieces(0):
             round_g(0, s0, s1)
         silu_factor(0, C, PAIR)
-        gather(1, 2)
-        gather(1, 3)
-        quantise_g(0, 0, C)
-        first_product(0, 0)
-        quantise_g(0, C, PAIR)
-        first_product(0, 1)
+        for j in (2, 3):
+            gather(1, j)
+        for v in range(2):
+            quantise_g(0, v * C, (v + 1) * C)
+            first_product(0, v)
         round_g(1, 0, PAIR)
         refill(-1)
 
         for n in range(PAIRS):
-            ahead = n + LEAD
+            ahead = n + GATHER_LEAD
             for v in range(2):
                 apply_tanh_factor(n, v)
-            if n + 1 < PAIRS:
-                silu_factor(n + 1)
+            if n == LAST:
+                second_product(n - 1, 0, 2)
+            else:
+                silu_factor(n + 1, 0, PAIR)
+            if n + 1 < LAST:
                 for v in range(2):
                     tanh_factor(n + 1, v)
             if ahead < PAIRS:
@@ -296,34 +314,41 @@ def tile_moe_bdx_mlp_silu_kernel(
                     gather(ahead, j)
             for v in range(2):
                 apply_silu_factor(n, v)
-            if n + 1 < PAIRS:
-                for s0, s1 in halves(n + 1):
+            if n < LAST:
+                for s0, s1 in pieces(n + 1):
                     quantise_g(n + 1, s0, s1)
                 for v in range(2):
                     first_product(n + 1, v)
-                if 1 <= n <= 7:
+                if n + 1 in WARM_PAIRS:
                     warm_up(n + 1)
-                second_product(n, 0, 2)
+                quantise_da(n, 0, 2)
+                if n + 1 < LAST:
+                    second_product(n, 0, 2)
             else:
-                for v in range(2):
-                    second_product(n, v, v + 1)
+                quantise_da(n, 0, 1)
+                second_product(n, 0, 1)
+                quantise_da(n, 1, 2)
+                last_second_product()
             if ahead < PAIRS:
                 for j in (3, 0):
                     gather(ahead, j)
-                for s0, s1 in halves(ahead):
+                for s0, s1 in pieces(ahead):
                     round_g(ahead, s0, s1)
+            if ahead == LAST:
+                for v in range(2):
+                    tanh_factor(LAST, v)
             refill(n)
 
-        sums = [[keep.tile([P, T], F32, name=f"sum{h}_{r}") for r in range(2)] for h in range(K_TILES)]
+        sums = [[keep.tile([P, T], F32, name=f"sum{h}_{x}") for x in range(2)] for h in range(K_TILES)]
         for r in range(TOP):
             for h in range(K_TILES):
-                dst, src = sums[h][r % 2], sums[h][(r + 1) % 2]
+                dst, so_far = sums[h][r % 2], sums[h][(r + 1) % 2]
                 if r == 0:
                     nc.vector.tensor_copy(dst[:], dx_sb[h][:].indirect(pos_sb[r][:]))
                     continue
                 cuts = (0, T // 2, T) if (r, h) == (TOP - 1, K_TILES - 1) else (0, T)
                 for t0, t1 in zip(cuts, cuts[1:]):
                     entries = pos_sb[r][:, t0 // LIST_COL : t1 // LIST_COL]
-                    nc.vector.tensor_tensor(dst[:, t0:t1], dx_sb[h][:].indirect(entries), src[:, t0:t1], ALU.add)
+                    nc.vector.tensor_tensor(dst[:, t0:t1], dx_sb[h][:].indirect(entries), so_far[:, t0:t1], ALU.add)
                     if r == TOP - 1:
                         nc.sync.dma_start(out[h * P : (h + 1) * P, t0:t1], dst[:, t0:t1])

@@ -15,11 +15,13 @@ PAIRS = E // 2
 LAST = PAIRS - 1
 WIDE = PACK * C
 GATE_COLS = 2 * PAIR
-GATHER_LEAD = 2
 STREAM_BUFS = 3
+A_BUFS = 4
+SILU_BUFS = 8
 
-SCALE_GROUPS = ((0, 4), (4, E))
-WARM_PAIRS = range(1, 8)
+W2_GROUPS = ((0, 2), (2, 6), (6, E))
+W1_GROUPS = ((0, 6), (6, E))
+WARM_PAIRS = range(2, 9)
 
 FLOPS = 2 * S * (N * H + H * K)
 BYTES = 4 * (N * T + H * S + S + K * T) + E * (2 * P + 16) * (H + K) + 2 * P * (S + TOP * T) // LIST_COL
@@ -44,6 +46,8 @@ def tile_moe_bdx_mlp_silu_kernel(
         keep = ctx.enter_context(tc.tile_pool(name="keep", bufs=1))
         ring2 = ctx.enter_context(tc.tile_pool(name="ring2", bufs=2))
         ring3 = ctx.enter_context(tc.tile_pool(name="ring3", bufs=STREAM_BUFS))
+        a_ring = ctx.enter_context(tc.tile_pool(name="a_ring", bufs=A_BUFS))
+        silu_ring = ctx.enter_context(tc.tile_pool(name="silu_ring", bufs=SILU_BUFS))
         banks = ctx.enter_context(tc.psum_pool(name="banks", bufs=1))
         banks2 = ctx.enter_context(tc.psum_pool(name="banks2", bufs=2))
 
@@ -51,21 +55,21 @@ def tile_moe_bdx_mlp_silu_kernel(
         pos_sb = [keep.tile([P, T // LIST_COL], U16, name=f"pos_sb{r}") for r in range(TOP)]
         dy_sb = [keep.tile([P, T], F32, name=f"dy_sb{j}") for j in range(PACK)]
         gate_sb, a_sb, w2_sb, w1_sb = {}, {}, {}, {}
-        w2_plane = [keep.tile([P, e1 - e0, H], U8, name=f"w2_plane{e0}", align_bytes=64) for e0, e1 in SCALE_GROUPS]
-        w1_plane = [keep.tile([P, e1 - e0, K], U8, name=f"w1_plane{e0}", align_bytes=64) for e0, e1 in SCALE_GROUPS]
+        w2_plane = {g: keep.tile([P, g[1] - g[0], H], U8, name=f"w2_plane{g[0]}", align_bytes=64) for g in W2_GROUPS}
+        w1_plane = {g: keep.tile([P, g[1] - g[0], K], U8, name=f"w1_plane{g[0]}", align_bytes=64) for g in W1_GROUPS}
         dx_sb = [keep.tile([P, S], F32, name=f"dx_sb{h}") for h in range(K_TILES)]
         ident = keep.tile([P, P], F32, name="ident")
-        work = [keep.tile([P, 5 * WIDE], F32, name=f"work{x}", align_bytes=64) for x in range(2)]
-        first_g = keep.tile([P, 2 * WIDE], F32, name="first_g")
-        codes = [keep.tile([P, 3 * C], U32, name=f"codes{x}", align_bytes=64) for x in range(2)]
-        code_scales = [keep.tile([P, PAIR], U8, name=f"code_scales{x}", align_bytes=64) for x in range(2)]
-        last_tanh = keep.tile([P, 2 * WIDE], F32, name="last_tanh")
-        first_tanh = keep.tile([P, WIDE], F32, name="first_tanh")
+        work = [keep.tile([P, 3 * WIDE], F32, name=f"work{x}", align_bytes=64) for x in range(3)]
+        code_scales = [keep.tile([P, 2 * PAIR], U8, name=f"code_scales{x}", align_bytes=64) for x in range(2)]
 
+        silu = {0: silu_ring.tile([P, WIDE], F32, name="silu")}
+        zero = silu[0][:, 0:1]
+        nc.vector.memset(zero, 0.0)
+        for g in W2_GROUPS:
+            nc.vector.memset(w2_plane[g][:].bitcast(I32), 0)
         make_identity(nc, ident[:])
-        for x in range(len(SCALE_GROUPS)):
-            nc.vector.memset(w2_plane[x][:].bitcast(I32), 0)
-            nc.gpsimd.memset(w1_plane[x][:].bitcast(I32), 0)
+        for g in W1_GROUPS:
+            nc.gpsimd.memset(w1_plane[g][:].bitcast(I32), 0)
 
         dy_rows = dyT.rearrange("(p j) t -> p j t", j=PACK)
         a_rows = a.rearrange("(p j) s -> p j s", j=PACK)
@@ -73,14 +77,14 @@ def tile_moe_bdx_mlp_silu_kernel(
         def load_dy(j):
             nc.sync.dma_start(dy_sb[j][:], dy_rows[:, j, :])
 
-        def load_gate(s0, s1):
-            c, first = divmod(s0, GATE_COLS)
-            if first == 0:
-                gate_sb[c] = ring2.tile([P, GATE_COLS], F32, name="gate_sb")
+        def load_gate(c):
+            gate_sb[c] = ring3.tile([P, GATE_COLS], F32, name="gate_sb")
+            s0, s1 = max((2 * c - 1) * PAIR, 0), min((2 * c + 1) * PAIR, S)
+            first = s0 - (2 * c - 1) * PAIR
             nc.sync.dma_start(gate_sb[c][:, first : first + s1 - s0], gate[0:P, s0:s1])
 
         def load_a(n):
-            a_sb[n] = ring3.tile([P, PACK, PAIR], F32, name="a_sb")
+            a_sb[n] = a_ring.tile([P, PACK, PAIR], F32, name="a_sb")
             nc.sync.dma_start(a_sb[n][:], a_rows[:, :, n * PAIR : (n + 1) * PAIR])
 
         def load_words(tiles, words, n, name):
@@ -94,100 +98,103 @@ def tile_moe_bdx_mlp_silu_kernel(
         def load_w1(n):
             load_words(w1_sb, w1_words, n, "w1_sb")
 
-        def load_plane(planes, scale_rows, x):
-            e0, e1 = SCALE_GROUPS[x]
-            for q in range(4):
-                src = scale_rows[e0:e1, 0, 4 * q : 4 * q + 4, :].rearrange("e f i -> f e i")
-                nc.sync.dma_start(planes[x][32 * q : 32 * q + 4, :, :].bitcast(I32), src.bitcast(I32))
+        def load_plane(planes, scale_rows, g):
+            for r in range(4):
+                src = scale_rows[g[0] : g[1], 0, r:16:4, :].rearrange("e f i -> f e i")
+                nc.sync.dma_start(planes[g][r:P:32, :, :].bitcast(I32), src.bitcast(I32))
 
         def plane_of(planes, e):
-            return [planes[x][:, e - e0, :] for x, (e0, e1) in enumerate(SCALE_GROUPS) if e0 <= e < e1][0]
+            return [plane[:, e - e0, :] for (e0, e1), plane in planes.items() if e0 <= e < e1][0]
 
         nc.sync.dma_start(offs_sb[:], offs)
-        load_dy(0)
-        load_gate(0, PAIR)
-        load_gate(PAIR, GATE_COLS)
-        load_dy(1)
+        load_gate(0)
+        for j in range(PACK):
+            load_dy(j)
+        load_gate(1)
         load_a(0)
-        load_dy(2)
-        load_dy(3)
-        load_plane(w2_plane, w2_scales, 0)
         load_w2(0)
-        load_gate(GATE_COLS, 2 * GATE_COLS)
+        load_plane(w2_plane, w2_scales, W2_GROUPS[0])
         load_a(1)
-        load_plane(w1_plane, w1_scales, 0)
         load_w2(1)
+        load_gate(2)
         load_w1(0)
+        load_plane(w2_plane, w2_scales, W2_GROUPS[1])
         load_a(2)
-        load_plane(w2_plane, w2_scales, 1)
+        load_plane(w1_plane, w1_scales, W1_GROUPS[0])
         load_w2(2)
         load_w1(1)
-        load_plane(w1_plane, w1_scales, 1)
         load_w1(2)
+        load_a(3)
+        load_plane(w2_plane, w2_scales, W2_GROUPS[2])
+        load_plane(w1_plane, w1_scales, W1_GROUPS[1])
         for r, pos in enumerate((pos1, pos2, pos3, pos4)):
             nc.sync.dma_start(pos_sb[r][:], pos)
 
         def refill(n):
+            if n % 2 == 0 or n < 0:
+                c = (n + 2) // 2 + STREAM_BUFS
+                if (2 * c - 1) < PAIRS:
+                    load_gate(c)
+            if n + 1 + A_BUFS < PAIRS:
+                load_a(n + 1 + A_BUFS)
             if n + 1 + STREAM_BUFS < PAIRS:
-                load_a(n + 1 + STREAM_BUFS)
                 load_w2(n + 1 + STREAM_BUFS)
-            if 0 <= n < PAIRS - STREAM_BUFS:
-                load_w1(n + STREAM_BUFS)
-            first_pair = n + GATHER_LEAD + 3
-            if n % 2 == 1 and first_pair < PAIRS:
-                load_gate(first_pair * PAIR, first_pair * PAIR + GATE_COLS)
+            if 1 <= n <= PAIRS - STREAM_BUFS:
+                load_w1(n - 1 + STREAM_BUFS)
 
-        g_bf, dh_ps, turned, da_bf = {}, {}, {}, {}
+        dh_ps, turned, odd_tanh, codes = {}, {}, {}, {}
 
-        def part(n, x0, x1):
-            return work[n % 2][:, x0 * WIDE : x1 * WIDE]
+        def part(m, x0, x1):
+            return work[m % 3][:, x0 * WIDE : x1 * WIDE]
 
-        def g_f32(n):
-            return first_g[:] if n == 0 else work[n % 2][:, PAIR : PAIR + 2 * WIDE]
+        def rounded(n):
+            return part(n, 1, 3).bitcast(BF16).rearrange("p (s j) -> p s j", j=PACK)
 
-        def tanh_of(n, v):
-            if (n, v) == (0, 0):
-                return first_tanh[:]
-            if n == LAST:
-                return last_tanh[:, v * WIDE : (v + 1) * WIDE]
-            return part(n, 1, 2) if v == 0 else part(n, 4, 5)
+        def odd_bytes(n, dtype):
+            return keep.tile([P, WIDE], dtype, name=f"odd{n % 2}", align_bytes=64)
 
-        def g_codes(n):
-            return codes[n % 2][:, C : 3 * C]
-
-        def gather(n, j):
-            c, first = divmod(n * PAIR, GATE_COLS)
-            entries = offs_sb[:, n * PAIR // LIST_COL : (n + 1) * PAIR // LIST_COL]
+        def gather(m, j):
+            c, half = divmod(m + 1, 2)
+            entries = offs_sb[:, m * PAIR // LIST_COL : (m + 1) * PAIR // LIST_COL]
             nc.vector.tensor_tensor(
-                g_f32(n)[:, j * PAIR : (j + 1) * PAIR],
+                part(m, 0, 2)[:, j * PAIR : (j + 1) * PAIR],
                 dy_sb[j][:].indirect(entries),
-                gate_sb[c][:, first : first + PAIR],
+                gate_sb[c][:, half * PAIR : (half + 1) * PAIR],
                 ALU.mult,
             )
 
-        def round_g(n, s0, s1):
-            words = part(0, 1, 2) if n == 0 else part(n - 1, 0, 1)
-            g_bf[n] = words.bitcast(BF16).rearrange("p (s j) -> p s j", j=PACK)
-            by_j = g_f32(n).rearrange("p (j s) -> p j s", j=PACK)
+        def round_g(m, s0, s1):
+            by_j = part(m, 0, 2).rearrange("p (j s) -> p j s", j=PACK)
             nc.scalar.copy(
-                g_bf[n][:, s0:s1, :].rearrange("p (s i) j -> p s j i", i=2),
+                rounded(m - 1)[:, PAIR + s0 : PAIR + s1, :].rearrange("p (s i) j -> p s j i", i=2),
                 by_j[:, :, s0:s1].rearrange("p j (s i) -> p s j i", i=2),
             )
 
-        def quantise_g(n, s0, s1):
+        def quantise(n, c0, c1):
+            if n not in codes:
+                codes[n] = odd_bytes(n, U32)
             nc.vector.quantize_mx(
-                out=g_codes(n)[:, s0:s1].bitcast(FP8X4),
-                scales=code_scales[n % 2][:, s0:s1],
-                in_=g_bf[n][:, s0:s1, :].rearrange("p s j -> p (s j)"),
+                out=codes[n][:, c0:c1].bitcast(FP8X4),
+                scales=code_scales[n % 2][:, c0:c1],
+                in_=rounded(n)[:, c0:c1, :].rearrange("p s j -> p (s j)"),
             )
 
-        def silu_factor(n, s0, s1):
+        def silu_factor(e):
+            n, v = divmod(e, 2)
+            if e > 0:
+                silu[e] = silu_ring.tile([P, WIDE], F32, name="silu")
             nc.scalar.activation(
-                part(n, 2, 4)[:, PACK * s0 : PACK * s1].rearrange("p (s i j) -> p s j i", i=2, j=PACK),
-                a_sb[n][:, :, s0:s1].rearrange("p j (s i) -> p s j i", i=2),
+                silu[e][:].rearrange("p (s i j) -> p s j i", i=2, j=PACK),
+                a_sb[n][:, :, v * C : (v + 1) * C].rearrange("p j (s i) -> p s j i", i=2),
                 ACT.Silu,
                 scale=-1.0,
             )
+
+        def silus_made(n):
+            return min(2 * n + 4 + max(n - 1, 0), E)
+
+        def tanh_of(n, v):
+            return part(n - 1, 0, 1) if v == 0 else odd_tanh[n][:]
 
         def bank(side, v):
             return banks.tile([P, WIDE], F32, name=f"bank{side}{v}")
@@ -196,14 +203,16 @@ def tile_moe_bdx_mlp_silu_kernel(
             a_turned = bank(min(n, LAST - 1) % 2, v)
             for j in range(PACK):
                 nc.tensor.transpose(a_turned[:, j * P : (j + 1) * P], a_sb[n][:, j, v * C : (v + 1) * C], ident[:])
-            nc.scalar.activation(tanh_of(n, v), a_turned[:], ACT.Tanh, scale=-0.5)
+            if v == 1:
+                odd_tanh[n] = odd_bytes(n, F32)
+            nc.scalar.activation(tanh_of(n, v), a_turned[:], ACT.Tanh, bias=(first_bias, zero)[v] if n == 0 else 0.0, scale=-0.5)
 
         def multiply_w2(dst, n, v):
-            cols = slice(v * C, (v + 1) * C)
+            cols = slice(PAIR + v * C, PAIR + (v + 1) * C)
             nc.tensor.matmul_mx(
                 out=dst[:],
-                lhsT=g_codes(n)[:, cols].bitcast(FP8X4),
-                lhsT_scale=code_scales[n % 2][:, cols],
+                lhsT=codes[n - 1][:, cols].bitcast(FP8X4),
+                lhsT_scale=code_scales[(n - 1) % 2][:, cols],
                 rhs=w2_sb[n][:, v, :].bitcast(FP4X4),
                 rhs_scale=plane_of(w2_plane, 2 * n + v),
                 start=True,
@@ -233,22 +242,13 @@ def tile_moe_bdx_mlp_silu_kernel(
                 nc.tensor.transpose(turned[n, v][:, j, :], half_da_t[:, j, :], ident[:])
 
         def apply_silu_factor(n, v):
-            if v == 0:
-                da_bf[n] = ring2.tile([P, PAIR, PACK], BF16, name="da_bf", align_bytes=64)
             nc.vector.scalar_tensor_tensor(
-                da_bf[n][:, v * C : (v + 1) * C, :],
-                part(n, 2 + v, 3 + v).rearrange("p (s j) -> p s j", j=PACK),
+                rounded(n + 1)[:, v * C : (v + 1) * C, :],
+                silu[2 * n + v][:].rearrange("p (s j) -> p s j", j=PACK),
                 1.0,
                 turned[n, v][:].rearrange("p j s -> p s j"),
                 ALU.subtract,
                 ALU.mult,
-            )
-
-        def quantise_da(n, v0, v1):
-            nc.vector.quantize_mx(
-                out=codes[(n + 1) % 2][:, v0 * C : v1 * C].bitcast(FP8X4),
-                scales=code_scales[n % 2][:, v0 * C : v1 * C],
-                in_=da_bf[n][:, v0 * C : v1 * C, :].rearrange("p s j -> p (s j)"),
             )
 
         def multiply_w1(dst, n, v, h):
@@ -257,8 +257,8 @@ def tile_moe_bdx_mlp_silu_kernel(
                 out=dst,
                 lhsT=w1_sb[n][:, v, 2 * P * h : 2 * P * (h + 1)].bitcast(FP4X4),
                 lhsT_scale=plane_of(w1_plane, 2 * n + v)[:, P * h : P * (h + 1)],
-                rhs=codes[(n + 1) % 2][:, cols].bitcast(FP8X4),
-                rhs_scale=code_scales[n % 2][:, cols],
+                rhs=codes[n + 1][:, cols].bitcast(FP8X4),
+                rhs_scale=code_scales[(n + 1) % 2][:, cols],
                 start=True,
                 stop=True,
             )
@@ -277,67 +277,60 @@ def tile_moe_bdx_mlp_silu_kernel(
                 multiply_w1(dx_ps, LAST, 1, h)
                 nc.scalar.activation(dx_sb[h][:, S - C : S], dx_ps, ACT.Copy, scale=0.5)
 
-        def pieces(n):
-            return ((0, C), (C, PAIR)) if n in (0, LAST) else ((0, PAIR),)
+        first_bias = part(0, 2, 3)[:, 0:1]
+        nc.scalar.activation(first_bias, zero, ACT.Silu)
 
-        silu_factor(0, 0, C)
-        for v in range(2):
-            tanh_factor(0, v)
         for j in range(PACK):
             gather(0, j)
-            if j < 2:
-                gather(1, j)
-        for s0, s1 in pieces(0):
-            round_g(0, s0, s1)
-        silu_factor(0, C, PAIR)
-        for j in (2, 3):
-            gather(1, j)
         for v in range(2):
-            quantise_g(0, v * C, (v + 1) * C)
+            round_g(0, v * C, (v + 1) * C)
+        for v in range(2):
+            tanh_factor(0, v)
+        for v in range(2):
+            quantise(-1, PAIR + v * C, PAIR + (v + 1) * C)
             first_product(0, v)
+        for j in range(PACK):
+            gather(1, j)
         round_g(1, 0, PAIR)
+        for j in (2, 3):
+            gather(2, j)
+        for e in range(silus_made(-1)):
+            silu_factor(e)
         refill(-1)
 
         for n in range(PAIRS):
-            ahead = n + GATHER_LEAD
             for v in range(2):
                 apply_tanh_factor(n, v)
-            if n == LAST:
-                second_product(n - 1, 0, 2)
-            else:
-                silu_factor(n + 1, 0, PAIR)
             if n + 1 < LAST:
                 for v in range(2):
                     tanh_factor(n + 1, v)
-            if ahead < PAIRS:
-                for j in (1, 2):
-                    gather(ahead, j)
-            for v in range(2):
-                apply_silu_factor(n, v)
+            if n + 2 < PAIRS:
+                for j in (0, 1):
+                    gather(n + 2, j)
+                round_g(n + 2, 0, PAIR)
+            quantise(n, 0 if n > 0 else PAIR, 2 * PAIR if n < LAST else PAIR)
             if n < LAST:
-                for s0, s1 in pieces(n + 1):
-                    quantise_g(n + 1, s0, s1)
                 for v in range(2):
                     first_product(n + 1, v)
-                if n + 1 in WARM_PAIRS:
-                    warm_up(n + 1)
-                quantise_da(n, 0, 2)
-                if n + 1 < LAST:
-                    second_product(n, 0, 2)
-            else:
-                quantise_da(n, 0, 1)
-                second_product(n, 0, 1)
-                quantise_da(n, 1, 2)
-                last_second_product()
-            if ahead < PAIRS:
-                for j in (3, 0):
-                    gather(ahead, j)
-                for s0, s1 in pieces(ahead):
-                    round_g(ahead, s0, s1)
-            if ahead == LAST:
+            if n > 0:
+                second_product(n - 1, 0, 2)
+            if n + 1 in WARM_PAIRS:
+                warm_up(n + 1)
+            for v in range(2):
+                apply_silu_factor(n, v)
+            if n + 3 < PAIRS:
+                for j in (2, 3):
+                    gather(n + 3, j)
+            if n + 2 == LAST:
                 for v in range(2):
                     tanh_factor(LAST, v)
+            for e in range(silus_made(n - 1), silus_made(n)):
+                silu_factor(e)
             refill(n)
+        quantise(PAIRS, 0, C)
+        second_product(LAST, 0, 1)
+        quantise(PAIRS, C, PAIR)
+        last_second_product()
 
         sums = [[keep.tile([P, T], F32, name=f"sum{h}_{x}") for x in range(2)] for h in range(K_TILES)]
         for r in range(TOP):

@@ -15,9 +15,12 @@ PAIRS = E // 2
 LAST = PAIRS - 1
 WIDE = PACK * C
 GATE_COLS = 2 * PAIR
-STREAM_BUFS = 3
-A_BUFS = 4
+STREAM_BUFS = 10
+A_BUFS = 10
 SILU_BUFS = 8
+WORK_TILES = 4
+HELPED = (1, 2, 4, 5, 7)
+SILUS_BY_STEP = (1, 1, 2, 2, 0, 2, 2, 0, 4, 1, 0)
 
 W2_GROUPS = ((0, 2), (2, 6), (6, E))
 W1_GROUPS = ((0, 6), (6, E))
@@ -47,7 +50,6 @@ def tile_moe_bdx_mlp_silu_kernel(
         ring2 = ctx.enter_context(tc.tile_pool(name="ring2", bufs=2))
         ring3 = ctx.enter_context(tc.tile_pool(name="ring3", bufs=STREAM_BUFS))
         a_ring = ctx.enter_context(tc.tile_pool(name="a_ring", bufs=A_BUFS))
-        silu_ring = ctx.enter_context(tc.tile_pool(name="silu_ring", bufs=SILU_BUFS))
         banks = ctx.enter_context(tc.psum_pool(name="banks", bufs=1))
         banks2 = ctx.enter_context(tc.psum_pool(name="banks2", bufs=2))
 
@@ -59,10 +61,15 @@ def tile_moe_bdx_mlp_silu_kernel(
         w1_plane = {g: keep.tile([P, g[1] - g[0], K], U8, name=f"w1_plane{g[0]}", align_bytes=64) for g in W1_GROUPS}
         dx_sb = [keep.tile([P, S], F32, name=f"dx_sb{h}") for h in range(K_TILES)]
         ident = keep.tile([P, P], F32, name="ident")
-        work = [keep.tile([P, 3 * WIDE], F32, name=f"work{x}", align_bytes=64) for x in range(3)]
+        work = [keep.tile([P, 6 * PAIR], F32, name=f"work{x}", align_bytes=64) for x in range(WORK_TILES)]
         code_scales = [keep.tile([P, 2 * PAIR], U8, name=f"code_scales{x}", align_bytes=64) for x in range(2)]
 
-        silu = {0: silu_ring.tile([P, WIDE], F32, name="silu")}
+        silu_order = [e for e in range(E) if not (e % 2 == 1 and e // 2 in HELPED)]
+
+        def silu_slot(e, dtype):
+            return keep.tile([P, WIDE], dtype, name=f"silu{silu_order.index(e) % SILU_BUFS}", align_bytes=64)
+
+        silu = {0: silu_slot(0, F32)}
         zero = silu[0][:, 0:1]
         nc.vector.memset(zero, 0.0)
         for g in W2_GROUPS:
@@ -78,7 +85,7 @@ def tile_moe_bdx_mlp_silu_kernel(
             nc.sync.dma_start(dy_sb[j][:], dy_rows[:, j, :])
 
         def load_gate(c):
-            gate_sb[c] = ring3.tile([P, GATE_COLS], F32, name="gate_sb")
+            gate_sb[c] = keep.tile([P, GATE_COLS], F32, name=f"gate_sb{c}")
             s0, s1 = max((2 * c - 1) * PAIR, 0), min((2 * c + 1) * PAIR, S)
             first = s0 - (2 * c - 1) * PAIR
             nc.sync.dma_start(gate_sb[c][:, first : first + s1 - s0], gate[0:P, s0:s1])
@@ -87,16 +94,16 @@ def tile_moe_bdx_mlp_silu_kernel(
             a_sb[n] = a_ring.tile([P, PACK, PAIR], F32, name="a_sb")
             nc.sync.dma_start(a_sb[n][:], a_rows[:, :, n * PAIR : (n + 1) * PAIR])
 
-        def load_words(tiles, words, n, name):
-            tiles[n] = ring3.tile([P, 2, words.shape[-1]], U8, name=name, align_bytes=64)
+        def load_words(pool, tiles, words, n, name):
+            tiles[n] = pool.tile([P, 2, words.shape[-1]], U8, name=name, align_bytes=64)
             src = words[2 * n : 2 * n + 2, 0].rearrange("e p b -> p e b")
             nc.sync.dma_start(tiles[n][:].bitcast(I32), src.bitcast(I32))
 
         def load_w2(n):
-            load_words(w2_sb, w2_words, n, "w2_sb")
+            load_words(ring3, w2_sb, w2_words, n, "w2_sb")
 
         def load_w1(n):
-            load_words(w1_sb, w1_words, n, "w1_sb")
+            load_words(a_ring, w1_sb, w1_words, n, "w1_sb")
 
         def load_plane(planes, scale_rows, g):
             for r in range(4):
@@ -115,74 +122,91 @@ def tile_moe_bdx_mlp_silu_kernel(
         load_w2(0)
         load_plane(w2_plane, w2_scales, W2_GROUPS[0])
         load_a(1)
-        load_w2(1)
-        load_gate(2)
-        load_w1(0)
         load_plane(w2_plane, w2_scales, W2_GROUPS[1])
+        load_w2(1)
         load_a(2)
-        load_plane(w1_plane, w1_scales, W1_GROUPS[0])
-        load_w2(2)
-        load_w1(1)
-        load_w1(2)
+        load_gate(2)
         load_a(3)
+        load_w2(2)
+        load_w1(0)
+        load_plane(w1_plane, w1_scales, W1_GROUPS[0])
+        load_gate(3)
+        load_a(4)
+        load_w2(3)
         load_plane(w2_plane, w2_scales, W2_GROUPS[2])
-        load_plane(w1_plane, w1_scales, W1_GROUPS[1])
+        for n in range(3, LAST + 3):
+            load_w1(n - 2)
+            if n - 2 == W1_GROUPS[1][0] // 2:
+                load_plane(w1_plane, w1_scales, W1_GROUPS[1])
+            if n + 2 < PAIRS:
+                load_a(n + 2)
+            if n in (3, 5):
+                load_gate((n + 5) // 2)
+            if n + 1 < PAIRS:
+                load_w2(n + 1)
         for r, pos in enumerate((pos1, pos2, pos3, pos4)):
             nc.sync.dma_start(pos_sb[r][:], pos)
 
-        def refill(n):
-            if n % 2 == 0 or n < 0:
-                c = (n + 2) // 2 + STREAM_BUFS
-                if (2 * c - 1) < PAIRS:
-                    load_gate(c)
-            if n + 1 + A_BUFS < PAIRS:
-                load_a(n + 1 + A_BUFS)
-            if n + 1 + STREAM_BUFS < PAIRS:
-                load_w2(n + 1 + STREAM_BUFS)
-            if 1 <= n <= PAIRS - STREAM_BUFS:
-                load_w1(n - 1 + STREAM_BUFS)
+        def silus_made(n):
+            return sum(SILUS_BY_STEP[: n + 2])
 
-        dh_ps, turned, odd_tanh, codes = {}, {}, {}, {}
+        first_odd = keep.tile([P, WIDE], F32, name="first_odd", align_bytes=64)
+        dh_ps, turned, codes, half, tanh_less_one = {}, {}, {}, {}, {}
 
-        def part(m, x0, x1):
-            return work[m % 3][:, x0 * WIDE : x1 * WIDE]
+        def units(n, u0, u1):
+            return work[n % WORK_TILES][:, u0 * PAIR : u1 * PAIR]
 
-        def rounded(n):
-            return part(n, 1, 3).bitcast(BF16).rearrange("p (s j) -> p s j", j=PACK)
+        def unit_pair(n, u0, u1):
+            return work[n % WORK_TILES][:].rearrange("p (u x) -> p u x", x=PAIR)[:, u0 : u1 + 1 : u1 - u0, :]
 
-        def odd_bytes(n, dtype):
-            return keep.tile([P, WIDE], dtype, name=f"odd{n % 2}", align_bytes=64)
+        def da_units(m):
+            return (2, 5) if m + 2 < LAST else (2, 3)
+
+        def rounded(n, u0, u1):
+            return units(n, u0, u1).bitcast(BF16).rearrange("p (s j) -> p s j", j=PACK)
+
+        def first_factor(n, v):
+            if (n, v) == (0, 1):
+                return first_odd[:].rearrange("p (u x) -> p u x", u=2)
+            if v == 1 or n == 0:
+                return unit_pair(n, 0, 1)
+            return unit_pair(n + 1, *(da_units(n - 1) if n < LAST else (4, 5)))
+
+        def gate_of(m):
+            c, side = divmod(m + 1, 2)
+            return gate_sb[c][:, side * PAIR : (side + 1) * PAIR]
 
         def gather(m, j):
-            c, half = divmod(m + 1, 2)
+            u = (0, 1, 3, 4)[j]
             entries = offs_sb[:, m * PAIR // LIST_COL : (m + 1) * PAIR // LIST_COL]
-            nc.vector.tensor_tensor(
-                part(m, 0, 2)[:, j * PAIR : (j + 1) * PAIR],
-                dy_sb[j][:].indirect(entries),
-                gate_sb[c][:, half * PAIR : (half + 1) * PAIR],
-                ALU.mult,
-            )
+            nc.vector.tensor_tensor(units(m - 2, u, u + 1), dy_sb[j][:].indirect(entries), gate_of(m), ALU.mult)
 
-        def round_g(m, s0, s1):
-            by_j = part(m, 0, 2).rearrange("p (j s) -> p j s", j=PACK)
+        def round_g(m):
+            by_j = units(m - 2, 0, 6).rearrange("p (u x) -> p u x", u=2)[:, :, 0 : 2 * PAIR]
             nc.scalar.copy(
-                rounded(m - 1)[:, PAIR + s0 : PAIR + s1, :].rearrange("p (s i) j -> p s j i", i=2),
-                by_j[:, :, s0:s1].rearrange("p j (s i) -> p s j i", i=2),
+                rounded(m - 1, 3, 5).rearrange("p (s i) (u j) -> p s u j i", i=2, u=2),
+                by_j.rearrange("p u (j s i) -> p s u j i", j=2, i=2),
             )
 
-        def quantise(n, c0, c1):
+        def quantise(n, u0, u1):
             if n not in codes:
-                codes[n] = odd_bytes(n, U32)
+                if n == 0:
+                    codes[n] = keep.tile([P, WIDE], U32, name="first_odd", align_bytes=64)
+                elif 0 < n < LAST:
+                    codes[n] = silu_slot(2 * (n - 1), U32)
+                else:
+                    codes[n] = ring2.tile([P, WIDE], U32, name="codes", align_bytes=64)
+            cols = slice((u0 - 2) * C, (u1 - 2) * C)
             nc.vector.quantize_mx(
-                out=codes[n][:, c0:c1].bitcast(FP8X4),
-                scales=code_scales[n % 2][:, c0:c1],
-                in_=rounded(n)[:, c0:c1, :].rearrange("p s j -> p (s j)"),
+                out=codes[n][:, cols].bitcast(FP8X4),
+                scales=code_scales[n % 2][:, cols],
+                in_=units(n, u0, u1).bitcast(BF16),
             )
 
         def silu_factor(e):
             n, v = divmod(e, 2)
             if e > 0:
-                silu[e] = silu_ring.tile([P, WIDE], F32, name="silu")
+                silu[e] = silu_slot(e, F32)
             nc.scalar.activation(
                 silu[e][:].rearrange("p (s i j) -> p s j i", i=2, j=PACK),
                 a_sb[n][:, :, v * C : (v + 1) * C].rearrange("p j (s i) -> p s j i", i=2),
@@ -190,25 +214,51 @@ def tile_moe_bdx_mlp_silu_kernel(
                 scale=-1.0,
             )
 
-        def silus_made(n):
-            return min(2 * n + 4 + max(n - 1, 0), E)
-
-        def tanh_of(n, v):
-            return part(n - 1, 0, 1) if v == 0 else odd_tanh[n][:]
-
         def bank(side, v):
             return banks.tile([P, WIDE], F32, name=f"bank{side}{v}")
 
-        def tanh_factor(n, v):
-            a_turned = bank(min(n, LAST - 1) % 2, v)
+        a_turned = {}
+
+        def turn_a(n, v):
+            if helped(n - 1, v) and helped(n - 2, v):
+                a_turned[n, v] = banks.tile([P, WIDE], F32, name="turned1")
+            else:
+                a_turned[n, v] = bank(n % 2, v)
             for j in range(PACK):
-                nc.tensor.transpose(a_turned[:, j * P : (j + 1) * P], a_sb[n][:, j, v * C : (v + 1) * C], ident[:])
-            if v == 1:
-                odd_tanh[n] = odd_bytes(n, F32)
-            nc.scalar.activation(tanh_of(n, v), a_turned[:], ACT.Tanh, bias=(first_bias, zero)[v] if n == 0 else 0.0, scale=-0.5)
+                nc.tensor.transpose(a_turned[n, v][:, j * P : (j + 1) * P], a_sb[n][:, j, v * C : (v + 1) * C], ident[:])
+
+        def helped(n, v):
+            return v == 1 and n in HELPED
+
+        def make_first_factor(n, v):
+            if helped(n, v):
+                nc.scalar.activation(
+                    first_factor(n, v).rearrange("s u (q j) -> s u q j", j=PACK),
+                    a_turned[n, v][:].rearrange("s (j u q) -> s u q j", j=PACK, u=2),
+                    ACT.Silu,
+                    scale=-1.0,
+                )
+            else:
+                nc.scalar.activation(
+                    first_factor(n, v),
+                    a_turned[n, v][:].rearrange("s (u x) -> s u x", u=2),
+                    ACT.Tanh,
+                    bias=(first_bias, zero)[v] if n == 0 else 0.0,
+                    scale=-0.5,
+                )
+
+        tanh_odd = {}
+
+        def make_tanh(n):
+            tanh_odd[n] = ring2.tile([P, P, PACK], F32, name="tanh_odd")
+            nc.scalar.activation(tanh_odd[n][:], a_turned[n, 1][:].rearrange("s (j p) -> s p j", j=PACK), ACT.Tanh, scale=-0.5)
+
+        def subtract_one(n):
+            tanh_less_one[n] = ring2.tile([P, WIDE], F32, name="tanh_less_one")
+            nc.scalar.activation(tanh_less_one[n][:], tanh_odd[n][:].rearrange("s p j -> s (p j)"), ACT.Copy, bias=-1.0)
 
         def multiply_w2(dst, n, v):
-            cols = slice(PAIR + v * C, PAIR + (v + 1) * C)
+            cols = slice((1 + v) * C, (2 + v) * C)
             nc.tensor.matmul_mx(
                 out=dst[:],
                 lhsT=codes[n - 1][:, cols].bitcast(FP8X4),
@@ -227,23 +277,27 @@ def tile_moe_bdx_mlp_silu_kernel(
             unread = banks2.tile([P, H], F32, name="dx")
             multiply_w2(unread, n, 1)
 
-        def apply_tanh_factor(n, v):
-            half_da_t = ring2.tile([P, PACK, P], F32, name="half_da_t")
-            nc.vector.scalar_tensor_tensor(
-                half_da_t[:],
-                tanh_of(n, v).rearrange("s (j p) -> s j p", j=PACK),
-                1.0,
-                dh_ps[n, v][:].rearrange("s (p j) -> s j p", j=PACK),
-                ALU.subtract,
-                ALU.mult,
-            )
+        def apply_first_factor(n, v):
+            half[n, v] = ring2.tile([P, WIDE], F32, name=f"half{v}")
+            if helped(n, v):
+                dh = dh_ps[n, v][:].rearrange("s (u x) -> s u x", u=2)
+                dst = half[n, v][:].rearrange("s (u x) -> s u x", u=2)
+                factor = first_factor(n, v)
+            else:
+                dh = dh_ps[n, v][:].rearrange("s (p u j) -> s u j p", u=2, j=2)
+                dst = half[n, v][:].rearrange("s (u j p) -> s u j p", u=2, j=2)
+                factor = first_factor(n, v).rearrange("s u (j p) -> s u j p", j=2)
+            nc.vector.scalar_tensor_tensor(dst, factor, 1.0, dh, ALU.subtract, ALU.mult)
+
+        def turn_half(n, v):
             turned[n, v] = banks.tile([P, PACK, C], F32, name=f"turned{v}")
             for j in range(PACK):
-                nc.tensor.transpose(turned[n, v][:, j, :], half_da_t[:, j, :], ident[:])
+                nc.tensor.transpose(turned[n, v][:, j, :], half[n, v][:, j * P : (j + 1) * P], ident[:])
 
         def apply_silu_factor(n, v):
+            u = da_units(n)[v]
             nc.vector.scalar_tensor_tensor(
-                rounded(n + 1)[:, v * C : (v + 1) * C, :],
+                rounded(n + 2, u, u + 1),
                 silu[2 * n + v][:].rearrange("p (s j) -> p s j", j=PACK),
                 1.0,
                 turned[n, v][:].rearrange("p j s -> p s j"),
@@ -251,85 +305,135 @@ def tile_moe_bdx_mlp_silu_kernel(
                 ALU.mult,
             )
 
+        def help_multiply(n):
+            words = gate_of(n + 2)
+            nc.gpsimd.tensor_tensor(words.bitcast(BF16), half[n, 1][:], tanh_less_one[n][:], ALU.mult)
+
+        def help_turn(n):
+            words = gate_of(n + 2)
+            turned[n, 1] = bank(n % 2, 1)[:, 0:PAIR].rearrange("p (u s) -> p u s", u=2)
+            for u in range(2):
+                nc.tensor.transpose(turned[n, 1][:, u, :], words[:, u:PAIR:2], ident[:])
+
+        def help_copy(n):
+            u = da_units(n)[1]
+            nc.scalar.copy(units(n + 2, u, u + 1).rearrange("p (s u) -> p s u", u=2), turned[n, 1].rearrange("p u s -> p s u"))
+
         def multiply_w1(dst, n, v, h):
-            cols = slice(v * C, (v + 1) * C)
+            u = da_units(n)[v]
+            cols = slice((u - 2) * C, (u - 1) * C)
             nc.tensor.matmul_mx(
                 out=dst,
                 lhsT=w1_sb[n][:, v, 2 * P * h : 2 * P * (h + 1)].bitcast(FP4X4),
                 lhsT_scale=plane_of(w1_plane, 2 * n + v)[:, P * h : P * (h + 1)],
-                rhs=codes[n + 1][:, cols].bitcast(FP8X4),
-                rhs_scale=code_scales[(n + 1) % 2][:, cols],
+                rhs=codes[n + 2][:, cols].bitcast(FP8X4),
+                rhs_scale=code_scales[n % 2][:, cols],
                 start=True,
                 stop=True,
             )
 
+        dx_ps = {}
+
         def second_product(n, v0, v1):
-            dx_ps = banks2.tile([P, K_TILES, (v1 - v0) * C], F32, name="dx")
+            dx_ps[n] = banks2.tile([P, K_TILES, (v1 - v0) * C], F32, name="dx")
             for h in range(K_TILES):
                 for v in range(v0, v1):
-                    multiply_w1(dx_ps[:, h, (v - v0) * C : (v - v0 + 1) * C], n, v, h)
+                    multiply_w1(dx_ps[n][:, h, (v - v0) * C : (v - v0 + 1) * C], n, v, h)
+
+        def empty_dx(n, v0, v1):
             for h in range(K_TILES):
-                nc.scalar.activation(dx_sb[h][:, n * PAIR + v0 * C : n * PAIR + v1 * C], dx_ps[:, h, :], ACT.Copy, scale=0.5)
+                nc.scalar.activation(dx_sb[h][:, n * PAIR + v0 * C : n * PAIR + v1 * C], dx_ps[n][:, h, :], ACT.Copy, scale=0.5)
 
         def last_second_product():
             for h in range(K_TILES):
-                dx_ps = bank(LAST % 2, h)[:, 0:C]
-                multiply_w1(dx_ps, LAST, 1, h)
-                nc.scalar.activation(dx_sb[h][:, S - C : S], dx_ps, ACT.Copy, scale=0.5)
+                last = bank(1, h)[:, 0:C]
+                multiply_w1(last, LAST, 1, h)
+                nc.scalar.activation(dx_sb[h][:, S - C : S], last, ACT.Copy, scale=0.5)
 
-        first_bias = part(0, 2, 3)[:, 0:1]
+        def silus(n):
+            for e in silu_order[silus_made(n - 1) if n >= 0 else 0 : silus_made(n)]:
+                silu_factor(e)
+
+        first_bias = units(0, 3, 4)[:, 0:1]
         nc.scalar.activation(first_bias, zero, ACT.Silu)
 
         for j in range(PACK):
             gather(0, j)
+        round_g(0)
         for v in range(2):
-            round_g(0, v * C, (v + 1) * C)
-        for v in range(2):
-            tanh_factor(0, v)
-        for v in range(2):
-            quantise(-1, PAIR + v * C, PAIR + (v + 1) * C)
-            first_product(0, v)
-        for j in range(PACK):
+            turn_a(0, v)
+            make_first_factor(0, v)
+        for j in (0, 1):
             gather(1, j)
-        round_g(1, 0, PAIR)
+        for v in range(2):
+            quantise(-1, 3 + v, 4 + v)
+            first_product(0, v)
         for j in (2, 3):
-            gather(2, j)
-        for e in range(silus_made(-1)):
-            silu_factor(e)
-        refill(-1)
+            gather(1, j)
+        silus(-1)
 
-        for n in range(PAIRS):
+        for n in range(LAST):
+            round_g(n + 1)
+            if n - 1 in HELPED:
+                help_multiply(n - 1)
             for v in range(2):
-                apply_tanh_factor(n, v)
-            if n + 1 < LAST:
-                for v in range(2):
-                    tanh_factor(n + 1, v)
+                apply_first_factor(n, v)
+            for v in range(2):
+                if n > 0 and not helped(n - 1, v):
+                    apply_silu_factor(n - 1, v)
+            words_first = n - 1 in HELPED and n not in HELPED
+            for v in range(2):
+                if v == 1 and words_first:
+                    help_turn(n - 1)
+                    help_copy(n - 1)
+                turn_a(n + 1, v)
+                make_first_factor(n + 1, v)
+            if n - 1 in HELPED and not words_first:
+                help_turn(n - 1)
+                help_copy(n - 1)
+            for v in range(2):
+                if not helped(n, v):
+                    turn_half(n, v)
             if n + 2 < PAIRS:
                 for j in (0, 1):
                     gather(n + 2, j)
-                round_g(n + 2, 0, PAIR)
-            quantise(n, 0 if n > 0 else PAIR, 2 * PAIR if n < LAST else PAIR)
-            if n < LAST:
-                for v in range(2):
-                    first_product(n + 1, v)
-            if n > 0:
-                second_product(n - 1, 0, 2)
+            for v in range(2):
+                if n >= 2:
+                    quantise(n, 2 + 2 * v, 4 + 2 * v)
+                else:
+                    quantise(n, 3 + v, 4 + v)
+            for v in range(2):
+                first_product(n + 1, v)
+            if n >= 2:
+                second_product(n - 2, 0, 2)
             if n + 1 in WARM_PAIRS:
                 warm_up(n + 1)
-            for v in range(2):
-                apply_silu_factor(n, v)
-            if n + 3 < PAIRS:
+            if n + 2 < PAIRS:
                 for j in (2, 3):
-                    gather(n + 3, j)
-            if n + 2 == LAST:
-                for v in range(2):
-                    tanh_factor(LAST, v)
-            for e in range(silus_made(n - 1), silus_made(n)):
-                silu_factor(e)
-            refill(n)
-        quantise(PAIRS, 0, C)
+                    gather(n + 2, j)
+            if n + 1 in HELPED:
+                make_tanh(n + 1)
+            silus(n)
+            if n + 1 in HELPED:
+                subtract_one(n + 1)
+            if n >= 2:
+                empty_dx(n - 2, 0, 2)
+
+        for v in range(2):
+            apply_silu_factor(LAST - 1, v)
+        for v in range(2):
+            apply_first_factor(LAST, v)
+            turn_half(LAST, v)
+        for m in (LAST - 2, LAST - 1):
+            quantise(m + 2, 2, 4)
+            second_product(m, 0, 2)
+            empty_dx(m, 0, 2)
+        for v in range(2):
+            apply_silu_factor(LAST, v)
+        quantise(LAST + 2, 2, 3)
         second_product(LAST, 0, 1)
-        quantise(PAIRS, C, PAIR)
+        empty_dx(LAST, 0, 1)
+        quantise(LAST + 2, 3, 4)
         last_second_product()
 
         sums = [[keep.tile([P, T], F32, name=f"sum{h}_{x}") for x in range(2)] for h in range(K_TILES)]

@@ -17,10 +17,10 @@ WIDE = PACK * C
 GATE_COLS = 2 * PAIR
 STREAM_BUFS = 10
 A_BUFS = 10
-SILU_BUFS = 8
+SILU_BUFS = 5
 WORK_TILES = 4
-HELPED = (1, 2, 4, 5, 7)
-SILUS_BY_STEP = (1, 1, 2, 2, 0, 2, 2, 0, 4, 1, 0)
+HELPED = (1, 4, 7)
+SILUS_BY_STEP = (1, 1, 3, 2, 0, 3, 2, 0, 3, 2, 0)
 
 W2_GROUPS = ((0, 2), (2, 6), (6, E))
 W1_GROUPS = ((0, 6), (6, E))
@@ -135,13 +135,13 @@ def tile_moe_bdx_mlp_silu_kernel(
         load_w2(3)
         load_plane(w2_plane, w2_scales, W2_GROUPS[2])
         for n in range(3, LAST + 3):
-            load_w1(n - 2)
-            if n - 2 == W1_GROUPS[1][0] // 2:
-                load_plane(w1_plane, w1_scales, W1_GROUPS[1])
             if n + 2 < PAIRS:
                 load_a(n + 2)
             if n in (3, 5):
                 load_gate((n + 5) // 2)
+            load_w1(n - 2)
+            if n - 2 == W1_GROUPS[1][0] // 2:
+                load_plane(w1_plane, w1_scales, W1_GROUPS[1])
             if n + 1 < PAIRS:
                 load_w2(n + 1)
         for r, pos in enumerate((pos1, pos2, pos3, pos4)):
@@ -220,10 +220,7 @@ def tile_moe_bdx_mlp_silu_kernel(
         a_turned = {}
 
         def turn_a(n, v):
-            if helped(n - 1, v) and helped(n - 2, v):
-                a_turned[n, v] = banks.tile([P, WIDE], F32, name="turned1")
-            else:
-                a_turned[n, v] = bank(n % 2, v)
+            a_turned[n, v] = bank(n % 2, v)
             for j in range(PACK):
                 nc.tensor.transpose(a_turned[n, v][:, j * P : (j + 1) * P], a_sb[n][:, j, v * C : (v + 1) * C], ident[:])
 
@@ -289,8 +286,11 @@ def tile_moe_bdx_mlp_silu_kernel(
                 factor = first_factor(n, v).rearrange("s u (j p) -> s u j p", j=2)
             nc.vector.scalar_tensor_tensor(dst, factor, 1.0, dh, ALU.subtract, ALU.mult)
 
+        def turn_bank(n, v):
+            return f"turned{(v + sum(m < n for m in HELPED)) % 2}"
+
         def turn_half(n, v):
-            turned[n, v] = banks.tile([P, PACK, C], F32, name=f"turned{v}")
+            turned[n, v] = banks.tile([P, PACK, C], F32, name=turn_bank(n, v))
             for j in range(PACK):
                 nc.tensor.transpose(turned[n, v][:, j, :], half[n, v][:, j * P : (j + 1) * P], ident[:])
 
@@ -311,13 +311,13 @@ def tile_moe_bdx_mlp_silu_kernel(
 
         def help_turn(n):
             words = gate_of(n + 2)
-            turned[n, 1] = bank(n % 2, 1)[:, 0:PAIR].rearrange("p (u s) -> p u s", u=2)
+            turned[n, 1] = banks.tile([P, 2, C], F32, name=turn_bank(n, 0))
             for u in range(2):
                 nc.tensor.transpose(turned[n, 1][:, u, :], words[:, u:PAIR:2], ident[:])
 
         def help_copy(n):
             u = da_units(n)[1]
-            nc.scalar.copy(units(n + 2, u, u + 1).rearrange("p (s u) -> p s u", u=2), turned[n, 1].rearrange("p u s -> p s u"))
+            nc.scalar.copy(units(n + 2, u, u + 1).rearrange("p (s u) -> p s u", u=2), turned[n, 1][:].rearrange("p u s -> p s u"))
 
         def multiply_w1(dst, n, v, h):
             u = da_units(n)[v]
@@ -381,14 +381,10 @@ def tile_moe_bdx_mlp_silu_kernel(
             for v in range(2):
                 if n > 0 and not helped(n - 1, v):
                     apply_silu_factor(n - 1, v)
-            words_first = n - 1 in HELPED and n not in HELPED
             for v in range(2):
-                if v == 1 and words_first:
-                    help_turn(n - 1)
-                    help_copy(n - 1)
                 turn_a(n + 1, v)
                 make_first_factor(n + 1, v)
-            if n - 1 in HELPED and not words_first:
+            if n - 1 in HELPED:
                 help_turn(n - 1)
                 help_copy(n - 1)
             for v in range(2):

@@ -17,12 +17,12 @@ WIDE = PACK * C
 GATE_COLS = 2 * PAIR
 STREAM_BUFS = 10
 A_BUFS = 10
-SILU_BUFS = 5
+SILU_BUFS = 6
 WORK_TILES = 4
-HELPED = (1, 4, 7)
-SILUS_BY_STEP = (1, 1, 3, 2, 0, 3, 2, 0, 3, 2, 0)
+HELPED = (1, 3, 5, 7)
+SILUS_BY_STEP = (1, 1, 3, 0, 3, 0, 3, 0, 3, 2, 0)
 
-W2_GROUPS = ((0, 2), (2, 6), (6, E))
+W2_GROUPS = ((0, 2), (2, 6), (6, 12), (12, E))
 W1_GROUPS = ((0, 6), (6, E))
 WARM_PAIRS = range(2, 9)
 
@@ -61,10 +61,10 @@ def tile_moe_bdx_mlp_silu_kernel(
         w1_plane = {g: keep.tile([P, g[1] - g[0], K], U8, name=f"w1_plane{g[0]}", align_bytes=64) for g in W1_GROUPS}
         dx_sb = [keep.tile([P, S], F32, name=f"dx_sb{h}") for h in range(K_TILES)]
         ident = keep.tile([P, P], F32, name="ident")
-        work = [keep.tile([P, 6 * PAIR], F32, name=f"work{x}", align_bytes=64) for x in range(WORK_TILES)]
+        work = [keep.tile([P, 7 * PAIR], F32, name=f"work{x}", align_bytes=64) for x in range(WORK_TILES)]
         code_scales = [keep.tile([P, 2 * PAIR], U8, name=f"code_scales{x}", align_bytes=64) for x in range(2)]
 
-        silu_order = [e for e in range(E) if not (e % 2 == 1 and e // 2 in HELPED)]
+        silu_order = [e for e in range(E) if not (e % 2 == 0 and e // 2 in HELPED)]
 
         def silu_slot(e, dtype):
             return keep.tile([P, WIDE], dtype, name=f"silu{silu_order.index(e) % SILU_BUFS}", align_bytes=64)
@@ -122,28 +122,29 @@ def tile_moe_bdx_mlp_silu_kernel(
         load_w2(0)
         load_plane(w2_plane, w2_scales, W2_GROUPS[0])
         load_a(1)
+        load_gate(2)
         load_plane(w2_plane, w2_scales, W2_GROUPS[1])
         load_w2(1)
         load_a(2)
-        load_gate(2)
-        load_a(3)
-        load_w2(2)
-        load_w1(0)
-        load_plane(w1_plane, w1_scales, W1_GROUPS[0])
         load_gate(3)
-        load_a(4)
-        load_w2(3)
-        load_plane(w2_plane, w2_scales, W2_GROUPS[2])
-        for n in range(3, LAST + 3):
-            if n + 2 < PAIRS:
+        load_w2(2)
+        load_a(3)
+        for n in range(2, LAST + 3):
+            if n == 5:
                 load_a(n + 2)
-            if n in (3, 5):
-                load_gate((n + 5) // 2)
             load_w1(n - 2)
-            if n - 2 == W1_GROUPS[1][0] // 2:
-                load_plane(w1_plane, w1_scales, W1_GROUPS[1])
+            for g in W1_GROUPS:
+                if g[0] == 2 * (n - 2):
+                    load_plane(w1_plane, w1_scales, g)
+            if n + 2 < PAIRS and n != 5:
+                load_a(n + 2)
             if n + 1 < PAIRS:
                 load_w2(n + 1)
+            for g in W2_GROUPS:
+                if g[0] == 2 * (n + 1):
+                    load_plane(w2_plane, w2_scales, g)
+            if n in (2, 4):
+                load_gate((n + 6) // 2)
         for r, pos in enumerate((pos1, pos2, pos3, pos4)):
             nc.sync.dma_start(pos_sb[r][:], pos)
 
@@ -169,7 +170,9 @@ def tile_moe_bdx_mlp_silu_kernel(
             if (n, v) == (0, 1):
                 return first_odd[:].rearrange("p (u x) -> p u x", u=2)
             if v == 1 or n == 0:
-                return unit_pair(n, 0, 1)
+                return unit_pair(n - 1, 0, 1)
+            if n - 1 in HELPED:
+                return unit_pair(n + 1, da_units(n - 1)[1], da_units(n - 1)[1] + 1)
             return unit_pair(n + 1, *(da_units(n - 1) if n < LAST else (4, 5)))
 
         def gate_of(m):
@@ -179,10 +182,10 @@ def tile_moe_bdx_mlp_silu_kernel(
         def gather(m, j):
             u = (0, 1, 3, 4)[j]
             entries = offs_sb[:, m * PAIR // LIST_COL : (m + 1) * PAIR // LIST_COL]
-            nc.vector.tensor_tensor(units(m - 2, u, u + 1), dy_sb[j][:].indirect(entries), gate_of(m), ALU.mult)
+            nc.vector.tensor_tensor(units(m - 3, u, u + 1), dy_sb[j][:].indirect(entries), gate_of(m), ALU.mult)
 
         def round_g(m):
-            by_j = units(m - 2, 0, 6).rearrange("p (u x) -> p u x", u=2)[:, :, 0 : 2 * PAIR]
+            by_j = units(m - 3, 0, 6).rearrange("p (u x) -> p u x", u=2)[:, :, 0 : 2 * PAIR]
             nc.scalar.copy(
                 rounded(m - 1, 3, 5).rearrange("p (s i) (u j) -> p s u j i", i=2, u=2),
                 by_j.rearrange("p u (j s i) -> p s u j i", j=2, i=2),
@@ -192,8 +195,8 @@ def tile_moe_bdx_mlp_silu_kernel(
             if n not in codes:
                 if n == 0:
                     codes[n] = keep.tile([P, WIDE], U32, name="first_odd", align_bytes=64)
-                elif 0 < n < LAST:
-                    codes[n] = silu_slot(2 * (n - 1), U32)
+                elif 0 < n < LAST - 1:
+                    codes[n] = silu_slot(2 * (n - 1) + (n - 1 in HELPED), U32)
                 else:
                     codes[n] = ring2.tile([P, WIDE], U32, name="codes", align_bytes=64)
             cols = slice((u0 - 2) * C, (u1 - 2) * C)
@@ -225,7 +228,7 @@ def tile_moe_bdx_mlp_silu_kernel(
                 nc.tensor.transpose(a_turned[n, v][:, j * P : (j + 1) * P], a_sb[n][:, j, v * C : (v + 1) * C], ident[:])
 
         def helped(n, v):
-            return v == 1 and n in HELPED
+            return v == 0 and n in HELPED
 
         def make_first_factor(n, v):
             if helped(n, v):
@@ -248,7 +251,7 @@ def tile_moe_bdx_mlp_silu_kernel(
 
         def make_tanh(n):
             tanh_odd[n] = ring2.tile([P, P, PACK], F32, name="tanh_odd")
-            nc.scalar.activation(tanh_odd[n][:], a_turned[n, 1][:].rearrange("s (j p) -> s p j", j=PACK), ACT.Tanh, scale=-0.5)
+            nc.scalar.activation(tanh_odd[n][:], a_turned[n, 0][:].rearrange("s (j p) -> s p j", j=PACK), ACT.Tanh, scale=-0.5)
 
         def subtract_one(n):
             tanh_less_one[n] = ring2.tile([P, WIDE], F32, name="tanh_less_one")
@@ -287,7 +290,7 @@ def tile_moe_bdx_mlp_silu_kernel(
             nc.vector.scalar_tensor_tensor(dst, factor, 1.0, dh, ALU.subtract, ALU.mult)
 
         def turn_bank(n, v):
-            return f"turned{(v + sum(m < n for m in HELPED)) % 2}"
+            return f"turned{(v + sum(m <= n for m in HELPED)) % 2}"
 
         def turn_half(n, v):
             turned[n, v] = banks.tile([P, PACK, C], F32, name=turn_bank(n, v))
@@ -305,19 +308,20 @@ def tile_moe_bdx_mlp_silu_kernel(
                 ALU.mult,
             )
 
+        words = {}
+
         def help_multiply(n):
-            words = gate_of(n + 2)
-            nc.gpsimd.tensor_tensor(words.bitcast(BF16), half[n, 1][:], tanh_less_one[n][:], ALU.mult)
+            words[n] = ring2.tile([P, PAIR], F32, name="words")
+            nc.gpsimd.tensor_tensor(words[n][:].bitcast(BF16), half[n, 0][:], tanh_less_one[n][:], ALU.mult)
 
         def help_turn(n):
-            words = gate_of(n + 2)
-            turned[n, 1] = banks.tile([P, 2, C], F32, name=turn_bank(n, 0))
+            turned[n, 0] = banks.tile([P, 2, C], F32, name=turn_bank(n, 0))
             for u in range(2):
-                nc.tensor.transpose(turned[n, 1][:, u, :], words[:, u:PAIR:2], ident[:])
+                nc.tensor.transpose(turned[n, 0][:, u, :], words[n][:, u:PAIR:2], ident[:])
 
         def help_copy(n):
-            u = da_units(n)[1]
-            nc.scalar.copy(units(n + 2, u, u + 1).rearrange("p (s u) -> p s u", u=2), turned[n, 1][:].rearrange("p u s -> p s u"))
+            u = da_units(n)[0]
+            nc.scalar.copy(units(n + 2, u, u + 1).rearrange("p (s u) -> p s u", u=2), turned[n, 0][:].rearrange("p u s -> p s u"))
 
         def multiply_w1(dst, n, v, h):
             u = da_units(n)[v]
@@ -363,36 +367,40 @@ def tile_moe_bdx_mlp_silu_kernel(
         for v in range(2):
             turn_a(0, v)
             make_first_factor(0, v)
-        for j in (0, 1):
+        for j in range(PACK):
             gather(1, j)
         for v in range(2):
             quantise(-1, 3 + v, 4 + v)
             first_product(0, v)
+        round_g(1)
         for j in (2, 3):
-            gather(1, j)
+            gather(2, j)
         silus(-1)
 
         for n in range(LAST):
-            round_g(n + 1)
-            if n - 1 in HELPED:
-                help_multiply(n - 1)
             for v in range(2):
                 apply_first_factor(n, v)
+            if n in HELPED:
+                help_multiply(n)
             for v in range(2):
                 if n > 0 and not helped(n - 1, v):
                     apply_silu_factor(n - 1, v)
-            for v in range(2):
-                turn_a(n + 1, v)
-                make_first_factor(n + 1, v)
-            if n - 1 in HELPED:
-                help_turn(n - 1)
-                help_copy(n - 1)
+            turn_a(n + 1, 0)
+            make_first_factor(n + 1, 0)
+            if n + 1 in HELPED:
+                make_tanh(n + 1)
+            turn_a(n + 1, 1)
+            make_first_factor(n + 1, 1)
+            if n + 1 in HELPED:
+                subtract_one(n + 1)
             for v in range(2):
                 if not helped(n, v):
                     turn_half(n, v)
-            if n + 2 < PAIRS:
-                for j in (0, 1):
-                    gather(n + 2, j)
+            if n in HELPED:
+                help_turn(n)
+                help_copy(n)
+            if n + 3 < PAIRS:
+                gather(n + 2, 0)
             for v in range(2):
                 if n >= 2:
                     quantise(n, 2 + 2 * v, 4 + 2 * v)
@@ -404,14 +412,16 @@ def tile_moe_bdx_mlp_silu_kernel(
                 second_product(n - 2, 0, 2)
             if n + 1 in WARM_PAIRS:
                 warm_up(n + 1)
+            if n + 3 == PAIRS:
+                gather(n + 2, 0)
             if n + 2 < PAIRS:
+                gather(n + 2, 1)
+            if n + 3 < PAIRS:
                 for j in (2, 3):
-                    gather(n + 2, j)
-            if n + 1 in HELPED:
-                make_tanh(n + 1)
+                    gather(n + 3, j)
             silus(n)
-            if n + 1 in HELPED:
-                subtract_one(n + 1)
+            if n + 2 < PAIRS:
+                round_g(n + 2)
             if n >= 2:
                 empty_dx(n - 2, 0, 2)
 

@@ -18,12 +18,14 @@ GATE_COLS = 2 * PAIR
 STREAM_BUFS = 10
 A_BUFS = 10
 SILU_BUFS = 6
-WORK_TILES = 4
+WORK_TILES = 5
 HELPED = (1, 3, 5, 7)
-SILUS_BY_STEP = (1, 1, 3, 0, 3, 0, 3, 0, 3, 2, 0)
+SHORT_STEP = 5
+ROUND_SHARE = 112
+SILUS_BY_STEP = (2, 0, 4, 1, 3, 1, 1, 0, 2, 2, 0)
 
-W2_GROUPS = ((0, 2), (2, 6), (6, 12), (12, E))
-W1_GROUPS = ((0, 6), (6, E))
+W2_GROUPS = ((0, 2), (2, 6), (6, 14), (14, E))
+W1_GROUPS = ((0, 8), (8, E))
 WARM_PAIRS = range(2, 9)
 
 FLOPS = 2 * S * (N * H + H * K)
@@ -69,8 +71,8 @@ def tile_moe_bdx_mlp_silu_kernel(
         def silu_slot(e, dtype):
             return keep.tile([P, WIDE], dtype, name=f"silu{silu_order.index(e) % SILU_BUFS}", align_bytes=64)
 
-        silu = {0: silu_slot(0, F32)}
-        zero = silu[0][:, 0:1]
+        silu = {}
+        zero = work[1][:, 3 * PAIR : 3 * PAIR + 1]
         nc.vector.memset(zero, 0.0)
         for g in W2_GROUPS:
             nc.vector.memset(w2_plane[g][:].bitcast(I32), 0)
@@ -121,8 +123,8 @@ def tile_moe_bdx_mlp_silu_kernel(
         load_a(0)
         load_w2(0)
         load_plane(w2_plane, w2_scales, W2_GROUPS[0])
-        load_a(1)
         load_gate(2)
+        load_a(1)
         load_plane(w2_plane, w2_scales, W2_GROUPS[1])
         load_w2(1)
         load_a(2)
@@ -130,13 +132,13 @@ def tile_moe_bdx_mlp_silu_kernel(
         load_w2(2)
         load_a(3)
         for n in range(2, LAST + 3):
-            if n == 5:
+            if 2 < n < PAIRS - 2:
                 load_a(n + 2)
             load_w1(n - 2)
             for g in W1_GROUPS:
                 if g[0] == 2 * (n - 2):
                     load_plane(w1_plane, w1_scales, g)
-            if n + 2 < PAIRS and n != 5:
+            if n == 2:
                 load_a(n + 2)
             if n + 1 < PAIRS:
                 load_w2(n + 1)
@@ -170,7 +172,7 @@ def tile_moe_bdx_mlp_silu_kernel(
             if (n, v) == (0, 1):
                 return first_odd[:].rearrange("p (u x) -> p u x", u=2)
             if v == 1 or n == 0:
-                return unit_pair(n - 1, 0, 1)
+                return unit_pair(n - (n > SHORT_STEP), 0, 1)
             if n - 1 in HELPED:
                 return unit_pair(n + 1, da_units(n - 1)[1], da_units(n - 1)[1] + 1)
             return unit_pair(n + 1, *(da_units(n - 1) if n < LAST else (4, 5)))
@@ -186,10 +188,17 @@ def tile_moe_bdx_mlp_silu_kernel(
 
         def round_g(m):
             by_j = units(m - 3, 0, 6).rearrange("p (u x) -> p u x", u=2)[:, :, 0 : 2 * PAIR]
+            by_j = by_j.rearrange("p u (j s) -> p u j s", j=2)
+            cut = PAIR - ROUND_SHARE if m in (4, 6, 9) else PAIR
             nc.scalar.copy(
-                rounded(m - 1, 3, 5).rearrange("p (s i) (u j) -> p s u j i", i=2, u=2),
-                by_j.rearrange("p u (j s i) -> p s u j i", j=2, i=2),
+                rounded(m - 1, 3, 5)[:, 0:cut, :].rearrange("p (s i) (u j) -> p s u j i", i=2, u=2),
+                by_j[:, :, :, 0:cut].rearrange("p u j (s i) -> p s u j i", i=2),
             )
+            if cut < PAIR:
+                nc.gpsimd.tensor_copy(
+                    rounded(m - 1, 3, 5)[:, cut:PAIR, :].rearrange("p s (u j) -> p s u j", u=2),
+                    by_j[:, :, :, cut:PAIR].rearrange("p u j s -> p s u j"),
+                )
 
         def quantise(n, u0, u1):
             if n not in codes:
@@ -208,8 +217,7 @@ def tile_moe_bdx_mlp_silu_kernel(
 
         def silu_factor(e):
             n, v = divmod(e, 2)
-            if e > 0:
-                silu[e] = silu_slot(e, F32)
+            silu[e] = silu_slot(e, F32)
             nc.scalar.activation(
                 silu[e][:].rearrange("p (s i j) -> p s j i", i=2, j=PACK),
                 a_sb[n][:, :, v * C : (v + 1) * C].rearrange("p j (s i) -> p s j i", i=2),
@@ -293,7 +301,8 @@ def tile_moe_bdx_mlp_silu_kernel(
             return f"turned{(v + sum(m <= n for m in HELPED)) % 2}"
 
         def turn_half(n, v):
-            turned[n, v] = banks.tile([P, PACK, C], F32, name=turn_bank(n, v))
+            name = f"bank{LAST % 2}{v}" if n == LAST - 1 else turn_bank(n, v)
+            turned[n, v] = banks.tile([P, PACK, C], F32, name=name)
             for j in range(PACK):
                 nc.tensor.transpose(turned[n, v][:, j, :], half[n, v][:, j * P : (j + 1) * P], ident[:])
 
@@ -369,6 +378,8 @@ def tile_moe_bdx_mlp_silu_kernel(
             make_first_factor(0, v)
         for j in range(PACK):
             gather(1, j)
+        for j in (0, 1):
+            gather(2, j)
         for v in range(2):
             quantise(-1, 3 + v, 4 + v)
             first_product(0, v)
@@ -377,7 +388,24 @@ def tile_moe_bdx_mlp_silu_kernel(
             gather(2, j)
         silus(-1)
 
+        def quantise_and_multiply(n):
+            for v in range(2):
+                if n >= 2:
+                    quantise(n, 2 + 2 * v, 4 + 2 * v)
+                else:
+                    quantise(n, 3 + v, 4 + v)
+            for v in range(2):
+                first_product(n + 1, v)
+            if n == LAST - 1:
+                for v in range(2):
+                    turn_half(n, v)
+            if n >= 2:
+                second_product(n - 2, 0, 2)
+            if n + 1 in WARM_PAIRS:
+                warm_up(n + 1)
+
         for n in range(LAST):
+            first = n + 3 if n < SHORT_STEP else n + 2
             for v in range(2):
                 apply_first_factor(n, v)
             if n in HELPED:
@@ -394,48 +422,38 @@ def tile_moe_bdx_mlp_silu_kernel(
             if n + 1 in HELPED:
                 subtract_one(n + 1)
             for v in range(2):
-                if not helped(n, v):
+                if not helped(n, v) and n < LAST - 1:
                     turn_half(n, v)
             if n in HELPED:
                 help_turn(n)
                 help_copy(n)
-            if n + 3 < PAIRS:
-                gather(n + 2, 0)
-            for v in range(2):
-                if n >= 2:
-                    quantise(n, 2 + 2 * v, 4 + 2 * v)
-                else:
-                    quantise(n, 3 + v, 4 + v)
-            for v in range(2):
-                first_product(n + 1, v)
-            if n >= 2:
-                second_product(n - 2, 0, 2)
-            if n + 1 in WARM_PAIRS:
-                warm_up(n + 1)
-            if n + 3 == PAIRS:
-                gather(n + 2, 0)
-            if n + 2 < PAIRS:
-                gather(n + 2, 1)
-            if n + 3 < PAIRS:
-                for j in (2, 3):
-                    gather(n + 3, j)
-            silus(n)
+            early = (0, 1) if n != SHORT_STEP and first < PAIRS else ()
+            late = (2, 3) if n + 3 < PAIRS else ()
+            if early and late:
+                gather(first, 0)
+            quantise_and_multiply(n)
+            for j in early[1:] if late else early:
+                gather(first, j)
+            for j in late:
+                gather(n + 3, j)
             if n + 2 < PAIRS:
                 round_g(n + 2)
+            silus(n)
             if n >= 2:
                 empty_dx(n - 2, 0, 2)
 
-        for v in range(2):
-            apply_silu_factor(LAST - 1, v)
+        quantise(LAST, 2, 4)
         for v in range(2):
             apply_first_factor(LAST, v)
             turn_half(LAST, v)
+        for v in range(2):
+            apply_silu_factor(LAST - 1, v)
+        apply_silu_factor(LAST, 0)
+        quantise(LAST + 1, 2, 4)
+        apply_silu_factor(LAST, 1)
         for m in (LAST - 2, LAST - 1):
-            quantise(m + 2, 2, 4)
             second_product(m, 0, 2)
             empty_dx(m, 0, 2)
-        for v in range(2):
-            apply_silu_factor(LAST, v)
         quantise(LAST + 2, 2, 3)
         second_product(LAST, 0, 1)
         empty_dx(LAST, 0, 1)
@@ -449,7 +467,7 @@ def tile_moe_bdx_mlp_silu_kernel(
                 if r == 0:
                     nc.vector.tensor_copy(dst[:], dx_sb[h][:].indirect(pos_sb[r][:]))
                     continue
-                cuts = (0, T // 2, T) if (r, h) == (TOP - 1, K_TILES - 1) else (0, T)
+                cuts = (0, T // 2, T - C, T) if (r, h) == (TOP - 1, K_TILES - 1) else (0, T)
                 for t0, t1 in zip(cuts, cuts[1:]):
                     entries = pos_sb[r][:, t0 // LIST_COL : t1 // LIST_COL]
                     nc.vector.tensor_tensor(dst[:, t0:t1], dx_sb[h][:].indirect(entries), so_far[:, t0:t1], ALU.add)

@@ -26,7 +26,7 @@ SILUS_BY_STEP = (2, 0, 4, 1, 3, 1, 1, 0, 2, 2, 0)
 
 W2_GROUPS = ((0, 2), (2, 6), (6, 14), (14, E))
 W1_GROUPS = ((0, 8), (8, E))
-WARM_PAIRS = range(2, 9)
+WARM_PAIRS = ()
 
 FLOPS = 2 * S * (N * H + H * K)
 BYTES = 4 * (N * T + H * S + S + K * T) + E * (2 * P + 16) * (H + K) + 2 * P * (S + TOP * T) // LIST_COL

@@ -14,19 +14,13 @@ PAIR = 2 * C
 PAIRS = E // 2
 LAST = PAIRS - 1
 WIDE = PACK * C
-GATE_COLS = 2 * PAIR
-STREAM_BUFS = 10
-A_BUFS = 10
-SILU_BUFS = 6
-WORK_TILES = 5
-HELPED = (1, 3, 5, 7)
-SHORT_STEP = 5
-ROUND_SHARE = 112
-SILUS_BY_STEP = (2, 0, 4, 1, 3, 1, 1, 0, 2, 2, 0)
+HALF = T // 2
+FIRST_HELPED = 2
+VECTOR_EMPTIES = 7
 
-W2_GROUPS = ((0, 2), (2, 6), (6, 14), (14, E))
-W1_GROUPS = ((0, 8), (8, E))
-WARM_PAIRS = ()
+GATE_GROUPS = ((0, 2), (2, 5), (5, PAIRS))
+W2_GROUPS = ((0, 2), (2, 5), (5, PAIRS))
+W1_GROUPS = ((0, 4), (4, PAIRS))
 
 FLOPS = 2 * S * (N * H + H * K)
 BYTES = 4 * (N * T + H * S + S + K * T) + E * (2 * P + 16) * (H + K) + 2 * P * (S + TOP * T) // LIST_COL
@@ -49,427 +43,324 @@ def tile_moe_bdx_mlp_silu_kernel(
     nc = tc.nc
     with ExitStack() as ctx:
         keep = ctx.enter_context(tc.tile_pool(name="keep", bufs=1))
-        ring2 = ctx.enter_context(tc.tile_pool(name="ring2", bufs=2))
-        ring3 = ctx.enter_context(tc.tile_pool(name="ring3", bufs=STREAM_BUFS))
-        a_ring = ctx.enter_context(tc.tile_pool(name="a_ring", bufs=A_BUFS))
         banks = ctx.enter_context(tc.psum_pool(name="banks", bufs=1))
-        banks2 = ctx.enter_context(tc.psum_pool(name="banks2", bufs=2))
 
         offs_sb = keep.tile([P, S // LIST_COL], U16, name="offs_sb")
         pos_sb = [keep.tile([P, T // LIST_COL], U16, name=f"pos_sb{r}") for r in range(TOP)]
         dy_sb = [keep.tile([P, T], F32, name=f"dy_sb{j}") for j in range(PACK)]
-        gate_sb, a_sb, w2_sb, w1_sb = {}, {}, {}, {}
-        w2_plane = {g: keep.tile([P, g[1] - g[0], H], U8, name=f"w2_plane{g[0]}", align_bytes=64) for g in W2_GROUPS}
-        w1_plane = {g: keep.tile([P, g[1] - g[0], K], U8, name=f"w1_plane{g[0]}", align_bytes=64) for g in W1_GROUPS}
+        gate_sb = {g: keep.tile([P, (g[1] - g[0]) * PAIR], F32, name=f"gate_sb{g[0]}") for g in GATE_GROUPS}
+        a_sb = [keep.tile([P, PACK, PAIR], F32, name=f"a_sb{n}") for n in range(PAIRS)]
+        w2_sb = [keep.tile([P, 2, 2 * H], U8, name=f"w2_sb{n}", align_bytes=64) for n in range(PAIRS)]
+        w1_sb = [keep.tile([P, 4, 2 * K], U8, name=f"w1_sb{n}", align_bytes=64) for n in range(PAIRS // 2)]
+        w2_plane = {g: keep.tile([P, 2 * (g[1] - g[0]), H], U8, name=f"w2_plane{g[0]}", align_bytes=64) for g in W2_GROUPS}
+        w1_plane = {g: keep.tile([P, 2 * (g[1] - g[0]), K], U8, name=f"w1_plane{g[0]}", align_bytes=64) for g in W1_GROUPS}
         dx_sb = [keep.tile([P, S], F32, name=f"dx_sb{h}") for h in range(K_TILES)]
         ident = keep.tile([P, P], F32, name="ident")
-        work = [keep.tile([P, 7 * PAIR], F32, name=f"work{x}", align_bytes=64) for x in range(WORK_TILES)]
-        code_scales = [keep.tile([P, 2 * PAIR], U8, name=f"code_scales{x}", align_bytes=64) for x in range(2)]
+        gathered = [keep.tile([P, PACK * PAIR], F32, name=f"gathered{x}") for x in range(2)]
+        zeros = keep.tile([P, 16], F32, name="zeros")
+        first_gathered = keep.tile([P, PACK * PAIR], F32, name="first_gathered")
+        early = keep.tile([P, PACK * 2 * PAIR], F32, name="early")
+        first_g = keep.tile([P, WIDE], F32, name="first_g", align_bytes=64)
+        rounded = keep.tile([P, 2 * WIDE], F32, name="rounded", align_bytes=64)
+        silu = [keep.tile([P, WIDE], F32, name=f"silu{v}") for v in range(2)]
 
-        silu_order = [e for e in range(E) if not (e % 2 == 0 and e // 2 in HELPED)]
-
-        def silu_slot(e, dtype):
-            return keep.tile([P, WIDE], dtype, name=f"silu{silu_order.index(e) % SILU_BUFS}", align_bytes=64)
-
-        silu = {}
-        zero = work[1][:, 3 * PAIR : 3 * PAIR + 1]
+        zero, first_bias = zeros[:, 0:1], zeros[:, 8:9]
         nc.vector.memset(zero, 0.0)
         for g in W2_GROUPS:
             nc.vector.memset(w2_plane[g][:].bitcast(I32), 0)
-        make_identity(nc, ident[:])
         for g in W1_GROUPS:
             nc.gpsimd.memset(w1_plane[g][:].bitcast(I32), 0)
+        make_identity(nc, ident[:])
 
         dy_rows = dyT.rearrange("(p j) t -> p j t", j=PACK)
         a_rows = a.rearrange("(p j) s -> p j s", j=PACK)
 
-        def load_dy(j):
-            nc.sync.dma_start(dy_sb[j][:], dy_rows[:, j, :])
+        def group_of(groups, n):
+            return [g for g in groups if g[0] <= n < g[1]][0]
 
-        def load_gate(c):
-            gate_sb[c] = keep.tile([P, GATE_COLS], F32, name=f"gate_sb{c}")
-            s0, s1 = max((2 * c - 1) * PAIR, 0), min((2 * c + 1) * PAIR, S)
-            first = s0 - (2 * c - 1) * PAIR
-            nc.sync.dma_start(gate_sb[c][:, first : first + s1 - s0], gate[0:P, s0:s1])
+        def load_gate(g):
+            nc.sync.dma_start(gate_sb[g][:], gate[0:P, g[0] * PAIR : g[1] * PAIR])
 
         def load_a(n):
-            a_sb[n] = a_ring.tile([P, PACK, PAIR], F32, name="a_sb")
             nc.sync.dma_start(a_sb[n][:], a_rows[:, :, n * PAIR : (n + 1) * PAIR])
 
-        def load_words(pool, tiles, words, n, name):
-            tiles[n] = pool.tile([P, 2, words.shape[-1]], U8, name=name, align_bytes=64)
-            src = words[2 * n : 2 * n + 2, 0].rearrange("e p b -> p e b")
-            nc.sync.dma_start(tiles[n][:].bitcast(I32), src.bitcast(I32))
-
-        def load_w2(n):
-            load_words(ring3, w2_sb, w2_words, n, "w2_sb")
-
-        def load_w1(n):
-            load_words(a_ring, w1_sb, w1_words, n, "w1_sb")
+        def load_words(tile, words, e0, e1):
+            nc.sync.dma_start(tile[:].bitcast(I32), words[e0:e1, 0].rearrange("e p b -> p e b").bitcast(I32))
 
         def load_plane(planes, scale_rows, g):
             for r in range(4):
-                src = scale_rows[g[0] : g[1], 0, r:16:4, :].rearrange("e f i -> f e i")
+                src = scale_rows[2 * g[0] : 2 * g[1], 0, r:16:4, :].rearrange("e f i -> f e i")
                 nc.sync.dma_start(planes[g][r:P:32, :, :].bitcast(I32), src.bitcast(I32))
 
-        def plane_of(planes, e):
-            return [plane[:, e - e0, :] for (e0, e1), plane in planes.items() if e0 <= e < e1][0]
+        def plane_of(planes, n, v):
+            g = group_of(planes, n)
+            return planes[g][:, 2 * (n - g[0]) + v, :]
 
         nc.sync.dma_start(offs_sb[:], offs)
-        load_gate(0)
         for j in range(PACK):
-            load_dy(j)
-        load_gate(1)
+            nc.sync.dma_start(dy_sb[j][:], dy_rows[:, j, :])
+        load_gate(GATE_GROUPS[0])
         load_a(0)
-        load_w2(0)
-        load_plane(w2_plane, w2_scales, W2_GROUPS[0])
-        load_gate(2)
         load_a(1)
-        load_plane(w2_plane, w2_scales, W2_GROUPS[1])
-        load_w2(1)
-        load_a(2)
-        load_gate(3)
-        load_w2(2)
-        load_a(3)
-        for n in range(2, LAST + 3):
-            if 2 < n < PAIRS - 2:
-                load_a(n + 2)
-            load_w1(n - 2)
+        for s in range(PAIRS + 2):
+            m = s - 2
+            if m >= 0 and m % 2 == 0:
+                load_words(w1_sb[m // 2], w1_words, 2 * m, 2 * m + 4)
             for g in W1_GROUPS:
-                if g[0] == 2 * (n - 2):
+                if g[0] == m:
                     load_plane(w1_plane, w1_scales, g)
-            if n == 2:
-                load_a(n + 2)
-            if n + 1 < PAIRS:
-                load_w2(n + 1)
+            if s < PAIRS:
+                load_words(w2_sb[s], w2_words, 2 * s, 2 * s + 2)
             for g in W2_GROUPS:
-                if g[0] == 2 * (n + 1):
+                if g[0] == s:
                     load_plane(w2_plane, w2_scales, g)
-            if n in (2, 4):
-                load_gate((n + 6) // 2)
+            for g in GATE_GROUPS[1:]:
+                if g[0] == s + 2:
+                    load_gate(g)
+            if 0 < s < PAIRS - 1:
+                load_a(s + 1)
         for r, pos in enumerate((pos1, pos2, pos3, pos4)):
             nc.sync.dma_start(pos_sb[r][:], pos)
 
-        def silus_made(n):
-            return sum(SILUS_BY_STEP[: n + 2])
+        nc.scalar.activation(first_bias, zero, ACT.Silu)
 
-        first_odd = keep.tile([P, WIDE], F32, name="first_odd", align_bytes=64)
-        dh_ps, turned, codes, half, tanh_less_one = {}, {}, {}, {}, {}
+        def gathered_of(m):
+            if m in (1, 2):
+                return early[:].rearrange("p (j s) -> p j s", j=PACK)[:, :, (m - 1) * PAIR : m * PAIR]
+            tile = gathered[m % 2] if m else first_gathered
+            return tile[:, 0 : PACK * PAIR].rearrange("p (j s) -> p j s", j=PACK)
 
-        def units(n, u0, u1):
-            return work[n % WORK_TILES][:, u0 * PAIR : u1 * PAIR]
+        def gather(on_vector, dst, j, m0, m1):
+            found = dy_sb[j][:].indirect(offs_sb[:, m0 * PAIR // LIST_COL : m1 * PAIR // LIST_COL])
+            if on_vector:
+                nc.vector.tensor_copy(dst, found)
+            else:
+                nc.scalar.activation(dst, found, ACT.Copy)
 
-        def unit_pair(n, u0, u1):
-            return work[n % WORK_TILES][:].rearrange("p (u x) -> p u x", x=PAIR)[:, u0 : u1 + 1 : u1 - u0, :]
+        def gather_rows(on_vector, m, j0, j1):
+            for j in range(j0, j1):
+                gather(on_vector, gathered_of(m)[:, j, :], j, m, m + 1)
 
-        def da_units(m):
-            return (2, 5) if m + 2 < LAST else (2, 3)
+        def g_of(m):
+            return (rounded[:, 0:WIDE] if m else first_g[:]).bitcast(BF16)
 
-        def rounded(n, u0, u1):
-            return units(n, u0, u1).bitcast(BF16).rearrange("p (s j) -> p s j", j=PACK)
+        def da_of(n):
+            return (rounded[:, WIDE:] if n < LAST else rounded[:, 0:WIDE]).bitcast(BF16)
 
-        def first_factor(n, v):
-            if (n, v) == (0, 1):
-                return first_odd[:].rearrange("p (u x) -> p u x", u=2)
-            if v == 1 or n == 0:
-                return unit_pair(n - (n > SHORT_STEP), 0, 1)
-            if n - 1 in HELPED:
-                return unit_pair(n + 1, da_units(n - 1)[1], da_units(n - 1)[1] + 1)
-            return unit_pair(n + 1, *(da_units(n - 1) if n < LAST else (4, 5)))
-
-        def gate_of(m):
-            c, side = divmod(m + 1, 2)
-            return gate_sb[c][:, side * PAIR : (side + 1) * PAIR]
-
-        def gather(m, j):
-            u = (0, 1, 3, 4)[j]
-            entries = offs_sb[:, m * PAIR // LIST_COL : (m + 1) * PAIR // LIST_COL]
-            nc.vector.tensor_tensor(units(m - 3, u, u + 1), dy_sb[j][:].indirect(entries), gate_of(m), ALU.mult)
-
-        def round_g(m):
-            by_j = units(m - 3, 0, 6).rearrange("p (u x) -> p u x", u=2)[:, :, 0 : 2 * PAIR]
-            by_j = by_j.rearrange("p u (j s) -> p u j s", j=2)
-            cut = PAIR - ROUND_SHARE if m in (4, 6, 9) else PAIR
-            nc.scalar.copy(
-                rounded(m - 1, 3, 5)[:, 0:cut, :].rearrange("p (s i) (u j) -> p s u j i", i=2, u=2),
-                by_j[:, :, :, 0:cut].rearrange("p u j (s i) -> p s u j i", i=2),
-            )
-            if cut < PAIR:
-                nc.gpsimd.tensor_copy(
-                    rounded(m - 1, 3, 5)[:, cut:PAIR, :].rearrange("p s (u j) -> p s u j", u=2),
-                    by_j[:, :, :, cut:PAIR].rearrange("p u j s -> p s u j"),
+        def round_g(m, v0, v1):
+            g = group_of(GATE_GROUPS, m)
+            first = (m - g[0]) * PAIR
+            weights = gate_sb[g][:, first + v0 * C : first + v1 * C]
+            if m >= FIRST_HELPED:
+                nc.gpsimd.tensor_tensor(
+                    g_of(m).rearrange("p (s j) -> p s j", j=PACK),
+                    gathered_of(m).rearrange("p j s -> p s j"),
+                    weights.unsqueeze(2).to_broadcast([P, PAIR, PACK]),
+                    ALU.mult,
                 )
-
-        def quantise(n, u0, u1):
-            if n not in codes:
-                if n == 0:
-                    codes[n] = keep.tile([P, WIDE], U32, name="first_odd", align_bytes=64)
-                elif 0 < n < LAST - 1:
-                    codes[n] = silu_slot(2 * (n - 1) + (n - 1 in HELPED), U32)
-                else:
-                    codes[n] = ring2.tile([P, WIDE], U32, name="codes", align_bytes=64)
-            cols = slice((u0 - 2) * C, (u1 - 2) * C)
-            nc.vector.quantize_mx(
-                out=codes[n][:, cols].bitcast(FP8X4),
-                scales=code_scales[n % 2][:, cols],
-                in_=units(n, u0, u1).bitcast(BF16),
+                return
+            weights = weights.rearrange("p (s i) -> p s i", i=2)
+            nc.vector.tensor_tensor(
+                g_of(m)[:, v0 * WIDE : v1 * WIDE].rearrange("p (s i j) -> p s j i", i=2, j=PACK),
+                gathered_of(m)[:, :, v0 * C : v1 * C].rearrange("p j (s i) -> p s j i", i=2),
+                weights.unsqueeze(2).to_broadcast([P, (v1 - v0) * C // 2, PACK, 2]),
+                ALU.mult,
             )
 
-        def silu_factor(e):
-            n, v = divmod(e, 2)
-            silu[e] = silu_slot(e, F32)
+        codes, scales, dh_ps, a_turned, half, turned, dx_ps = {}, {}, {}, {}, {}, {}, {}
+
+        def quantise(s, values, c0, c1):
+            if s not in codes:
+                codes[s] = keep.tile([P, 2 * PAIR], U32, name="codes" if 0 <= s <= LAST else "end_codes", align_bytes=64)
+                scales[s] = keep.tile([P, 2 * PAIR], U8, name="scales" if 0 <= s <= LAST else "end_scales", align_bytes=64)
+            nc.vector.quantize_mx(out=codes[s][:, c0:c1].bitcast(FP8X4), scales=scales[s][:, c0:c1], in_=values)
+
+        def make_silu(n, v):
             nc.scalar.activation(
-                silu[e][:].rearrange("p (s i j) -> p s j i", i=2, j=PACK),
+                silu[v][:].rearrange("p (s i j) -> p s j i", i=2, j=PACK),
                 a_sb[n][:, :, v * C : (v + 1) * C].rearrange("p j (s i) -> p s j i", i=2),
                 ACT.Silu,
                 scale=-1.0,
             )
 
-        def bank(side, v):
-            return banks.tile([P, WIDE], F32, name=f"bank{side}{v}")
-
-        a_turned = {}
-
         def turn_a(n, v):
-            a_turned[n, v] = bank(n % 2, v)
+            a_turned[n, v] = banks.tile([P, WIDE], F32, name=f"a_bank{v}")
             for j in range(PACK):
                 nc.tensor.transpose(a_turned[n, v][:, j * P : (j + 1) * P], a_sb[n][:, j, v * C : (v + 1) * C], ident[:])
 
-        def helped(n, v):
-            return v == 0 and n in HELPED
+        def tanh_of(n, v):
+            return gathered[n % 2][:, (1 - v) * WIDE : (2 - v) * WIDE]
 
-        def make_first_factor(n, v):
-            if helped(n, v):
-                nc.scalar.activation(
-                    first_factor(n, v).rearrange("s u (q j) -> s u q j", j=PACK),
-                    a_turned[n, v][:].rearrange("s (j u q) -> s u q j", j=PACK, u=2),
-                    ACT.Silu,
-                    scale=-1.0,
-                )
-            else:
-                nc.scalar.activation(
-                    first_factor(n, v),
-                    a_turned[n, v][:].rearrange("s (u x) -> s u x", u=2),
-                    ACT.Tanh,
-                    bias=(first_bias, zero)[v] if n == 0 else 0.0,
-                    scale=-0.5,
-                )
+        def make_tanh(n, v):
+            bias = first_bias if (n, v) == (0, 0) else 0.0
+            nc.scalar.activation(tanh_of(n, v), a_turned[n, v][:], ACT.Tanh, bias=bias, scale=-0.5)
 
-        tanh_odd = {}
-
-        def make_tanh(n):
-            tanh_odd[n] = ring2.tile([P, P, PACK], F32, name="tanh_odd")
-            nc.scalar.activation(tanh_odd[n][:], a_turned[n, 0][:].rearrange("s (j p) -> s p j", j=PACK), ACT.Tanh, scale=-0.5)
-
-        def subtract_one(n):
-            tanh_less_one[n] = ring2.tile([P, WIDE], F32, name="tanh_less_one")
-            nc.scalar.activation(tanh_less_one[n][:], tanh_odd[n][:].rearrange("s p j -> s (p j)"), ACT.Copy, bias=-1.0)
-
-        def multiply_w2(dst, n, v):
-            cols = slice((1 + v) * C, (2 + v) * C)
+        def first_product(n, v):
+            dh_ps[n, v] = banks.tile([P, H], F32, name=f"dh_bank{v}")
             nc.tensor.matmul_mx(
-                out=dst[:],
-                lhsT=codes[n - 1][:, cols].bitcast(FP8X4),
-                lhsT_scale=code_scales[(n - 1) % 2][:, cols],
+                out=dh_ps[n, v][:],
+                lhsT=codes[n - 1][:, v * C : (v + 1) * C].bitcast(FP8X4),
+                lhsT_scale=scales[n - 1][:, v * C : (v + 1) * C],
                 rhs=w2_sb[n][:, v, :].bitcast(FP4X4),
-                rhs_scale=plane_of(w2_plane, 2 * n + v),
+                rhs_scale=plane_of(w2_plane, n, v),
                 start=True,
                 stop=True,
             )
 
-        def first_product(n, v):
-            dh_ps[n, v] = bank((n + 1) % 2, v)
-            multiply_w2(dh_ps[n, v], n, v)
-
-        def warm_up(n):
-            unread = banks2.tile([P, H], F32, name="dx")
-            multiply_w2(unread, n, 1)
-
-        def apply_first_factor(n, v):
-            half[n, v] = ring2.tile([P, WIDE], F32, name=f"half{v}")
-            if helped(n, v):
-                dh = dh_ps[n, v][:].rearrange("s (u x) -> s u x", u=2)
-                dst = half[n, v][:].rearrange("s (u x) -> s u x", u=2)
-                factor = first_factor(n, v)
-            else:
-                dh = dh_ps[n, v][:].rearrange("s (p u j) -> s u j p", u=2, j=2)
-                dst = half[n, v][:].rearrange("s (u j p) -> s u j p", u=2, j=2)
-                factor = first_factor(n, v).rearrange("s u (j p) -> s u j p", j=2)
-            nc.vector.scalar_tensor_tensor(dst, factor, 1.0, dh, ALU.subtract, ALU.mult)
-
-        def turn_bank(n, v):
-            return f"turned{(v + sum(m <= n for m in HELPED)) % 2}"
+        def apply_tanh(n, v):
+            half[n, v] = keep.tile([P, PACK, P], F32, name=f"half{v}")
+            nc.vector.scalar_tensor_tensor(
+                half[n, v][:],
+                tanh_of(n, v).rearrange("s (j p) -> s j p", j=PACK),
+                1.0,
+                dh_ps[n, v][:].rearrange("s (p j) -> s j p", j=PACK),
+                ALU.subtract,
+                ALU.mult,
+            )
 
         def turn_half(n, v):
-            name = f"bank{LAST % 2}{v}" if n == LAST - 1 else turn_bank(n, v)
-            turned[n, v] = banks.tile([P, PACK, C], F32, name=name)
+            turned[n, v] = banks.tile([P, PACK, C], F32, name=f"half_bank{v}")
             for j in range(PACK):
-                nc.tensor.transpose(turned[n, v][:, j, :], half[n, v][:, j * P : (j + 1) * P], ident[:])
+                nc.tensor.transpose(turned[n, v][:, j, :], half[n, v][:, j, :], ident[:])
 
-        def apply_silu_factor(n, v):
-            u = da_units(n)[v]
+        def apply_silu(n, v):
             nc.vector.scalar_tensor_tensor(
-                rounded(n + 2, u, u + 1),
-                silu[2 * n + v][:].rearrange("p (s j) -> p s j", j=PACK),
+                da_of(n)[:, v * WIDE : (v + 1) * WIDE].rearrange("p (s j) -> p s j", j=PACK),
+                silu[v][:].rearrange("p (s j) -> p s j", j=PACK),
                 1.0,
                 turned[n, v][:].rearrange("p j s -> p s j"),
                 ALU.subtract,
                 ALU.mult,
             )
 
-        words = {}
-
-        def help_multiply(n):
-            words[n] = ring2.tile([P, PAIR], F32, name="words")
-            nc.gpsimd.tensor_tensor(words[n][:].bitcast(BF16), half[n, 0][:], tanh_less_one[n][:], ALU.mult)
-
-        def help_turn(n):
-            turned[n, 0] = banks.tile([P, 2, C], F32, name=turn_bank(n, 0))
-            for u in range(2):
-                nc.tensor.transpose(turned[n, 0][:, u, :], words[n][:, u:PAIR:2], ident[:])
-
-        def help_copy(n):
-            u = da_units(n)[0]
-            nc.scalar.copy(units(n + 2, u, u + 1).rearrange("p (s u) -> p s u", u=2), turned[n, 0][:].rearrange("p u s -> p s u"))
-
         def multiply_w1(dst, n, v, h):
-            u = da_units(n)[v]
-            cols = slice((u - 2) * C, (u - 1) * C)
+            cols = slice(PAIR + v * C, PAIR + (v + 1) * C)
             nc.tensor.matmul_mx(
                 out=dst,
-                lhsT=w1_sb[n][:, v, 2 * P * h : 2 * P * (h + 1)].bitcast(FP4X4),
-                lhsT_scale=plane_of(w1_plane, 2 * n + v)[:, P * h : P * (h + 1)],
-                rhs=codes[n + 2][:, cols].bitcast(FP8X4),
-                rhs_scale=code_scales[n % 2][:, cols],
+                lhsT=w1_sb[n // 2][:, 2 * (n % 2) + v, 2 * P * h : 2 * P * (h + 1)].bitcast(FP4X4),
+                lhsT_scale=plane_of(w1_plane, n, v)[:, P * h : P * (h + 1)],
+                rhs=codes[n + 1][:, cols].bitcast(FP8X4),
+                rhs_scale=scales[n + 1][:, cols],
                 start=True,
                 stop=True,
             )
 
-        dx_ps = {}
-
-        def second_product(n, v0, v1):
-            dx_ps[n] = banks2.tile([P, K_TILES, (v1 - v0) * C], F32, name="dx")
+        def second_product(n, v0, v1, bank):
+            dx_ps[n] = banks.tile([P, K_TILES, (v1 - v0) * C], F32, name=bank)
             for h in range(K_TILES):
                 for v in range(v0, v1):
                     multiply_w1(dx_ps[n][:, h, (v - v0) * C : (v - v0 + 1) * C], n, v, h)
 
+        def halve(on_vector, dst, src):
+            if on_vector:
+                nc.vector.tensor_scalar(dst, src, 0.5, None, ALU.mult)
+            else:
+                nc.scalar.activation(dst, src, ACT.Copy, scale=0.5)
+
         def empty_dx(n, v0, v1):
             for h in range(K_TILES):
-                nc.scalar.activation(dx_sb[h][:, n * PAIR + v0 * C : n * PAIR + v1 * C], dx_ps[n][:, h, :], ACT.Copy, scale=0.5)
+                halve(n < VECTOR_EMPTIES, dx_sb[h][:, n * PAIR + v0 * C : n * PAIR + v1 * C], dx_ps[n][:, h, :])
 
-        def last_second_product():
-            for h in range(K_TILES):
-                last = bank(1, h)[:, 0:C]
-                multiply_w1(last, LAST, 1, h)
-                nc.scalar.activation(dx_sb[h][:, S - C : S], last, ACT.Copy, scale=0.5)
-
-        def silus(n):
-            for e in silu_order[silus_made(n - 1) if n >= 0 else 0 : silus_made(n)]:
-                silu_factor(e)
-
-        first_bias = units(0, 3, 4)[:, 0:1]
-        nc.scalar.activation(first_bias, zero, ACT.Silu)
-
-        for j in range(PACK):
-            gather(0, j)
-        round_g(0)
+        gather_rows(True, 0, 0, PACK)
+        for j in range(PACK - 1):
+            gather(False, early[:, j * 2 * PAIR : (j + 1) * 2 * PAIR], j, 1, 3)
+        gather_rows(True, 1, PACK - 1, PACK)
+        gather_rows(False, 2, PACK - 1, PACK)
+        for v in range(2):
+            round_g(0, v, v + 1)
         for v in range(2):
             turn_a(0, v)
-            make_first_factor(0, v)
-        for j in range(PACK):
-            gather(1, j)
-        for j in (0, 1):
-            gather(2, j)
         for v in range(2):
-            quantise(-1, 3 + v, 4 + v)
+            quantise(-1, g_of(0)[:, v * WIDE : (v + 1) * WIDE], v * C, (v + 1) * C)
             first_product(0, v)
-        round_g(1)
-        for j in (2, 3):
-            gather(2, j)
-        silus(-1)
+            make_tanh(0, v)
+        round_g(1, 0, 2)
+        quantise(0, g_of(1), 0, PAIR)
 
-        def quantise_and_multiply(n):
+        for s in range(PAIRS):
+            if FIRST_HELPED <= s + 1 < PAIRS:
+                round_g(s + 1, 0, 2)
             for v in range(2):
-                if n >= 2:
-                    quantise(n, 2 + 2 * v, 4 + 2 * v)
-                else:
-                    quantise(n, 3 + v, 4 + v)
+                if s > 0:
+                    first_product(s, v)
+            if s >= 2:
+                second_product(s - 2, 0, 2, "dx_bank")
             for v in range(2):
-                first_product(n + 1, v)
-            if n == LAST - 1:
-                for v in range(2):
-                    turn_half(n, v)
-            if n >= 2:
-                second_product(n - 2, 0, 2)
-            if n + 1 in WARM_PAIRS:
-                warm_up(n + 1)
+                if s < LAST:
+                    turn_a(s + 1, v)
+            for v in range(2):
+                if s > 0:
+                    apply_silu(s - 1, v)
+                make_silu(s, v)
+            for v in range(2):
+                apply_tanh(s, v)
+                turn_half(s, v)
+            if s >= 2:
+                empty_dx(s - 2, 0, 2)
+            if 0 < s < PAIRS - 2:
+                for j in (2, 0, 1):
+                    gather_rows(False, s + 2, j, j + 1)
+                gather_rows(True, s + 2, PACK - 1, PACK)
+            if 0 < s < LAST:
+                quantise(s, rounded[:].bitcast(BF16), 0, 2 * PAIR)
+            for v in range(2):
+                if s < LAST:
+                    make_tanh(s + 1, v)
 
-        for n in range(LAST):
-            first = n + 3 if n < SHORT_STEP else n + 2
-            for v in range(2):
-                apply_first_factor(n, v)
-            if n in HELPED:
-                help_multiply(n)
-            for v in range(2):
-                if n > 0 and not helped(n - 1, v):
-                    apply_silu_factor(n - 1, v)
-            turn_a(n + 1, 0)
-            make_first_factor(n + 1, 0)
-            if n + 1 in HELPED:
-                make_tanh(n + 1)
-            turn_a(n + 1, 1)
-            make_first_factor(n + 1, 1)
-            if n + 1 in HELPED:
-                subtract_one(n + 1)
-            for v in range(2):
-                if not helped(n, v) and n < LAST - 1:
-                    turn_half(n, v)
-            if n in HELPED:
-                help_turn(n)
-                help_copy(n)
-            early = (0, 1) if n != SHORT_STEP and first < PAIRS else ()
-            late = (2, 3) if n + 3 < PAIRS else ()
-            if early and late:
-                gather(first, 0)
-            quantise_and_multiply(n)
-            for j in early[1:] if late else early:
-                gather(first, j)
-            for j in late:
-                gather(n + 3, j)
-            if n + 2 < PAIRS:
-                round_g(n + 2)
-            silus(n)
-            if n >= 2:
-                empty_dx(n - 2, 0, 2)
-
-        quantise(LAST, 2, 4)
+        quantise(LAST, da_of(LAST - 1), PAIR, 2 * PAIR)
+        second_product(LAST - 1, 0, 2, "spare_bank")
+        empty_dx(LAST - 1, 0, 2)
         for v in range(2):
-            apply_first_factor(LAST, v)
-            turn_half(LAST, v)
-        for v in range(2):
-            apply_silu_factor(LAST - 1, v)
-        apply_silu_factor(LAST, 0)
-        quantise(LAST + 1, 2, 4)
-        apply_silu_factor(LAST, 1)
-        for m in (LAST - 2, LAST - 1):
-            second_product(m, 0, 2)
-            empty_dx(m, 0, 2)
-        quantise(LAST + 2, 2, 3)
-        second_product(LAST, 0, 1)
+            apply_silu(LAST, v)
+        quantise(LAST + 1, da_of(LAST)[:, 0:WIDE], PAIR, PAIR + C)
+        second_product(LAST, 0, 1, "dh_bank0")
         empty_dx(LAST, 0, 1)
-        quantise(LAST + 2, 3, 4)
-        last_second_product()
+        quantise(LAST + 1, da_of(LAST)[:, WIDE:], PAIR + C, 2 * PAIR)
+        for h in range(K_TILES):
+            last = banks.tile([P, C], F32, name=f"a_bank{h}")
+            multiply_w1(last[:], LAST, 1, h)
+            halve(h == 0, dx_sb[h][:, S - C : S], last[:])
 
-        sums = [[keep.tile([P, T], F32, name=f"sum{h}_{x}") for x in range(2)] for h in range(K_TILES)]
-        for r in range(TOP):
-            for h in range(K_TILES):
-                dst, so_far = sums[h][r % 2], sums[h][(r + 1) % 2]
-                if r == 0:
-                    nc.vector.tensor_copy(dst[:], dx_sb[h][:].indirect(pos_sb[r][:]))
-                    continue
-                cuts = (0, T // 2, T - C, T) if (r, h) == (TOP - 1, K_TILES - 1) else (0, T)
-                for t0, t1 in zip(cuts, cuts[1:]):
-                    entries = pos_sb[r][:, t0 // LIST_COL : t1 // LIST_COL]
-                    nc.vector.tensor_tensor(dst[:, t0:t1], dx_sb[h][:].indirect(entries), so_far[:, t0:t1], ALU.add)
-                    if r == TOP - 1:
-                        nc.sync.dma_start(out[h * P : (h + 1) * P, t0:t1], dst[:, t0:t1])
+        parts = [(0, 0), (1, 0), (0, 1), (1, 1)]
+        got = {}
+
+        def fetch(on_vector, part, r, other=None):
+            h, u = parts[part]
+            got[part, r] = keep.tile([P, HALF], F32, name=f"got{part}_{r}")
+            found = dx_sb[h][:].indirect(pos_sb[r][:, u * HALF // LIST_COL : (u + 1) * HALF // LIST_COL])
+            if not on_vector:
+                nc.scalar.activation(got[part, r][:], found, ACT.Copy)
+            elif other is None:
+                nc.vector.tensor_copy(got[part, r][:], found)
+            else:
+                nc.vector.tensor_tensor(got[part, r][:], found, got[part, other][:], ALU.add)
+
+        def add(part, name, x, y):
+            got[part, name] = keep.tile([P, HALF], F32, name=f"got{part}_{name}")
+            nc.vector.tensor_tensor(got[part, name][:], got[part, x][:], got[part, y][:], ALU.add)
+            if name == "all":
+                h, u = parts[part]
+                nc.sync.dma_start(out[h * P : (h + 1) * P, u * HALF : (u + 1) * HALF], got[part, name][:])
+
+        fetch(True, 0, 0)
+        fetch(False, 1, 1)
+        fetch(True, 1, 0, 1)
+        fetch(False, 0, 1)
+        fetch(True, 0, 2, 1)
+        fetch(False, 2, 1)
+        fetch(True, 2, 0, 1)
+        fetch(False, 1, 3)
+        fetch(True, 1, 2, 3)
+        fetch(False, 3, 1)
+        fetch(True, 3, 0, 1)
+        add(1, "all", 0, 2)
+        fetch(False, 2, 3)
+        fetch(True, 2, 2, 3)
+        add(0, "three", 0, 2)
+        add(2, "all", 0, 2)
+        fetch(False, 0, 3)
+        fetch(False, 3, 2)
+        add(3, "three", 0, 2)
+        add(0, "all", "three", 3)
+        fetch(False, 3, 3)
+        add(3, "all", "three", 3)

@@ -57,15 +57,15 @@ def tile_moe_bdx_mlp_silu_kernel(
         dx_sb = [keep.tile([P, S], F32, name=f"dx_sb{h}") for h in range(K_TILES)]
         ident = keep.tile([P, P], F32, name="ident")
         gathered = [keep.tile([P, PACK * PAIR], F32, name=f"gathered{x}") for x in range(2)]
-        zeros = keep.tile([P, 16], F32, name="zeros")
         first_gathered = keep.tile([P, PACK * PAIR], F32, name="first_gathered")
         early = keep.tile([P, PACK * 2 * PAIR], F32, name="early")
         first_g = keep.tile([P, WIDE], F32, name="first_g", align_bytes=64)
-        rounded = keep.tile([P, 2 * WIDE], F32, name="rounded", align_bytes=64)
+        rounded = keep.tile([P, 3 * WIDE], F32, name="rounded", align_bytes=64)
         silu = [keep.tile([P, WIDE], F32, name=f"silu{v}") for v in range(2)]
 
-        zero, first_bias = zeros[:, 0:1], zeros[:, 8:9]
-        nc.vector.memset(zero, 0.0)
+        zeros = gathered[1][:, PAIR : 3 * PAIR : PAIR]
+        first_bias = gathered[1][:, 0:1]
+        nc.vector.memset(zeros, 0.0)
         for g in W2_GROUPS:
             nc.vector.memset(w2_plane[g][:].bitcast(I32), 0)
         for g in W1_GROUPS:
@@ -96,9 +96,10 @@ def tile_moe_bdx_mlp_silu_kernel(
             g = group_of(planes, n)
             return planes[g][:, 2 * (n - g[0]) + v, :]
 
-        nc.sync.dma_start(offs_sb[:], offs)
         for j in range(PACK):
             nc.sync.dma_start(dy_sb[j][:], dy_rows[:, j, :])
+            if j == 0:
+                nc.sync.dma_start(offs_sb[:], offs)
         load_gate(GATE_GROUPS[0])
         load_a(0)
         load_a(1)
@@ -122,7 +123,7 @@ def tile_moe_bdx_mlp_silu_kernel(
         for r, pos in enumerate((pos1, pos2, pos3, pos4)):
             nc.sync.dma_start(pos_sb[r][:], pos)
 
-        nc.scalar.activation(first_bias, zero, ACT.Silu)
+        nc.scalar.activation(first_bias, zeros[:, 0:1], ACT.Silu)
 
         def gathered_of(m):
             if m in (1, 2):
@@ -130,22 +131,26 @@ def tile_moe_bdx_mlp_silu_kernel(
             tile = gathered[m % 2] if m else first_gathered
             return tile[:, 0 : PACK * PAIR].rearrange("p (j s) -> p j s", j=PACK)
 
-        def gather(on_vector, dst, j, m0, m1):
-            found = dy_sb[j][:].indirect(offs_sb[:, m0 * PAIR // LIST_COL : m1 * PAIR // LIST_COL])
+        def gather(on_vector, dst, j, s0, s1):
+            found = dy_sb[j][:].indirect(offs_sb[:, s0 // LIST_COL : s1 // LIST_COL])
             if on_vector:
                 nc.vector.tensor_copy(dst, found)
             else:
                 nc.scalar.activation(dst, found, ACT.Copy)
 
+        def gather_slots(on_vector, m, j, s0, s1):
+            gather(on_vector, gathered_of(m)[:, j, s0:s1], j, m * PAIR + s0, m * PAIR + s1)
+
         def gather_rows(on_vector, m, j0, j1):
             for j in range(j0, j1):
-                gather(on_vector, gathered_of(m)[:, j, :], j, m, m + 1)
+                gather_slots(on_vector, m, j, 0, PAIR)
 
         def g_of(m):
-            return (rounded[:, 0:WIDE] if m else first_g[:]).bitcast(BF16)
+            unit = 2 * (m % 2) if m > 1 else 0
+            return (rounded[:, unit * WIDE : (unit + 1) * WIDE] if m else first_g[:]).bitcast(BF16)
 
         def da_of(n):
-            return (rounded[:, WIDE:] if n < LAST else rounded[:, 0:WIDE]).bitcast(BF16)
+            return (rounded[:, WIDE : 2 * WIDE] if n < LAST else rounded[:, 0:WIDE]).bitcast(BF16)
 
         def round_g(m, v0, v1):
             g = group_of(GATE_GROUPS, m)
@@ -180,27 +185,31 @@ def tile_moe_bdx_mlp_silu_kernel(
                 silu[v][:].rearrange("p (s i j) -> p s j i", i=2, j=PACK),
                 a_sb[n][:, :, v * C : (v + 1) * C].rearrange("p j (s i) -> p s j i", i=2),
                 ACT.Silu,
+                bias=zeros[:, 1:2] if (n, v) == (0, 1) else 0.0,
                 scale=-1.0,
             )
 
         def turn_a(n, v):
-            a_turned[n, v] = banks.tile([P, WIDE], F32, name=f"a_bank{v}")
+            a_turned[n, v] = banks.tile([P, WIDE], F32, name=("spare_bank", "dx_bank")[v] if n == 1 else f"bank{(n + 1) % 2}{v}")
             for j in range(PACK):
                 nc.tensor.transpose(a_turned[n, v][:, j * P : (j + 1) * P], a_sb[n][:, j, v * C : (v + 1) * C], ident[:])
 
         def tanh_of(n, v):
+            if n == 1:
+                return rounded[:, 2 * WIDE :] if v else first_gathered[:, 0:WIDE]
             return gathered[n % 2][:, (1 - v) * WIDE : (2 - v) * WIDE]
 
         def make_tanh(n, v):
-            bias = first_bias if (n, v) == (0, 0) else 0.0
+            bias = (first_bias, zeros[:, 0:1])[v] if n == 0 else 0.0
             nc.scalar.activation(tanh_of(n, v), a_turned[n, v][:], ACT.Tanh, bias=bias, scale=-0.5)
 
         def first_product(n, v):
-            dh_ps[n, v] = banks.tile([P, H], F32, name=f"dh_bank{v}")
+            cols = slice((n % 2) * PAIR + v * C, (n % 2) * PAIR + (v + 1) * C)
+            dh_ps[n, v] = banks.tile([P, H], F32, name=f"bank{n % 2}{v}")
             nc.tensor.matmul_mx(
                 out=dh_ps[n, v][:],
-                lhsT=codes[n - 1][:, v * C : (v + 1) * C].bitcast(FP8X4),
-                lhsT_scale=scales[n - 1][:, v * C : (v + 1) * C],
+                lhsT=codes[n - 1][:, cols].bitcast(FP8X4),
+                lhsT_scale=scales[n - 1][:, cols],
                 rhs=w2_sb[n][:, v, :].bitcast(FP4X4),
                 rhs_scale=plane_of(w2_plane, n, v),
                 start=True,
@@ -234,7 +243,7 @@ def tile_moe_bdx_mlp_silu_kernel(
             )
 
         def multiply_w1(dst, n, v, h):
-            cols = slice(PAIR + v * C, PAIR + (v + 1) * C)
+            cols = slice(((n + 1) % 2) * PAIR + v * C, ((n + 1) % 2) * PAIR + (v + 1) * C)
             nc.tensor.matmul_mx(
                 out=dst,
                 lhsT=w1_sb[n // 2][:, 2 * (n % 2) + v, 2 * P * h : 2 * P * (h + 1)].bitcast(FP4X4),
@@ -263,7 +272,7 @@ def tile_moe_bdx_mlp_silu_kernel(
 
         gather_rows(True, 0, 0, PACK)
         for j in range(PACK - 1):
-            gather(False, early[:, j * 2 * PAIR : (j + 1) * 2 * PAIR], j, 1, 3)
+            gather(False, early[:, j * 2 * PAIR : (j + 1) * 2 * PAIR], j, PAIR, 3 * PAIR)
         gather_rows(True, 1, PACK - 1, PACK)
         gather_rows(False, 2, PACK - 1, PACK)
         for v in range(2):
@@ -275,7 +284,10 @@ def tile_moe_bdx_mlp_silu_kernel(
             first_product(0, v)
             make_tanh(0, v)
         round_g(1, 0, 2)
-        quantise(0, g_of(1), 0, PAIR)
+        quantise(0, g_of(1), PAIR, 2 * PAIR)
+        for v in range(2):
+            turn_a(1, v)
+        gather_rows(True, 3, PACK - 1, PACK)
 
         for s in range(PAIRS):
             if FIRST_HELPED <= s + 1 < PAIRS:
@@ -286,48 +298,50 @@ def tile_moe_bdx_mlp_silu_kernel(
             if s >= 2:
                 second_product(s - 2, 0, 2, "dx_bank")
             for v in range(2):
-                if s < LAST:
-                    turn_a(s + 1, v)
-            for v in range(2):
                 if s > 0:
                     apply_silu(s - 1, v)
                 make_silu(s, v)
             for v in range(2):
                 apply_tanh(s, v)
                 turn_half(s, v)
+            for v in range(2):
+                if 0 < s < LAST:
+                    turn_a(s + 1, v)
             if s >= 2:
                 empty_dx(s - 2, 0, 2)
-            if 0 < s < PAIRS - 2:
-                for j in (2, 0, 1):
-                    gather_rows(False, s + 2, j, j + 1)
+            if 1 < s < PAIRS - 2:
+                gather_rows(False, s + 2, 2, 3)
+                gather_rows(False, s + 2, 0, 2)
                 gather_rows(True, s + 2, PACK - 1, PACK)
             if 0 < s < LAST:
-                quantise(s, rounded[:].bitcast(BF16), 0, 2 * PAIR)
+                quantise(s, rounded[:, ((s + 1) % 2) * WIDE : ((s + 1) % 2 + 2) * WIDE].bitcast(BF16), 0, 2 * PAIR)
             for v in range(2):
                 if s < LAST:
                     make_tanh(s + 1, v)
+            if s == 0:
+                gather_rows(False, 3, 0, PACK - 1)
 
         quantise(LAST, da_of(LAST - 1), PAIR, 2 * PAIR)
         second_product(LAST - 1, 0, 2, "spare_bank")
         empty_dx(LAST - 1, 0, 2)
         for v in range(2):
             apply_silu(LAST, v)
-        quantise(LAST + 1, da_of(LAST)[:, 0:WIDE], PAIR, PAIR + C)
-        second_product(LAST, 0, 1, "dh_bank0")
+        quantise(LAST + 1, da_of(LAST)[:, 0:WIDE], 0, C)
+        second_product(LAST, 0, 1, "bank00")
         empty_dx(LAST, 0, 1)
-        quantise(LAST + 1, da_of(LAST)[:, WIDE:], PAIR + C, 2 * PAIR)
+        quantise(LAST + 1, da_of(LAST)[:, WIDE:], C, PAIR)
         for h in range(K_TILES):
-            last = banks.tile([P, C], F32, name=f"a_bank{h}")
+            last = banks.tile([P, C], F32, name=f"bank1{h}")
             multiply_w1(last[:], LAST, 1, h)
             halve(h == 0, dx_sb[h][:, S - C : S], last[:])
 
-        parts = [(0, 0), (1, 0), (0, 1), (1, 1)]
+        parts = [(0, 0, 3 * C), (1, 0, HALF), (0, 3 * C, T), (1, HALF, T)]
         got = {}
 
         def fetch(on_vector, part, r, other=None):
-            h, u = parts[part]
-            got[part, r] = keep.tile([P, HALF], F32, name=f"got{part}_{r}")
-            found = dx_sb[h][:].indirect(pos_sb[r][:, u * HALF // LIST_COL : (u + 1) * HALF // LIST_COL])
+            h, t0, t1 = parts[part]
+            got[part, r] = keep.tile([P, t1 - t0], F32, name=f"got{part}_{r}")
+            found = dx_sb[h][:].indirect(pos_sb[r][:, t0 // LIST_COL : t1 // LIST_COL])
             if not on_vector:
                 nc.scalar.activation(got[part, r][:], found, ACT.Copy)
             elif other is None:
@@ -335,12 +349,14 @@ def tile_moe_bdx_mlp_silu_kernel(
             else:
                 nc.vector.tensor_tensor(got[part, r][:], found, got[part, other][:], ALU.add)
 
-        def add(part, name, x, y):
-            got[part, name] = keep.tile([P, HALF], F32, name=f"got{part}_{name}")
-            nc.vector.tensor_tensor(got[part, name][:], got[part, x][:], got[part, y][:], ALU.add)
-            if name == "all":
-                h, u = parts[part]
-                nc.sync.dma_start(out[h * P : (h + 1) * P, u * HALF : (u + 1) * HALF], got[part, name][:])
+        def add(part, name, x, y, cuts=None):
+            h, t0, t1 = parts[part]
+            got[part, name] = keep.tile([P, t1 - t0], F32, name=f"got{part}_{name}")
+            cuts = cuts or (0, t1 - t0)
+            for c0, c1 in zip(cuts, cuts[1:]):
+                nc.vector.tensor_tensor(got[part, name][:, c0:c1], got[part, x][:, c0:c1], got[part, y][:, c0:c1], ALU.add)
+                if name == "all":
+                    nc.sync.dma_start(out[h * P : (h + 1) * P, t0 + c0 : t0 + c1], got[part, name][:, c0:c1])
 
         fetch(True, 0, 0)
         fetch(False, 1, 1)
@@ -363,4 +379,4 @@ def tile_moe_bdx_mlp_silu_kernel(
         add(3, "three", 0, 2)
         add(0, "all", "three", 3)
         fetch(False, 3, 3)
-        add(3, "all", "three", 3)
+        add(3, "all", "three", 3, (0, HALF - C, HALF))

@@ -100,11 +100,15 @@ def tile_moe_bdx_mlp_silu_kernel(
             nc.sync.dma_start(dy_sb[j][:], dy_rows[:, j, :])
             if j == 0:
                 nc.sync.dma_start(offs_sb[:], offs)
+        load_plane(w2_plane, w2_scales, W2_GROUPS[0])
         load_gate(GATE_GROUPS[0])
         load_a(0)
         load_a(1)
         for s in range(PAIRS + 2):
             m = s - 2
+            for g in W2_GROUPS[1:]:
+                if g[0] == s:
+                    load_plane(w2_plane, w2_scales, g)
             if m >= 0 and m % 2 == 0:
                 load_words(w1_sb[m // 2], w1_words, 2 * m, 2 * m + 4)
             for g in W1_GROUPS:
@@ -112,9 +116,6 @@ def tile_moe_bdx_mlp_silu_kernel(
                     load_plane(w1_plane, w1_scales, g)
             if s < PAIRS:
                 load_words(w2_sb[s], w2_words, 2 * s, 2 * s + 2)
-            for g in W2_GROUPS:
-                if g[0] == s:
-                    load_plane(w2_plane, w2_scales, g)
             for g in GATE_GROUPS[1:]:
                 if g[0] == s + 2:
                     load_gate(g)

from contextlib import ExitStack

import concourse.mybir as mybir
from concourse.masks import make_identity

K, T, E, C, H, N = 256, 640, 20, 128, 512, 512
TOP = 4
S = E * C
P = 128
PACK = 4
LIST_COL = 16
K_TILES = K // P
PAIR = 2 * C
PAIRS = E // 2
LAST = PAIRS - 1
WIDE = PACK * C
HALF = T // 2
FIRST_HELPED = 2
VECTOR_EMPTIES = 7

GATE_GROUPS = ((0, 2), (2, 5), (5, PAIRS))
W2_GROUPS = ((0, 2), (2, 5), (5, PAIRS))
W1_GROUPS = ((0, 4), (4, PAIRS))

FLOPS = 2 * S * (N * H + H * K)
BYTES = 4 * (N * T + H * S + S + K * T) + E * (2 * P + 16) * (H + K) + 2 * P * (S + TOP * T) // LIST_COL

F32 = mybir.dt.float32
BF16 = mybir.dt.bfloat16
I32 = mybir.dt.int32
U32 = mybir.dt.uint32
U16 = mybir.dt.uint16
U8 = mybir.dt.uint8
FP8X4 = mybir.dt.float8_e4m3fn_x4
FP4X4 = mybir.dt.float4_e2m1fn_x4
ALU = mybir.AluOpType
ACT = mybir.ActivationFunctionType


def tile_moe_bdx_mlp_silu_kernel(
    tc, dyT, a, w2_words, w2_scales, w1_words, w1_scales, gate, offs, pos1, pos2, pos3, pos4, out
):
    nc = tc.nc
    with ExitStack() as ctx:
        keep = ctx.enter_context(tc.tile_pool(name="keep", bufs=1))
        banks = ctx.enter_context(tc.psum_pool(name="banks", bufs=1))

        offs_sb = keep.tile([P, S // LIST_COL], U16, name="offs_sb")
        pos_sb = [keep.tile([P, T // LIST_COL], U16, name=f"pos_sb{r}") for r in range(TOP)]
        dy_sb = [keep.tile([P, T], F32, name=f"dy_sb{j}") for j in range(PACK)]
        gate_sb = {g: keep.tile([P, (g[1] - g[0]) * PAIR], F32, name=f"gate_sb{g[0]}") for g in GATE_GROUPS}
        a_sb = [keep.tile([P, PACK, PAIR], F32, name=f"a_sb{n}") for n in range(PAIRS)]
        w2_sb = [keep.tile([P, 2, 2 * H], U8, name=f"w2_sb{n}", align_bytes=64) for n in range(PAIRS)]
        w1_sb = [keep.tile([P, 4, 2 * K], U8, name=f"w1_sb{n}", align_bytes=64) for n in range(PAIRS // 2)]
        w2_plane = {g: keep.tile([P, 2 * (g[1] - g[0]), H], U8, name=f"w2_plane{g[0]}", align_bytes=64) for g in W2_GROUPS}
        w1_plane = {g: keep.tile([P, 2 * (g[1] - g[0]), K], U8, name=f"w1_plane{g[0]}", align_bytes=64) for g in W1_GROUPS}
        dx_sb = [keep.tile([P, S], F32, name=f"dx_sb{h}") for h in range(K_TILES)]
        ident = keep.tile([P, P], F32, name="ident")
        gathered = [keep.tile([P, PACK * PAIR], F32, name=f"gathered{x}") for x in range(2)]
        first_gathered = keep.tile([P, PACK * PAIR], F32, name="first_gathered")
        early = keep.tile([P, PACK * 2 * PAIR], F32, name="early")
        first_g = keep.tile([P, WIDE], F32, name="first_g", align_bytes=64)
        rounded = keep.tile([P, 3 * WIDE], F32, name="rounded", align_bytes=64)
        silu = [keep.tile([P, WIDE], F32, name=f"silu{v}") for v in range(2)]

        zeros = gathered[1][:, PAIR : 3 * PAIR : PAIR]
        first_bias = gathered[1][:, 0:1]
        nc.vector.memset(zeros, 0.0)
        for g in W2_GROUPS:
            nc.vector.memset(w2_plane[g][:].bitcast(I32), 0)
        for g in W1_GROUPS:
            nc.gpsimd.memset(w1_plane[g][:].bitcast(I32), 0)
        make_identity(nc, ident[:])

        dy_rows = dyT.rearrange("(p j) t -> p j t", j=PACK)
        a_rows = a.rearrange("(p j) s -> p j s", j=PACK)

        def group_of(groups, n):
            return [g for g in groups if g[0] <= n < g[1]][0]

        def load_gate(g):
            nc.sync.dma_start(gate_sb[g][:], gate[0:P, g[0] * PAIR : g[1] * PAIR])

        def load_a(n):
            nc.sync.dma_start(a_sb[n][:], a_rows[:, :, n * PAIR : (n + 1) * PAIR])

        def load_words(tile, words, e0, e1):
            nc.sync.dma_start(tile[:].bitcast(I32), words[e0:e1, 0].rearrange("e p b -> p e b").bitcast(I32))

        def load_plane(planes, scale_rows, g):
            for r in range(4):
                src = scale_rows[2 * g[0] : 2 * g[1], 0, r:16:4, :].rearrange("e f i -> f e i")
                nc.sync.dma_start(planes[g][r:P:32, :, :].bitcast(I32), src.bitcast(I32))

        def plane_of(planes, n, v):
            g = group_of(planes, n)
            return planes[g][:, 2 * (n - g[0]) + v, :]

        for j in range(PACK):
            nc.sync.dma_start(dy_sb[j][:], dy_rows[:, j, :])
            if j == 0:
                nc.sync.dma_start(offs_sb[:], offs)
        load_plane(w2_plane, w2_scales, W2_GROUPS[0])
        load_gate(GATE_GROUPS[0])
        load_a(0)
        load_a(1)
        for s in range(PAIRS + 2):
            m = s - 2
            for g in W2_GROUPS[1:]:
                if g[0] == s:
                    load_plane(w2_plane, w2_scales, g)
            if m >= 0 and m % 2 == 0:
                load_words(w1_sb[m // 2], w1_words, 2 * m, 2 * m + 4)
            for g in W1_GROUPS:
                if g[0] == m:
                    load_plane(w1_plane, w1_scales, g)
            if s < PAIRS:
                load_words(w2_sb[s], w2_words, 2 * s, 2 * s + 2)
            for g in GATE_GROUPS[1:]:
                if g[0] == s + 2:
                    load_gate(g)
            if 0 < s < PAIRS - 1:
                load_a(s + 1)
        for r, pos in enumerate((pos1, pos2, pos3, pos4)):
            nc.sync.dma_start(pos_sb[r][:], pos)

        nc.scalar.activation(first_bias, zeros[:, 0:1], ACT.Silu)

        def gathered_of(m):
            if m in (1, 2):
                return early[:].rearrange("p (j s) -> p j s", j=PACK)[:, :, (m - 1) * PAIR : m * PAIR]
            tile = gathered[m % 2] if m else first_gathered
            return tile[:, 0 : PACK * PAIR].rearrange("p (j s) -> p j s", j=PACK)

        def gather(on_vector, dst, j, s0, s1):
            found = dy_sb[j][:].indirect(offs_sb[:, s0 // LIST_COL : s1 // LIST_COL])
            if on_vector:
                nc.vector.tensor_copy(dst, found)
            else:
                nc.scalar.activation(dst, found, ACT.Copy)

        def gather_slots(on_vector, m, j, s0, s1):
            gather(on_vector, gathered_of(m)[:, j, s0:s1], j, m * PAIR + s0, m * PAIR + s1)

        def gather_rows(on_vector, m, j0, j1):
            for j in range(j0, j1):
                gather_slots(on_vector, m, j, 0, PAIR)

        def g_of(m):
            unit = 2 * (m % 2) if m > 1 else 0
            return (rounded[:, unit * WIDE : (unit + 1) * WIDE] if m else first_g[:]).bitcast(BF16)

        def da_of(n):
            return (rounded[:, WIDE : 2 * WIDE] if n < LAST else rounded[:, 0:WIDE]).bitcast(BF16)

        def round_g(m, v0, v1):
            g = group_of(GATE_GROUPS, m)
            first = (m - g[0]) * PAIR
            weights = gate_sb[g][:, first + v0 * C : first + v1 * C]
            if m >= FIRST_HELPED:
                nc.gpsimd.tensor_tensor(
                    g_of(m).rearrange("p (s j) -> p s j", j=PACK),
                    gathered_of(m).rearrange("p j s -> p s j"),
                    weights.unsqueeze(2).to_broadcast([P, PAIR, PACK]),
                    ALU.mult,
                )
                return
            weights = weights.rearrange("p (s i) -> p s i", i=2)
            nc.vector.tensor_tensor(
                g_of(m)[:, v0 * WIDE : v1 * WIDE].rearrange("p (s i j) -> p s j i", i=2, j=PACK),
                gathered_of(m)[:, :, v0 * C : v1 * C].rearrange("p j (s i) -> p s j i", i=2),
                weights.unsqueeze(2).to_broadcast([P, (v1 - v0) * C // 2, PACK, 2]),
                ALU.mult,
            )

        codes, scales, dh_ps, a_turned, half, turned, dx_ps = {}, {}, {}, {}, {}, {}, {}

        def quantise(s, values, c0, c1):
            if s not in codes:
                codes[s] = keep.tile([P, 2 * PAIR], U32, name="codes" if 0 <= s <= LAST else "end_codes", align_bytes=64)
                scales[s] = keep.tile([P, 2 * PAIR], U8, name="scales" if 0 <= s <= LAST else "end_scales", align_bytes=64)
            nc.vector.quantize_mx(out=codes[s][:, c0:c1].bitcast(FP8X4), scales=scales[s][:, c0:c1], in_=values)

        def make_silu(n, v):
            nc.scalar.activation(
                silu[v][:].rearrange("p (s i j) -> p s j i", i=2, j=PACK),
                a_sb[n][:, :, v * C : (v + 1) * C].rearrange("p j (s i) -> p s j i", i=2),
                ACT.Silu,
                bias=zeros[:, 1:2] if (n, v) == (0, 1) else 0.0,
                scale=-1.0,
            )

        def turn_a(n, v):
            a_turned[n, v] = banks.tile([P, WIDE], F32, name=("spare_bank", "dx_bank")[v] if n == 1 else f"bank{(n + 1) % 2}{v}")
            for j in range(PACK):
                nc.tensor.transpose(a_turned[n, v][:, j * P : (j + 1) * P], a_sb[n][:, j, v * C : (v + 1) * C], ident[:])

        def tanh_of(n, v):
            if n == 1:
                return rounded[:, 2 * WIDE :] if v else first_gathered[:, 0:WIDE]
            return gathered[n % 2][:, (1 - v) * WIDE : (2 - v) * WIDE]

        def make_tanh(n, v):
            bias = (first_bias, zeros[:, 0:1])[v] if n == 0 else 0.0
            nc.scalar.activation(tanh_of(n, v), a_turned[n, v][:], ACT.Tanh, bias=bias, scale=-0.5)

        def first_product(n, v):
            cols = slice((n % 2) * PAIR + v * C, (n % 2) * PAIR + (v + 1) * C)
            dh_ps[n, v] = banks.tile([P, H], F32, name=f"bank{n % 2}{v}")
            nc.tensor.matmul_mx(
                out=dh_ps[n, v][:],
                lhsT=codes[n - 1][:, cols].bitcast(FP8X4),
                lhsT_scale=scales[n - 1][:, cols],
                rhs=w2_sb[n][:, v, :].bitcast(FP4X4),
                rhs_scale=plane_of(w2_plane, n, v),
                start=True,
                stop=True,
            )

        def apply_tanh(n, v):
            half[n, v] = keep.tile([P, PACK, P], F32, name=f"half{v}")
            nc.vector.scalar_tensor_tensor(
                half[n, v][:],
                tanh_of(n, v).rearrange("s (j p) -> s j p", j=PACK),
                1.0,
                dh_ps[n, v][:].rearrange("s (p j) -> s j p", j=PACK),
                ALU.subtract,
                ALU.mult,
            )

        def turn_half(n, v):
            turned[n, v] = banks.tile([P, PACK, C], F32, name=f"half_bank{v}")
            for j in range(PACK):
                nc.tensor.transpose(turned[n, v][:, j, :], half[n, v][:, j, :], ident[:])

        def apply_silu(n, v):
            nc.vector.scalar_tensor_tensor(
                da_of(n)[:, v * WIDE : (v + 1) * WIDE].rearrange("p (s j) -> p s j", j=PACK),
                silu[v][:].rearrange("p (s j) -> p s j", j=PACK),
                1.0,
                turned[n, v][:].rearrange("p j s -> p s j"),
                ALU.subtract,
                ALU.mult,
            )

        def multiply_w1(dst, n, v, h):
            cols = slice(((n + 1) % 2) * PAIR + v * C, ((n + 1) % 2) * PAIR + (v + 1) * C)
            nc.tensor.matmul_mx(
                out=dst,
                lhsT=w1_sb[n // 2][:, 2 * (n % 2) + v, 2 * P * h : 2 * P * (h + 1)].bitcast(FP4X4),
                lhsT_scale=plane_of(w1_plane, n, v)[:, P * h : P * (h + 1)],
                rhs=codes[n + 1][:, cols].bitcast(FP8X4),
                rhs_scale=scales[n + 1][:, cols],
                start=True,
                stop=True,
            )

        def second_product(n, v0, v1, bank):
            dx_ps[n] = banks.tile([P, K_TILES, (v1 - v0) * C], F32, name=bank)
            for h in range(K_TILES):
                for v in range(v0, v1):
                    multiply_w1(dx_ps[n][:, h, (v - v0) * C : (v - v0 + 1) * C], n, v, h)

        def halve(on_vector, dst, src):
            if on_vector:
                nc.vector.tensor_scalar(dst, src, 0.5, None, ALU.mult)
            else:
                nc.scalar.activation(dst, src, ACT.Copy, scale=0.5)

        def empty_dx(n, v0, v1):
            for h in range(K_TILES):
                halve(n < VECTOR_EMPTIES, dx_sb[h][:, n * PAIR + v0 * C : n * PAIR + v1 * C], dx_ps[n][:, h, :])

        gather_rows(True, 0, 0, PACK)
        for j in range(PACK - 1):
            gather(False, early[:, j * 2 * PAIR : (j + 1) * 2 * PAIR], j, PAIR, 3 * PAIR)
        gather_rows(True, 1, PACK - 1, PACK)
        gather_rows(False, 2, PACK - 1, PACK)
        for v in range(2):
            round_g(0, v, v + 1)
        for v in range(2):
            turn_a(0, v)
        for v in range(2):
            quantise(-1, g_of(0)[:, v * WIDE : (v + 1) * WIDE], v * C, (v + 1) * C)
            first_product(0, v)
            make_tanh(0, v)
        round_g(1, 0, 2)
        quantise(0, g_of(1), PAIR, 2 * PAIR)
        for v in range(2):
            turn_a(1, v)
        gather_rows(True, 3, PACK - 1, PACK)

        for s in range(PAIRS):
            if FIRST_HELPED <= s + 1 < PAIRS:
                round_g(s + 1, 0, 2)
            for v in range(2):
                if s > 0:
                    first_product(s, v)
            if s >= 2:
                second_product(s - 2, 0, 2, "dx_bank")
            for v in range(2):
                if s > 0:
                    apply_silu(s - 1, v)
                make_silu(s, v)
            for v in range(2):
                apply_tanh(s, v)
                turn_half(s, v)
            for v in range(2):
                if 0 < s < LAST:
                    turn_a(s + 1, v)
            if s >= 2:
                empty_dx(s - 2, 0, 2)
            if 1 < s < PAIRS - 2:
                gather_rows(False, s + 2, 2, 3)
                gather_rows(False, s + 2, 0, 2)
                gather_rows(True, s + 2, PACK - 1, PACK)
            if 0 < s < LAST:
                quantise(s, rounded[:, ((s + 1) % 2) * WIDE : ((s + 1) % 2 + 2) * WIDE].bitcast(BF16), 0, 2 * PAIR)
            for v in range(2):
                if s < LAST:
                    make_tanh(s + 1, v)
            if s == 0:
                gather_rows(False, 3, 0, PACK - 1)

        quantise(LAST, da_of(LAST - 1), PAIR, 2 * PAIR)
        second_product(LAST - 1, 0, 2, "spare_bank")
        empty_dx(LAST - 1, 0, 2)
        for v in range(2):
            apply_silu(LAST, v)
        quantise(LAST + 1, da_of(LAST)[:, 0:WIDE], 0, C)
        second_product(LAST, 0, 1, "bank00")
        empty_dx(LAST, 0, 1)
        quantise(LAST + 1, da_of(LAST)[:, WIDE:], C, PAIR)
        for h in range(K_TILES):
            last = banks.tile([P, C], F32, name=f"bank1{h}")
            multiply_w1(last[:], LAST, 1, h)
            halve(h == 0, dx_sb[h][:, S - C : S], last[:])

        parts = [(0, 0, 3 * C), (1, 0, HALF), (0, 3 * C, T), (1, HALF, T)]
        got = {}

        def fetch(on_vector, part, r, other=None):
            h, t0, t1 = parts[part]
            got[part, r] = keep.tile([P, t1 - t0], F32, name=f"got{part}_{r}")
            found = dx_sb[h][:].indirect(pos_sb[r][:, t0 // LIST_COL : t1 // LIST_COL])
            if not on_vector:
                nc.scalar.activation(got[part, r][:], found, ACT.Copy)
            elif other is None:
                nc.vector.tensor_copy(got[part, r][:], found)
            else:
                nc.vector.tensor_tensor(got[part, r][:], found, got[part, other][:], ALU.add)

        def add(part, name, x, y, cuts=None):
            h, t0, t1 = parts[part]
            got[part, name] = keep.tile([P, t1 - t0], F32, name=f"got{part}_{name}")
            cuts = cuts or (0, t1 - t0)
            for c0, c1 in zip(cuts, cuts[1:]):
                nc.vector.tensor_tensor(got[part, name][:, c0:c1], got[part, x][:, c0:c1], got[part, y][:, c0:c1], ALU.add)
                if name == "all":
                    nc.sync.dma_start(out[h * P : (h + 1) * P, t0 + c0 : t0 + c1], got[part, name][:, c0:c1])

        fetch(True, 0, 0)
        fetch(False, 1, 1)
        fetch(True, 1, 0, 1)
        fetch(False, 0, 1)
        fetch(True, 0, 2, 1)
        fetch(False, 2, 1)
        fetch(True, 2, 0, 1)
        fetch(False, 1, 3)
        fetch(True, 1, 2, 3)
        fetch(False, 3, 1)
        fetch(True, 3, 0, 1)
        add(1, "all", 0, 2)
        fetch(False, 2, 3)
        fetch(True, 2, 2, 3)
        add(0, "three", 0, 2)
        add(2, "all", 0, 2)
        fetch(False, 0, 3)
        fetch(False, 3, 2)
        add(3, "three", 0, 2)
        add(0, "all", "three", 3)
        fetch(False, 3, 3)
        add(3, "all", "three", 3, (0, HALF - C, HALF))
